import numpy as np
import ml_dtypes


def mxq(x, axis, fmt="e4m3"):
    dtype, down = {"e4m3": (ml_dtypes.float8_e4m3fn, 7), "e5m2": (ml_dtypes.float8_e5m2, 14)}[fmt]
    v = np.moveaxis(np.asarray(x, np.float32).astype(ml_dtypes.bfloat16).astype(np.float64), axis, -1)
    blocks = v.reshape(v.shape[:-1] + (-1, 32))
    amax = np.abs(blocks).max(-1, keepdims=True)
    byte = np.maximum(np.where(amax > 0, np.frexp(amax)[1] - 1 + 127, 0) - down, 1)
    scale = np.exp2(byte - 127.0)
    codes = (blocks / scale).astype(np.float32).astype(dtype).astype(np.float64)
    return np.moveaxis((codes * scale).reshape(v.shape), -1, axis)


WIDE = False


def mx_kscale(k):
    if not WIDE:
        return np.ones(k)
    levels = np.array([10, -10, 5, -5, 0])
    if k % 512:
        return np.exp2(np.random.permutation(np.resize(levels, k // 32))).repeat(32)
    a = np.empty((k // 512, 16))
    for p in range(k // 512):
        a[p, :8] = np.random.permutation(np.resize(levels, 8))
        for g in range(8):
            far = levels[np.abs(levels - a[p, g]) >= 10]
            a[p, g + 8] = far[np.random.randint(len(far))]
    return np.exp2(a.ravel()).repeat(32)


def f64(x):
    return np.asarray(x).astype(np.float64)


def striped(idx):
    return np.tile(idx.reshape(-1, 16).T, (8, 1)).astype(np.uint16)


def unstriped(offs):
    return offs[:16].T.reshape(-1).astype(np.int64)


E2M1 = np.array([0.0, 0.5, 1.0, 1.5, 2.0, 3.0, 4.0, 6.0, -0.0, -0.5, -1.0, -1.5, -2.0, -3.0, -4.0, -6.0])


def pack_weight(w, fmt):
    k, n = w.shape
    w = f64(np.asarray(w, np.float32).astype(ml_dtypes.bfloat16)).reshape(k // 32, 32, n)
    amax = np.abs(w).max(1)
    if fmt == "e4m3":
        byte = np.frexp(amax)[1] - 1 + 127 - 7
    else:
        mant, ex = np.frexp(amax / 6.0)
        byte = np.where(mant > 0.5, ex, ex - 1) + 127
    byte = np.clip(np.where(amax > 0, byte, 1), 1, 254)
    scaled = (w * np.exp2(127.0 - byte)[:, None, :]).reshape(k, n).astype(np.float32)
    by_word = np.ascontiguousarray(scaled.reshape(k // 512, 128, 4, n).transpose(0, 1, 3, 2))
    if fmt == "e4m3":
        words = by_word.astype(ml_dtypes.float8_e4m3fn).view(np.uint8)
    else:
        c = by_word.astype(ml_dtypes.float4_e2m1fn).view(np.uint8) & 0xF
        words = (c[..., 0::2] | (c[..., 1::2] << 4)).reshape(k // 512, 128, 2 * n)
    return np.ascontiguousarray(words), np.ascontiguousarray(byte.astype(np.uint8).reshape(k // 512, 16, n))


def unpack_weight(words, scales, fmt):
    g, _, n = scales.shape
    words = np.ascontiguousarray(words).reshape(g, 128, n, -1)
    if fmt == "e4m3":
        vals = words.view(ml_dtypes.float8_e4m3fn).astype(np.float64)
    else:
        nib = np.empty((g, 128, n, 4), np.uint8)
        nib[..., 0::2] = words & 0xF
        nib[..., 1::2] = words >> 4
        vals = E2M1[nib]
    vals = vals * np.repeat(np.exp2(scales.astype(np.float64) - 127.0), 8, axis=1)[..., None]
    return vals.transpose(0, 1, 3, 2).reshape(g * 512, n)


def gelu(v):
    return 0.5 * v * (1.0 + np.tanh(np.sqrt(2.0 / np.pi) * (v + 0.044715 * v**3)))


K, K2, H, N, T, P, T2, S = 1024, 512, 1024, 512, 2048, 512, 1024, 512


def setup_inputs():
    n = np.random.standard_normal
    s = mx_kscale(K)[:, None]
    s2 = mx_kscale(K2)[:, None]
    u = mx_kscale(H)[:, None]
    tab_words, tab_scales = pack_weight(n((K, T)) * s, "e4m3")
    w2_words, w2_scales = pack_weight(n((K, H)) / np.sqrt(K) * u.T / s, "e2m1")
    w3_words, w3_scales = pack_weight(n((H, N)) / np.sqrt(H) / u, "e4m3")
    return {
        "xs": (np.round(16 * n((K2, S))) / 16 * s2).astype(np.float32),
        "base": (n((K2, T2)) * s2).astype(np.float32),
        "w1": (n((K2, H)) / np.sqrt(K2) * u.T / s2).astype(np.float32),
        "clear": ((0.3 + 0.3 * np.abs(n(H))) * u[:, 0]).astype(np.float32),
        "tab_words": tab_words, "tab_scales": tab_scales,
        "w2_words": w2_words, "w2_scales": w2_scales,
        "w3_words": w3_words, "w3_scales": w3_scales,
        "offs": striped(np.random.permutation(T)[:P]),
        "offs2": striped(np.random.permutation(T2)[:S]),
        "offs3": striped(np.random.permutation(T2)[:P]),
    }


def reference(xs, base, w1, clear, tab_words, tab_scales, w2_words, w2_scales,
              w3_words, w3_scales, offs, offs2, offs3):
    page = f64(base).copy()
    page[:, unstriped(offs2)] = f64(xs)
    a = mxq(f64(w1), 0, "e4m3").T @ mxq(page, 0, "e4m3")
    x = a[:, unstriped(offs3)]
    v = unpack_weight(tab_words, tab_scales, "e4m3")[:, unstriped(offs)]
    b = unpack_weight(w2_words, w2_scales, "e2m1").T @ v
    z = np.maximum(x, b) - f64(clear)[:, None]
    out = unpack_weight(w3_words, w3_scales, "e4m3").T @ mxq(z, 0, "e4m3")
    return out

@@ -1,0 +1,271 @@
+from contextlib import ExitStack
+
+import concourse.mybir as mybir
+
+K, K2, H, N, T, PICKS, T2, S = 1024, 512, 1024, 512, 2048, 512, 1024, 512
+FLOPS = 2 * K2 * H * T2 + 2 * K * H * PICKS + 2 * H * N * PICKS
+
+F32 = mybir.dt.float32
+BF16 = mybir.dt.bfloat16
+I32 = mybir.dt.int32
+U32 = mybir.dt.uint32
+U16 = mybir.dt.uint16
+U8 = mybir.dt.uint8
+FP8X4 = mybir.dt.float8_e4m3fn_x4
+FP4X4 = mybir.dt.float4_e2m1fn_x4
+IDENTITY = mybir.ActivationFunctionType.Identity
+MAX = mybir.AluOpType.max
+
+P = 128
+PACK = 4
+K_PASS = P * PACK
+BANK = 512
+HALF = 256
+
+
+def tile_list_free_space_fusion_kernel(
+    tc, xs, base, w1, clear, tab_words, tab_scales, w2_words, w2_scales, w3_words, w3_scales, offs, offs2, offs3, out
+):
+    nc = tc.nc
+    with ExitStack() as ctx:
+        sb = ctx.enter_context(tc.tile_pool(name="sb", bufs=1))
+        psum = ctx.enter_context(tc.psum_pool(name="psum", bufs=8))
+
+        def tile(name, shape, dtype, tag=None):
+            return sb.tile(shape, dtype, name=name, tag=tag or name, align_bytes=64)
+
+        def bank(name, width):
+            return psum.tile([P, width], F32, name=name, tag="bank")
+
+        idx = tile("idx", [P, PICKS // 16], U16)
+        idx2 = tile("idx2", [P, S // 16], U16)
+        idx3 = tile("idx3", [P, PICKS // 16], U16)
+
+        tab_s = tile("tab_s", [P, T], U8)
+        w2_s = tile("w2_s", [P, H], U8)
+        v_s1 = tile("v_s1", [P, PICKS], U8)
+        w2p_s1 = tile("w2p_s1", [P, H], U8)
+        for plane in (tab_s, w2_s, v_s1, w2p_s1):
+            nc.vector.memset(plane[:].bitcast(I32), 0)
+
+        base_rows = base.rearrange("(p t) c -> p t c", t=PACK)
+        xs_rows = xs.rearrange("(p t) c -> p t c", t=PACK)
+        w1_rows = w1.rearrange("(p j) r -> p j r", j=PACK)
+        page = [tile(f"page{t}", [P, T2], F32) for t in range(PACK)]
+        scan = [tile(f"scan{t}", [P, S], F32) for t in range(PACK)]
+        w1_raw = [tile(f"w1_raw{q}", [P, PACK, HALF], F32) for q in range(4)]
+        clear_t = tile("clear_t", [P, 2, PACK], F32)
+
+        def load_plane(t):
+            nc.sync.dma_start(scan[t][:], xs_rows[:, t, :])
+            nc.sync.dma_start(page[t][:], base_rows[:, t, :])
+
+        def load_w1(q):
+            nc.sync.dma_start(w1_raw[q][:], w1_rows[:, :, q * HALF : (q + 1) * HALF])
+
+        def load_scales(plane, scales):
+            for q in range(4):
+                nc.sync.dma_start(
+                    plane[32 * q : 32 * q + 8, :].bitcast(I32), scales[:, 4 * q : 4 * q + 4, :].bitcast(I32)
+                )
+
+        nc.sync.dma_start(idx2[:], offs2)
+        load_plane(0)
+        load_w1(0)
+        load_plane(1)
+        load_w1(1)
+        load_w1(2)
+        load_plane(2)
+        load_w1(3)
+        load_plane(3)
+        nc.sync.dma_start(idx[:], offs)
+        nc.sync.dma_start(clear_t[:], clear.rearrange("(b p t) -> p b t", p=P, t=PACK))
+        nc.sync.dma_start(idx3[:], offs3)
+        load_scales(tab_s, tab_scales)
+        load_scales(w2_s, w2_scales)
+
+        w1_g = [tile(f"w1_g{b}", [P, PACK * K_PASS], BF16) for b in range(2)]
+
+        def group_w1(q):
+            b, half = divmod(q, 2)
+            nc.scalar.copy(
+                w1_g[b][:].rearrange("p (t m j) -> p m j t", t=PACK, j=PACK)[:, half * 64 : (half + 1) * 64],
+                w1_raw[q][:].rearrange("p j (m t) -> p m j t", t=PACK),
+            )
+
+        group_w1(0)
+        group_w1(1)
+        pairs = [tile(f"pairs{h}", [P, 2, BANK, 2], BF16, tag=f"w1_raw{h}") for h in range(2)]
+
+        def scatter(t):
+            nc.vector.tensor_copy(page[t][:].indirect(idx2[:]), scan[t][:])
+            for h in range(2):
+                nc.scalar.copy(pairs[h][:, t // 2, :, t % 2], page[t][:, h * BANK : (h + 1) * BANK])
+
+        scatter(0)
+        scatter(1)
+        group_w1(2)
+        group_w1(3)
+        scatter(2)
+        scatter(3)
+
+        tab_w = [tile("tab_w0", [P, T], I32, tag="scan0"), tile("tab_w1", [P, T], I32, tag="page0")]
+        w2_w = tile("w2_w", [P, 2, 2 * H], U8, tag="scan1")
+        w3_w = tile("w3_w", [P, 2, N], I32, tag="page1")
+        w3_s = tile("w3_s", [P, N], U8, tag="scan2")
+        for a in range(2):
+            nc.sync.dma_start(tab_w[a][:], tab_words[a].rearrange("p t i -> p (t i)").bitcast(I32))
+        nc.sync.dma_start(w2_w[:].bitcast(I32), w2_words.rearrange("a p c -> p a c").bitcast(I32))
+        nc.sync.dma_start(w3_w[:], w3_words.rearrange("a p c i -> p a (c i)").bitcast(I32))
+        nc.gpsimd.memset(w3_s[:].bitcast(I32), 0)
+        load_scales(w3_s, w3_scales)
+
+        page_g = [tile(f"page_g{h}", [P, PACK * BANK], BF16) for h in range(2)]
+        for h in range(2):
+            nc.scalar.copy(
+                page_g[h][:].bitcast(F32).rearrange("p (c u) -> p c u", u=2),
+                pairs[h][:].rearrange("p u c e -> p u (c e)").bitcast(F32).rearrange("p u c -> p c u"),
+            )
+        neg_clear = tile("neg_clear", [P, 2 * PACK], F32)
+        nc.scalar.mul(neg_clear[:], clear_t[:].rearrange("p b t -> p (b t)"), -1.0)
+
+        w1_c = tile("w1_c", [P, H], U32, tag="scan3")
+        w1_s = [tile(f"w1_s{b}", [P, K_PASS], U8) for b in range(2)]
+        for b in range(2):
+            nc.vector.quantize_mx(out=w1_c[:, b * K_PASS : (b + 1) * K_PASS].bitcast(FP8X4), scales=w1_s[b][:], in_=w1_g[b][:])
+
+        v_s0 = tile("v_s0", [P, PICKS], U8)
+        nc.vector.tensor_copy(v_s0[:], tab_s[:].indirect(idx[:]))
+        nc.gpsimd.dma_start(v_s1[0:100, :].bitcast(I32), v_s0[4:104, :].bitcast(I32))
+        w2p_s0 = tile("w2p_s0", [P, H], U8)
+        nc.vector.tensor_copy(
+            w2p_s0[:].rearrange("p (b t m) -> p b t m", b=2, t=PACK),
+            w2_s[:].rearrange("p (b m t) -> p b t m", b=2, t=PACK),
+        )
+        nc.gpsimd.dma_start(w2p_s1[0:100, :].bitcast(I32), w2p_s0[4:104, :].bitcast(I32))
+        def quantize_page(h, codes_tag, scales_tag):
+            codes = tile(f"page_c{h}", [P, BANK], U32, tag=codes_tag)
+            scales = tile(f"page_s{h}", [P, BANK], U8, tag=scales_tag)
+            nc.vector.quantize_mx(out=codes[:].bitcast(FP8X4), scales=scales[:], in_=page_g[h][:])
+            return codes, scales
+
+        def gather_words(a, tag):
+            words = tile(f"v_c{a}", [P, PICKS], U32, tag=tag)
+            nc.vector.tensor_copy(words[:], tab_w[a][:].bitcast(U32).indirect(idx[:]))
+            return words
+
+        page_q0 = quantize_page(0, "tab_s", "w2_s")
+        v_c0 = gather_words(0, "page_g0")
+        page_q1 = quantize_page(1, "scan0", None)
+        w2p_w = tile("w2p_w", [P, 2, 2 * H], U8, tag="page_g1")
+        nc.vector.tensor_copy(
+            w2p_w[:].bitcast(U16).rearrange("p a (b t m) -> p (a b) t m", b=2, t=PACK),
+            w2_w[:].bitcast(U16).rearrange("p a (b m t) -> p (a b) t m", b=2, t=PACK),
+        )
+        v_c1 = gather_words(1, "scan1")
+        page_c, page_s = zip(page_q0, page_q1)
+        v_c = [v_c0, v_c1]
+        v_s = [v_s0, v_s1]
+        w2p_s = [w2p_s0, w2p_s1]
+
+        a_sb = [tile(f"a_sb{k}", [P, T2], F32) for k in range(8)]
+        x_sb = [tile("x_sb0", [P, PACK, PICKS], F32, tag="page0"), tile("x_sb1", [P, PACK, PICKS], F32)]
+        b_sb = [tile(f"b_sb{b}", [P, PACK, PICKS], F32) for b in range(2)]
+
+        def make_x(k):
+            b, t = divmod(k, PACK)
+            cols = slice(t * P, (t + 1) * P)
+            for h in range(2):
+                acc = bank(f"a{k}_{h}", BANK)
+                nc.tensor.matmul_mx(
+                    out=acc[:],
+                    lhsT=w1_c[:, k * P : (k + 1) * P].bitcast(FP8X4),
+                    lhsT_scale=w1_s[b][:, cols],
+                    rhs=page_c[h][:].bitcast(FP8X4),
+                    rhs_scale=page_s[h][:],
+                    start=True,
+                    stop=True,
+                )
+                nc.scalar.activation(
+                    a_sb[k][:, h * BANK : (h + 1) * BANK], acc[:], IDENTITY, bias=neg_clear[:, k : k + 1], scale=1.0
+                )
+            nc.vector.tensor_copy(x_sb[b][:, t, :], a_sb[k][:].indirect(idx3[:]))
+
+        def make_b(k):
+            b, t = divmod(k, PACK)
+            acc = bank(f"b{k}", BANK)
+            for a in range(2):
+                nc.tensor.matmul_mx(
+                    out=acc[:],
+                    lhsT=w2p_w[:, a, 2 * k * P : 2 * (k + 1) * P].bitcast(FP4X4),
+                    lhsT_scale=w2p_s[a][:, k * P : (k + 1) * P],
+                    rhs=v_c[a][:].bitcast(FP8X4),
+                    rhs_scale=v_s[a][:],
+                    start=(a == 0),
+                    stop=(a == 1),
+                )
+            nc.scalar.activation(b_sb[b][:, t, :], acc[:], IDENTITY, bias=neg_clear[:, k : k + 1], scale=1.0)
+
+        def make_z(b, j0, width):
+            z_g = tile(f"z_g{b}_{j0}", [P, PACK * width], BF16)
+            nc.vector.tensor_tensor(
+                z_g[:].rearrange("p (c i t) -> p c t i", i=2, t=PACK),
+                x_sb[b][:, :, j0 : j0 + width].rearrange("p t (c i) -> p c t i", i=2),
+                b_sb[b][:, :, j0 : j0 + width].rearrange("p t (c i) -> p c t i", i=2),
+                MAX,
+            )
+            return z_g
+
+        def quantize_z(b, j0, width, z_g):
+            z_c = tile(f"z_c{b}_{j0}", [P, width], U32)
+            z_s = tile(f"z_s{b}_{j0}", [P, width], U8)
+            nc.vector.quantize_mx(out=z_c[:].bitcast(FP8X4), scales=z_s[:], in_=z_g[:])
+            return z_c, z_s
+
+        for k in range(6):
+            make_x(k)
+        for k in range(4):
+            make_b(k)
+        z0 = make_z(0, 0, PICKS)
+        make_x(6)
+        z0_c, z0_s = quantize_z(0, 0, PICKS, z0)
+        make_x(7)
+        for k in range(4, 8):
+            make_b(k)
+        z1 = [make_z(1, h * HALF, HALF) for h in range(2)]
+        z1_q = [quantize_z(1, h * HALF, HALF, z1[h]) for h in range(2)]
+
+        accs = {}
+        for h in range(2):
+            for n in range(4):
+                accs[h, n] = bank(f"o{h}_{n}", HALF)
+                nc.tensor.matmul_mx(
+                    out=accs[h, n][:],
+                    lhsT=w3_w[:, 0, n * P : (n + 1) * P].bitcast(FP8X4),
+                    lhsT_scale=w3_s[:, n * P : (n + 1) * P],
+                    rhs=z0_c[:, h * HALF : (h + 1) * HALF].bitcast(FP8X4),
+                    rhs_scale=z0_s[:, h * HALF : (h + 1) * HALF],
+                    start=True,
+                    stop=False,
+                )
+        out_rows = out.rearrange("(n p) j -> p n j", p=P)
+        for h in range(2):
+            z_c, z_s = z1_q[h]
+            for n in range(4):
+                nc.tensor.matmul_mx(
+                    out=accs[h, n][:],
+                    lhsT=w3_w[:, 1, n * P : (n + 1) * P].bitcast(FP8X4),
+                    lhsT_scale=w3_s[4:P, n * P : (n + 1) * P],
+                    rhs=z_c[:].bitcast(FP8X4),
+                    rhs_scale=z_s[:],
+                    start=False,
+                    stop=True,
+                )
+            for e in range(2):
+                res = tile(f"res{h}_{e}", [P, 2, HALF], F32)
+                for i in range(2):
+                    if e == 0 or h == 0:
+                        nc.scalar.copy(res[:, i, :], accs[h, 2 * i + e][:])
+                    else:
+                        nc.vector.tensor_copy(res[:, i, :], accs[h, 2 * i + e][:])
+                nc.sync.dma_start(out_rows[:, e:4:2, h * HALF : (h + 1) * HALF], res[:])

@@ -43,9 +43,10 @@ def tile_list_free_space_fusion_kernel(
 
         tab_s = tile("tab_s", [P, T], U8)
         w2_s = tile("w2_s", [P, H], U8)
+        w3_s = tile("w3_s", [P, N], U8)
         v_s1 = tile("v_s1", [P, PICKS], U8)
         w2p_s1 = tile("w2p_s1", [P, H], U8)
-        for plane in (tab_s, w2_s, v_s1, w2p_s1):
+        for plane in (tab_s, w2_s, w3_s, v_s1, w2p_s1):
             nc.vector.memset(plane[:].bitcast(I32), 0)
 
         base_rows = base.rearrange("(p t) c -> p t c", t=PACK)
@@ -65,7 +66,7 @@ def tile_list_free_space_fusion_kernel(
 
         def load_scales(plane, scales):
             for q in range(4):
-                nc.sync.dma_start(
+                nc.gpsimd.dma_start(
                     plane[32 * q : 32 * q + 8, :].bitcast(I32), scales[:, 4 * q : 4 * q + 4, :].bitcast(I32)
                 )
 
@@ -79,28 +80,43 @@ def tile_list_free_space_fusion_kernel(
         load_w1(3)
         load_plane(3)
         nc.sync.dma_start(idx[:], offs)
-        nc.sync.dma_start(clear_t[:], clear.rearrange("(b p t) -> p b t", p=P, t=PACK))
+        tab_w = [tile(f"tab_w{a}", [P, T], I32) for a in range(2)]
+        w2_w = tile("w2_w", [P, 2, 2 * H], U8)
+        w3_w = tile("w3_w", [P, 2, N], I32)
+        nc.sync.dma_start(tab_w[0][:], tab_words[0].rearrange("p t i -> p (t i)").bitcast(I32))
+        nc.sync.dma_start(w2_w[:].bitcast(I32), w2_words.rearrange("a p c -> p a c").bitcast(I32))
+        nc.sync.dma_start(tab_w[1][:], tab_words[1].rearrange("p t i -> p (t i)").bitcast(I32))
         nc.sync.dma_start(idx3[:], offs3)
+        nc.sync.dma_start(w3_w[:], w3_words.rearrange("a p c i -> p a (c i)").bitcast(I32))
+        nc.gpsimd.dma_start(clear_t[:], clear.rearrange("(b p t) -> p b t", p=P, t=PACK))
         load_scales(tab_s, tab_scales)
         load_scales(w2_s, w2_scales)
+        load_scales(w3_s, w3_scales)
 
         w1_g = [tile(f"w1_g{b}", [P, PACK * K_PASS], BF16) for b in range(2)]
 
         def group_w1(q):
             b, half = divmod(q, 2)
             nc.scalar.copy(
-                w1_g[b][:].rearrange("p (t m j) -> p m j t", t=PACK, j=PACK)[:, half * 64 : (half + 1) * 64],
-                w1_raw[q][:].rearrange("p j (m t) -> p m j t", t=PACK),
+                w1_g[b][:].rearrange("p (u e m j) -> p u m j e", u=2, e=2, j=PACK)[:, :, half * 64 : (half + 1) * 64],
+                w1_raw[q][:].rearrange("p j (m u e) -> p u m j e", u=2, e=2),
             )
 
         group_w1(0)
         group_w1(1)
         pairs = [tile(f"pairs{h}", [P, 2, BANK, 2], BF16, tag=f"w1_raw{h}") for h in range(2)]
 
+        page_g = [tile(f"page_g{h}", [P, PACK * BANK], BF16) for h in range(2)]
+
         def scatter(t):
             nc.vector.tensor_copy(page[t][:].indirect(idx2[:]), scan[t][:])
             for h in range(2):
                 nc.scalar.copy(pairs[h][:, t // 2, :, t % 2], page[t][:, h * BANK : (h + 1) * BANK])
+                if t == PACK - 1:
+                    nc.scalar.copy(
+                        page_g[h][:].bitcast(F32).rearrange("p (c u) -> p c u", u=2),
+                        pairs[h][:].rearrange("p u c e -> p u (c e)").bitcast(F32).rearrange("p u c -> p c u"),
+                    )
 
         scatter(0)
         scatter(1)
@@ -109,23 +125,6 @@ def tile_list_free_space_fusion_kernel(
         scatter(2)
         scatter(3)
 
-        tab_w = [tile("tab_w0", [P, T], I32, tag="scan0"), tile("tab_w1", [P, T], I32, tag="page0")]
-        w2_w = tile("w2_w", [P, 2, 2 * H], U8, tag="scan1")
-        w3_w = tile("w3_w", [P, 2, N], I32, tag="page1")
-        w3_s = tile("w3_s", [P, N], U8, tag="scan2")
-        for a in range(2):
-            nc.sync.dma_start(tab_w[a][:], tab_words[a].rearrange("p t i -> p (t i)").bitcast(I32))
-        nc.sync.dma_start(w2_w[:].bitcast(I32), w2_words.rearrange("a p c -> p a c").bitcast(I32))
-        nc.sync.dma_start(w3_w[:], w3_words.rearrange("a p c i -> p a (c i)").bitcast(I32))
-        nc.gpsimd.memset(w3_s[:].bitcast(I32), 0)
-        load_scales(w3_s, w3_scales)
-
-        page_g = [tile(f"page_g{h}", [P, PACK * BANK], BF16) for h in range(2)]
-        for h in range(2):
-            nc.scalar.copy(
-                page_g[h][:].bitcast(F32).rearrange("p (c u) -> p c u", u=2),
-                pairs[h][:].rearrange("p u c e -> p u (c e)").bitcast(F32).rearrange("p u c -> p c u"),
-            )
         neg_clear = tile("neg_clear", [P, 2 * PACK], F32)
         nc.scalar.mul(neg_clear[:], clear_t[:].rearrange("p b t -> p (b t)"), -1.0)
 
@@ -134,10 +133,10 @@ def tile_list_free_space_fusion_kernel(
         for b in range(2):
             nc.vector.quantize_mx(out=w1_c[:, b * K_PASS : (b + 1) * K_PASS].bitcast(FP8X4), scales=w1_s[b][:], in_=w1_g[b][:])
 
-        v_s0 = tile("v_s0", [P, PICKS], U8)
+        v_s0 = tile("v_s0", [P, PICKS], U8, tag="w1_g0")
         nc.vector.tensor_copy(v_s0[:], tab_s[:].indirect(idx[:]))
         nc.gpsimd.dma_start(v_s1[0:100, :].bitcast(I32), v_s0[4:104, :].bitcast(I32))
-        w2p_s0 = tile("w2p_s0", [P, H], U8)
+        w2p_s0 = tile("w2p_s0", [P, H], U8, tag="w1_g1")
         nc.vector.tensor_copy(
             w2p_s0[:].rearrange("p (b t m) -> p b t m", b=2, t=PACK),
             w2_s[:].rearrange("p (b m t) -> p b t m", b=2, t=PACK),
@@ -156,40 +155,46 @@ def tile_list_free_space_fusion_kernel(
 
         page_q0 = quantize_page(0, "tab_s", "w2_s")
         v_c0 = gather_words(0, "page_g0")
-        page_q1 = quantize_page(1, "scan0", None)
+        page_q1 = quantize_page(1, "tab_w0", None)
         w2p_w = tile("w2p_w", [P, 2, 2 * H], U8, tag="page_g1")
         nc.vector.tensor_copy(
             w2p_w[:].bitcast(U16).rearrange("p a (b t m) -> p (a b) t m", b=2, t=PACK),
             w2_w[:].bitcast(U16).rearrange("p a (b m t) -> p (a b) t m", b=2, t=PACK),
         )
-        v_c1 = gather_words(1, "scan1")
+        v_c1 = gather_words(1, "w2_w")
         page_c, page_s = zip(page_q0, page_q1)
         v_c = [v_c0, v_c1]
         v_s = [v_s0, v_s1]
         w2p_s = [w2p_s0, w2p_s1]
 
         a_sb = [tile(f"a_sb{k}", [P, T2], F32) for k in range(8)]
-        x_sb = [tile("x_sb0", [P, PACK, PICKS], F32, tag="page0"), tile("x_sb1", [P, PACK, PICKS], F32)]
+        x_sb = [tile("x_sb0", [P, PACK, PICKS], F32, tag="tab_w1"), tile("x_sb1", [P, PACK, PICKS], F32)]
         b_sb = [tile(f"b_sb{b}", [P, PACK, PICKS], F32) for b in range(2)]
 
-        def make_x(k):
+        def make_a(k, h):
             b, t = divmod(k, PACK)
-            cols = slice(t * P, (t + 1) * P)
-            for h in range(2):
-                acc = bank(f"a{k}_{h}", BANK)
-                nc.tensor.matmul_mx(
-                    out=acc[:],
-                    lhsT=w1_c[:, k * P : (k + 1) * P].bitcast(FP8X4),
-                    lhsT_scale=w1_s[b][:, cols],
-                    rhs=page_c[h][:].bitcast(FP8X4),
-                    rhs_scale=page_s[h][:],
-                    start=True,
-                    stop=True,
-                )
-                nc.scalar.activation(
-                    a_sb[k][:, h * BANK : (h + 1) * BANK], acc[:], IDENTITY, bias=neg_clear[:, k : k + 1], scale=1.0
-                )
+            acc = bank(f"a{k}_{h}", BANK)
+            nc.tensor.matmul_mx(
+                out=acc[:],
+                lhsT=w1_c[:, k * P : (k + 1) * P].bitcast(FP8X4),
+                lhsT_scale=w1_s[b][:, t * P : (t + 1) * P],
+                rhs=page_c[h][:].bitcast(FP8X4),
+                rhs_scale=page_s[h][:],
+                start=True,
+                stop=True,
+            )
+            nc.scalar.activation(
+                a_sb[k][:, h * BANK : (h + 1) * BANK], acc[:], IDENTITY, bias=neg_clear[:, k : k + 1], scale=1.0
+            )
+
+        def pick(k):
+            b, t = divmod(k, PACK)
             nc.vector.tensor_copy(x_sb[b][:, t, :], a_sb[k][:].indirect(idx3[:]))
+
+        def make_x(k):
+            make_a(k, 0)
+            make_a(k, 1)
+            pick(k)
 
         def make_b(k):
             b, t = divmod(k, PACK)
@@ -216,20 +221,25 @@ def tile_list_free_space_fusion_kernel(
             )
             return z_g
 
-        def quantize_z(b, j0, width, z_g):
-            z_c = tile(f"z_c{b}_{j0}", [P, width], U32)
+        def quantize_z(b, j0, width, z_g, tag=None):
+            z_c = tile(f"z_c{b}_{j0}", [P, width], U32, tag=tag)
             z_s = tile(f"z_s{b}_{j0}", [P, width], U8)
             nc.vector.quantize_mx(out=z_c[:].bitcast(FP8X4), scales=z_s[:], in_=z_g[:])
             return z_c, z_s
 
-        for k in range(6):
+        for k in range(3):
+            make_a(k, 0)
+        for k in range(3):
+            make_a(k, 1)
+            pick(k)
+        for k in range(3, 6):
             make_x(k)
         for k in range(4):
             make_b(k)
         z0 = make_z(0, 0, PICKS)
         make_x(6)
-        z0_c, z0_s = quantize_z(0, 0, PICKS, z0)
         make_x(7)
+        z0_c, z0_s = quantize_z(0, 0, PICKS, z0, tag="a_sb7")
         for k in range(4, 8):
             make_b(k)
         z1 = [make_z(1, h * HALF, HALF) for h in range(2)]

@@ -43,11 +43,14 @@ def tile_list_free_space_fusion_kernel(
 
         tab_s = tile("tab_s", [P, T], U8)
         w2_s = tile("w2_s", [P, H], U8)
+        for rows in (tab_s, w2_s):
+            nc.vector.memset(rows[32:64, :].bitcast(I32), 0)
+            nc.vector.memset(rows[64:P, :].bitcast(I32), 0)
+        v_s = tile("v_s", [P, 2, PICKS], U8)
+        w2p_s = tile("w2p_s", [P, 2, H], U8)
         w3_s = tile("w3_s", [P, N], U8)
-        v_s1 = tile("v_s1", [P, PICKS], U8)
-        w2p_s1 = tile("w2p_s1", [P, H], U8)
-        for plane in (tab_s, w2_s, w3_s, v_s1, w2p_s1):
-            nc.vector.memset(plane[:].bitcast(I32), 0)
+        for plane in (v_s, w2p_s, w3_s):
+            nc.gpsimd.memset(plane[:].bitcast(I32), 0)
 
         base_rows = base.rearrange("(p t) c -> p t c", t=PACK)
         xs_rows = xs.rearrange("(p t) c -> p t c", t=PACK)
@@ -64,14 +67,20 @@ def tile_list_free_space_fusion_kernel(
         def load_w1(q):
             nc.sync.dma_start(w1_raw[q][:], w1_rows[:, :, q * HALF : (q + 1) * HALF])
 
-        def load_scales(plane, scales):
-            for q in range(4):
-                nc.gpsimd.dma_start(
-                    plane[32 * q : 32 * q + 8, :].bitcast(I32), scales[:, 4 * q : 4 * q + 4, :].bitcast(I32)
-                )
+        def spread_scales(queue, planes, rows):
+            for a in range(2):
+                for q in range(4):
+                    first = 16 * a + 4 * q
+                    queue.dma_start(
+                        planes[32 * q : 32 * q + 4, a, :].bitcast(I32), rows[first : first + 4, :].bitcast(I32)
+                    )
 
+        nc.sync.dma_start(idx[:], offs)
+        nc.sync.dma_start(tab_s[0:32, :].bitcast(I32), tab_scales.rearrange("a q t -> (a q) t").bitcast(I32))
+        nc.sync.dma_start(w2_s[0:32, :].bitcast(I32), w2_scales.rearrange("a q c -> (a q) c").bitcast(I32))
         nc.sync.dma_start(idx2[:], offs2)
         load_plane(0)
+        nc.sync.dma_start(clear_t[:], clear.rearrange("(b p t) -> p b t", p=P, t=PACK))
         load_w1(0)
         load_plane(1)
         load_w1(1)
@@ -79,7 +88,6 @@ def tile_list_free_space_fusion_kernel(
         load_plane(2)
         load_w1(3)
         load_plane(3)
-        nc.sync.dma_start(idx[:], offs)
         tab_w = [tile(f"tab_w{a}", [P, T], I32) for a in range(2)]
         w2_w = tile("w2_w", [P, 2, 2 * H], U8)
         w3_w = tile("w3_w", [P, 2, N], I32)
@@ -88,10 +96,20 @@ def tile_list_free_space_fusion_kernel(
         nc.sync.dma_start(tab_w[1][:], tab_words[1].rearrange("p t i -> p (t i)").bitcast(I32))
         nc.sync.dma_start(idx3[:], offs3)
         nc.sync.dma_start(w3_w[:], w3_words.rearrange("a p c i -> p a (c i)").bitcast(I32))
-        nc.gpsimd.dma_start(clear_t[:], clear.rearrange("(b p t) -> p b t", p=P, t=PACK))
-        load_scales(tab_s, tab_scales)
-        load_scales(w2_s, w2_scales)
-        load_scales(w3_s, w3_scales)
+        for q in range(4):
+            nc.sync.dma_start(
+                w3_s[32 * q : 32 * q + 8, :].bitcast(I32), w3_scales[:, 4 * q : 4 * q + 4, :].bitcast(I32)
+            )
+
+        v_rows = tile("v_rows", [P, PICKS], U8)
+        nc.vector.tensor_copy(v_rows[:], tab_s[:].indirect(idx[:]))
+        spread_scales(nc.gpsimd, v_s, v_rows)
+        w2p_rows = tile("w2p_rows", [P, H], U8)
+        nc.vector.tensor_copy(
+            w2p_rows[:].rearrange("p (b t m) -> p b t m", b=2, t=PACK),
+            w2_s[:].rearrange("p (b m t) -> p b t m", b=2, t=PACK),
+        )
+        spread_scales(nc.sync, w2p_s, w2p_rows)
 
         w1_g = [tile(f"w1_g{b}", [P, PACK * K_PASS], BF16) for b in range(2)]
 
@@ -104,7 +122,8 @@ def tile_list_free_space_fusion_kernel(
 
         group_w1(0)
         group_w1(1)
-        pairs = [tile(f"pairs{h}", [P, 2, BANK, 2], BF16, tag=f"w1_raw{h}") for h in range(2)]
+        group_w1(2)
+        pairs = [tile(f"pairs{h}", [P, 2, BANK, 2], BF16, tag=f"w1_raw{h + 1}") for h in range(2)]
 
         page_g = [tile(f"page_g{h}", [P, PACK * BANK], BF16) for h in range(2)]
 
@@ -120,9 +139,8 @@ def tile_list_free_space_fusion_kernel(
 
         scatter(0)
         scatter(1)
-        group_w1(2)
-        group_w1(3)
         scatter(2)
+        group_w1(3)
         scatter(3)
 
         neg_clear = tile("neg_clear", [P, 2 * PACK], F32)
@@ -133,15 +151,6 @@ def tile_list_free_space_fusion_kernel(
         for b in range(2):
             nc.vector.quantize_mx(out=w1_c[:, b * K_PASS : (b + 1) * K_PASS].bitcast(FP8X4), scales=w1_s[b][:], in_=w1_g[b][:])
 
-        v_s0 = tile("v_s0", [P, PICKS], U8, tag="w1_g0")
-        nc.vector.tensor_copy(v_s0[:], tab_s[:].indirect(idx[:]))
-        nc.gpsimd.dma_start(v_s1[0:100, :].bitcast(I32), v_s0[4:104, :].bitcast(I32))
-        w2p_s0 = tile("w2p_s0", [P, H], U8, tag="w1_g1")
-        nc.vector.tensor_copy(
-            w2p_s0[:].rearrange("p (b t m) -> p b t m", b=2, t=PACK),
-            w2_s[:].rearrange("p (b m t) -> p b t m", b=2, t=PACK),
-        )
-        nc.gpsimd.dma_start(w2p_s1[0:100, :].bitcast(I32), w2p_s0[4:104, :].bitcast(I32))
         def quantize_page(h, codes_tag, scales_tag):
             codes = tile(f"page_c{h}", [P, BANK], U32, tag=codes_tag)
             scales = tile(f"page_s{h}", [P, BANK], U8, tag=scales_tag)
@@ -153,19 +162,17 @@ def tile_list_free_space_fusion_kernel(
             nc.vector.tensor_copy(words[:], tab_w[a][:].bitcast(U32).indirect(idx[:]))
             return words
 
-        page_q0 = quantize_page(0, "tab_s", "w2_s")
-        v_c0 = gather_words(0, "page_g0")
-        page_q1 = quantize_page(1, "tab_w0", None)
-        w2p_w = tile("w2p_w", [P, 2, 2 * H], U8, tag="page_g1")
+        v_c0 = gather_words(0, None)
+        page_q0 = quantize_page(0, "tab_w0", None)
+        w2p_w = tile("w2p_w", [P, 2, 2 * H], U8)
         nc.vector.tensor_copy(
             w2p_w[:].bitcast(U16).rearrange("p a (b t m) -> p (a b) t m", b=2, t=PACK),
             w2_w[:].bitcast(U16).rearrange("p a (b m t) -> p (a b) t m", b=2, t=PACK),
         )
-        v_c1 = gather_words(1, "w2_w")
+        page_q1 = quantize_page(1, "w2_w", None)
+        v_c1 = gather_words(1, None)
         page_c, page_s = zip(page_q0, page_q1)
         v_c = [v_c0, v_c1]
-        v_s = [v_s0, v_s1]
-        w2p_s = [w2p_s0, w2p_s1]
 
         a_sb = [tile(f"a_sb{k}", [P, T2], F32) for k in range(8)]
         x_sb = [tile("x_sb0", [P, PACK, PICKS], F32, tag="tab_w1"), tile("x_sb1", [P, PACK, PICKS], F32)]
@@ -197,19 +204,22 @@ def tile_list_free_space_fusion_kernel(
             pick(k)
 
         def make_b(k):
-            b, t = divmod(k, PACK)
             acc = bank(f"b{k}", BANK)
             for a in range(2):
                 nc.tensor.matmul_mx(
                     out=acc[:],
                     lhsT=w2p_w[:, a, 2 * k * P : 2 * (k + 1) * P].bitcast(FP4X4),
-                    lhsT_scale=w2p_s[a][:, k * P : (k + 1) * P],
+                    lhsT_scale=w2p_s[:, a, k * P : (k + 1) * P],
                     rhs=v_c[a][:].bitcast(FP8X4),
-                    rhs_scale=v_s[a][:],
+                    rhs_scale=v_s[:, a, :],
                     start=(a == 0),
                     stop=(a == 1),
                 )
-            nc.scalar.activation(b_sb[b][:, t, :], acc[:], IDENTITY, bias=neg_clear[:, k : k + 1], scale=1.0)
+            return acc
+
+        def take_b(k, acc, cols):
+            b, t = divmod(k, PACK)
+            nc.scalar.activation(b_sb[b][:, t, cols], acc[:, cols], IDENTITY, bias=neg_clear[:, k : k + 1], scale=1.0)
 
         def make_z(b, j0, width):
             z_g = tile(f"z_g{b}_{j0}", [P, PACK * width], BF16)
@@ -235,47 +245,53 @@ def tile_list_free_space_fusion_kernel(
         for k in range(3, 6):
             make_x(k)
         for k in range(4):
-            make_b(k)
+            take_b(k, make_b(k), slice(0, PICKS))
         z0 = make_z(0, 0, PICKS)
         make_x(6)
         make_x(7)
         z0_c, z0_s = quantize_z(0, 0, PICKS, z0, tag="a_sb7")
-        for k in range(4, 8):
-            make_b(k)
-        z1 = [make_z(1, h * HALF, HALF) for h in range(2)]
-        z1_q = [quantize_z(1, h * HALF, HALF, z1[h]) for h in range(2)]
+        b_acc = {k: make_b(k) for k in range(4, 8)}
+        pieces = [(0, 256), (256, 128), (384, 128)]
+        for h in range(2):
+            for k in range(4, 8):
+                take_b(k, b_acc[k], slice(h * HALF, (h + 1) * HALF))
+        z1 = [make_z(1, *pieces[0]), make_z(1, *pieces[1])]
+        z1_q = [quantize_z(1, *pieces[0], z1[0])]
+        z1.append(make_z(1, *pieces[2]))
+        z1_q.extend(quantize_z(1, *pieces[i], z1[i]) for i in (1, 2))
 
-        accs = {}
-        for h in range(2):
-            for n in range(4):
-                accs[h, n] = bank(f"o{h}_{n}", HALF)
-                nc.tensor.matmul_mx(
-                    out=accs[h, n][:],
-                    lhsT=w3_w[:, 0, n * P : (n + 1) * P].bitcast(FP8X4),
-                    lhsT_scale=w3_s[:, n * P : (n + 1) * P],
-                    rhs=z0_c[:, h * HALF : (h + 1) * HALF].bitcast(FP8X4),
-                    rhs_scale=z0_s[:, h * HALF : (h + 1) * HALF],
-                    start=True,
-                    stop=False,
-                )
         out_rows = out.rearrange("(n p) j -> p n j", p=P)
-        for h in range(2):
-            z_c, z_s = z1_q[h]
+
+        def out_pass(acc, n, a, z_c, z_s):
+            nc.tensor.matmul_mx(
+                out=acc[:],
+                lhsT=w3_w[:, a, n * P : (n + 1) * P].bitcast(FP8X4),
+                lhsT_scale=w3_s[4 * a : P, n * P : (n + 1) * P],
+                rhs=z_c.bitcast(FP8X4),
+                rhs_scale=z_s,
+                start=(a == 0),
+                stop=(a == 1),
+            )
+
+        def open_piece(i):
+            j0, width = pieces[i]
+            accs = [bank(f"o{i}_{n}", width) for n in range(4)]
             for n in range(4):
-                nc.tensor.matmul_mx(
-                    out=accs[h, n][:],
-                    lhsT=w3_w[:, 1, n * P : (n + 1) * P].bitcast(FP8X4),
-                    lhsT_scale=w3_s[4:P, n * P : (n + 1) * P],
-                    rhs=z_c[:].bitcast(FP8X4),
-                    rhs_scale=z_s[:],
-                    start=False,
-                    stop=True,
-                )
-            for e in range(2):
-                res = tile(f"res{h}_{e}", [P, 2, HALF], F32)
-                for i in range(2):
-                    if e == 0 or h == 0:
-                        nc.scalar.copy(res[:, i, :], accs[h, 2 * i + e][:])
-                    else:
-                        nc.vector.tensor_copy(res[:, i, :], accs[h, 2 * i + e][:])
-                nc.sync.dma_start(out_rows[:, e:4:2, h * HALF : (h + 1) * HALF], res[:])
+                out_pass(accs[n], n, 0, z0_c[:, j0 : j0 + width], z0_s[:, j0 : j0 + width])
+            return accs
+
+        def close_piece(i, accs):
+            j0, width = pieces[i]
+            res = tile(f"res{i}", [P, 4, width], F32)
+            for n in range(4):
+                out_pass(accs[n], n, 1, z1_q[i][0][:], z1_q[i][1][:])
+                if i == len(pieces) - 1 and n % 2 == 1:
+                    nc.vector.tensor_copy(res[:, n, :], accs[n][:])
+                else:
+                    nc.scalar.copy(res[:, n, :], accs[n][:])
+            nc.sync.dma_start(out_rows[:, :, j0 : j0 + width], res[:])
+
+        accs = [open_piece(0), open_piece(1)]
+        close_piece(0, accs[0])
+        close_piece(1, accs[1])
+        close_piece(2, open_piece(2))

@@ -29,13 +29,12 @@ def tile_list_free_space_fusion_kernel(
     nc = tc.nc
     with ExitStack() as ctx:
         sb = ctx.enter_context(tc.tile_pool(name="sb", bufs=1))
-        psum = ctx.enter_context(tc.psum_pool(name="psum", bufs=8))
+        psum = ctx.enter_context(tc.psum_pool(name="psum", bufs=1))
 
         def tile(name, shape, dtype, tag=None):
             return sb.tile(shape, dtype, name=name, tag=tag or name, align_bytes=64)
 
-        def bank(name, width):
-            return psum.tile([P, width], F32, name=name, tag="bank")
+        banks = [psum.tile([P, BANK], F32, name=f"bank{number}") for number in range(8)]
 
         idx = tile("idx", [P, PICKS // 16], U16)
         idx2 = tile("idx2", [P, S // 16], U16)
@@ -57,7 +56,13 @@ def tile_list_free_space_fusion_kernel(
         w1_rows = w1.rearrange("(p j) r -> p j r", j=PACK)
         page = [tile(f"page{t}", [P, T2], F32) for t in range(PACK)]
         scan = [tile(f"scan{t}", [P, S], F32) for t in range(PACK)]
-        w1_raw = [tile(f"w1_raw{q}", [P, PACK, HALF], F32) for q in range(4)]
+        pairs = tile("pairs", [P, 2, 2 * T2], BF16)
+        w1_raw = [
+            pairs[:, q // 2, :].bitcast(F32).rearrange("p (j c) -> p j c", j=PACK)
+            if q % 2 == 0
+            else tile(f"w1_raw{q}", [P, PACK, HALF], F32)[:]
+            for q in range(4)
+        ]
         clear_t = tile("clear_t", [P, 2, PACK], F32)
 
         def load_plane(t):
@@ -65,7 +70,7 @@ def tile_list_free_space_fusion_kernel(
             nc.sync.dma_start(page[t][:], base_rows[:, t, :])
 
         def load_w1(q):
-            nc.sync.dma_start(w1_raw[q][:], w1_rows[:, :, q * HALF : (q + 1) * HALF])
+            nc.sync.dma_start(w1_raw[q], w1_rows[:, :, q * HALF : (q + 1) * HALF])
 
         def spread_scales(queue, planes, rows):
             for a in range(2):
@@ -75,41 +80,46 @@ def tile_list_free_space_fusion_kernel(
                         planes[32 * q : 32 * q + 4, a, :].bitcast(I32), rows[first : first + 4, :].bitcast(I32)
                     )
 
+        tab_w = [tile(f"tab_w{a}", [P, T], I32) for a in range(2)]
+        w2_w = [tile(f"w2_w{b}", [P, 2, H], U8) for b in range(2)]
+        w2_rows = w2_words.rearrange("a p (b c) -> p b a c", b=2)
+        w3_w = tile("w3_w", [P, 2, N], I32)
         nc.sync.dma_start(idx[:], offs)
         nc.sync.dma_start(tab_s[0:32, :].bitcast(I32), tab_scales.rearrange("a q t -> (a q) t").bitcast(I32))
         nc.sync.dma_start(w2_s[0:32, :].bitcast(I32), w2_scales.rearrange("a q c -> (a q) c").bitcast(I32))
         nc.sync.dma_start(idx2[:], offs2)
-        load_plane(0)
-        nc.sync.dma_start(clear_t[:], clear.rearrange("(b p t) -> p b t", p=P, t=PACK))
-        load_w1(0)
-        load_plane(1)
-        load_w1(1)
-        load_w1(2)
-        load_plane(2)
+        for t in range(PACK - 1):
+            load_plane(t)
+            load_w1(t)
         load_w1(3)
         load_plane(3)
-        tab_w = [tile(f"tab_w{a}", [P, T], I32) for a in range(2)]
-        w2_w = tile("w2_w", [P, 2, 2 * H], U8)
-        w3_w = tile("w3_w", [P, 2, N], I32)
-        nc.sync.dma_start(tab_w[0][:], tab_words[0].rearrange("p t i -> p (t i)").bitcast(I32))
-        nc.sync.dma_start(w2_w[:].bitcast(I32), w2_words.rearrange("a p c -> p a c").bitcast(I32))
-        nc.sync.dma_start(tab_w[1][:], tab_words[1].rearrange("p t i -> p (t i)").bitcast(I32))
+        nc.sync.dma_start(clear_t[:], clear.rearrange("(b p t) -> p b t", p=P, t=PACK))
+        for a in range(2):
+            nc.sync.dma_start(w2_w[a][:].bitcast(I32), w2_rows[:, a].bitcast(I32))
+            nc.sync.dma_start(tab_w[a][:], tab_words[a].rearrange("p t i -> p (t i)").bitcast(I32))
         nc.sync.dma_start(idx3[:], offs3)
-        nc.sync.dma_start(w3_w[:], w3_words.rearrange("a p c i -> p a (c i)").bitcast(I32))
-        for q in range(4):
-            nc.sync.dma_start(
-                w3_s[32 * q : 32 * q + 8, :].bitcast(I32), w3_scales[:, 4 * q : 4 * q + 4, :].bitcast(I32)
-            )
 
         v_rows = tile("v_rows", [P, PICKS], U8)
         nc.vector.tensor_copy(v_rows[:], tab_s[:].indirect(idx[:]))
-        spread_scales(nc.gpsimd, v_s, v_rows)
         w2p_rows = tile("w2p_rows", [P, H], U8)
-        nc.vector.tensor_copy(
+        nc.gpsimd.tensor_copy(
             w2p_rows[:].rearrange("p (b t m) -> p b t m", b=2, t=PACK),
             w2_s[:].rearrange("p (b m t) -> p b t m", b=2, t=PACK),
         )
+        spread_scales(nc.gpsimd, v_s, v_rows)
         spread_scales(nc.sync, w2p_s, w2p_rows)
+
+        def deal_w2(b, tag):
+            dealt = tile(f"w2p_w{b}", [P, 2, H], U8, tag=tag)
+            for a in range(2):
+                for u in range(2):
+                    nc.gpsimd.tensor_copy(
+                        dealt[:, a, :].rearrange("p (t m e) -> p t m e", t=PACK, e=2)[:, 2 * u : 2 * u + 2],
+                        w2_w[b][:, a, :].rearrange("p (m t e) -> p t m e", t=PACK, e=2)[:, 2 * u : 2 * u + 2],
+                    )
+            return dealt
+
+        w2p_w = [deal_w2(0, None)]
 
         w1_g = [tile(f"w1_g{b}", [P, PACK * K_PASS], BF16) for b in range(2)]
 
@@ -117,39 +127,50 @@ def tile_list_free_space_fusion_kernel(
             b, half = divmod(q, 2)
             nc.scalar.copy(
                 w1_g[b][:].rearrange("p (u e m j) -> p u m j e", u=2, e=2, j=PACK)[:, :, half * 64 : (half + 1) * 64],
-                w1_raw[q][:].rearrange("p j (m u e) -> p u m j e", u=2, e=2),
+                w1_raw[q].rearrange("p j (m u e) -> p u m j e", u=2, e=2),
             )
 
         group_w1(0)
-        group_w1(1)
-        group_w1(2)
-        pairs = [tile(f"pairs{h}", [P, 2, BANK, 2], BF16, tag=f"w1_raw{h + 1}") for h in range(2)]
-
         page_g = [tile(f"page_g{h}", [P, PACK * BANK], BF16) for h in range(2)]
 
         def scatter(t):
             nc.vector.tensor_copy(page[t][:].indirect(idx2[:]), scan[t][:])
-            for h in range(2):
-                nc.scalar.copy(pairs[h][:, t // 2, :, t % 2], page[t][:, h * BANK : (h + 1) * BANK])
-                if t == PACK - 1:
-                    nc.scalar.copy(
-                        page_g[h][:].bitcast(F32).rearrange("p (c u) -> p c u", u=2),
-                        pairs[h][:].rearrange("p u c e -> p u (c e)").bitcast(F32).rearrange("p u c -> p c u"),
-                    )
 
-        scatter(0)
-        scatter(1)
-        scatter(2)
+        def round_plane(t, c0, width):
+            lane = pairs[:, t // 2, :].rearrange("p (c e) -> p c e", e=2)[:, c0 : c0 + width, t % 2]
+            nc.scalar.copy(lane, page[t][:, c0 : c0 + width])
+
+        def weave_page(h):
+            nc.scalar.copy(
+                page_g[h][:].bitcast(F32).rearrange("p (c u) -> p c u", u=2),
+                pairs[:].bitcast(F32)[:, :, h * BANK : (h + 1) * BANK].rearrange("p u c -> p c u"),
+            )
+
+        for t in range(PACK):
+            scatter(t)
+        round_plane(0, 0, T2)
+        group_w1(1)
+        round_plane(1, 0, T2)
+        group_w1(2)
         group_w1(3)
-        scatter(3)
+        round_plane(2, 0, T2)
+        for h in range(2):
+            round_plane(3, h * BANK, BANK)
+            weave_page(h)
+
+        nc.sync.dma_start(w3_w[:], w3_words.rearrange("a p c i -> p a (c i)").bitcast(I32))
+        for q in range(4):
+            nc.sync.dma_start(
+                w3_s[32 * q : 32 * q + 8, :].bitcast(I32), w3_scales[:, 4 * q : 4 * q + 4, :].bitcast(I32)
+            )
 
         neg_clear = tile("neg_clear", [P, 2 * PACK], F32)
         nc.scalar.mul(neg_clear[:], clear_t[:].rearrange("p b t -> p (b t)"), -1.0)
 
-        w1_c = tile("w1_c", [P, H], U32, tag="scan3")
-        w1_s = [tile(f"w1_s{b}", [P, K_PASS], U8) for b in range(2)]
+        w1_c = tile("w1_c", [P, 2, K_PASS], U32, tag="scan3")
+        w1_s = tile("w1_s", [P, 2, K_PASS], U8)
         for b in range(2):
-            nc.vector.quantize_mx(out=w1_c[:, b * K_PASS : (b + 1) * K_PASS].bitcast(FP8X4), scales=w1_s[b][:], in_=w1_g[b][:])
+            nc.vector.quantize_mx(out=w1_c[:, b, :].bitcast(FP8X4), scales=w1_s[:, b, :], in_=w1_g[b][:])
 
         def quantize_page(h, codes_tag, scales_tag):
             codes = tile(f"page_c{h}", [P, BANK], U32, tag=codes_tag)
@@ -164,27 +185,27 @@ def tile_list_free_space_fusion_kernel(
 
         v_c0 = gather_words(0, None)
         page_q0 = quantize_page(0, "tab_w0", None)
-        w2p_w = tile("w2p_w", [P, 2, 2 * H], U8)
-        nc.vector.tensor_copy(
-            w2p_w[:].bitcast(U16).rearrange("p a (b t m) -> p (a b) t m", b=2, t=PACK),
-            w2_w[:].bitcast(U16).rearrange("p a (b m t) -> p (a b) t m", b=2, t=PACK),
-        )
-        page_q1 = quantize_page(1, "w2_w", None)
-        v_c1 = gather_words(1, None)
+        page_q1 = quantize_page(1, "page_g0", None)
+        v_c1 = gather_words(1, "pairs")
+        w2p_w.append(deal_w2(1, "tab_w1"))
         page_c, page_s = zip(page_q0, page_q1)
         v_c = [v_c0, v_c1]
 
         a_sb = [tile(f"a_sb{k}", [P, T2], F32) for k in range(8)]
-        x_sb = [tile("x_sb0", [P, PACK, PICKS], F32, tag="tab_w1"), tile("x_sb1", [P, PACK, PICKS], F32)]
-        b_sb = [tile(f"b_sb{b}", [P, PACK, PICKS], F32) for b in range(2)]
+        x0 = tile("x0", [P, PACK, PICKS], F32)
+        b0 = tile("b0", [P, PACK, PICKS], F32)
+        shared = tile("shared", [P, PACK + 2, PICKS], F32)
+        x1 = shared[:, 0:PACK, :]
+        b1_lo = shared[:, 2 : PACK + 2, HALF:PICKS]
+        b1_hi = tile("b1_hi", [P, PACK, HALF], F32)
 
-        def make_a(k, h):
+        def make_a(k, h, number):
             b, t = divmod(k, PACK)
-            acc = bank(f"a{k}_{h}", BANK)
+            acc = banks[number]
             nc.tensor.matmul_mx(
                 out=acc[:],
-                lhsT=w1_c[:, k * P : (k + 1) * P].bitcast(FP8X4),
-                lhsT_scale=w1_s[b][:, t * P : (t + 1) * P],
+                lhsT=w1_c[:, b, t * P : (t + 1) * P].bitcast(FP8X4),
+                lhsT_scale=w1_s[:, b, t * P : (t + 1) * P],
                 rhs=page_c[h][:].bitcast(FP8X4),
                 rhs_scale=page_s[h][:],
                 start=True,
@@ -194,21 +215,15 @@ def tile_list_free_space_fusion_kernel(
                 a_sb[k][:, h * BANK : (h + 1) * BANK], acc[:], IDENTITY, bias=neg_clear[:, k : k + 1], scale=1.0
             )
 
-        def pick(k):
-            b, t = divmod(k, PACK)
-            nc.vector.tensor_copy(x_sb[b][:, t, :], a_sb[k][:].indirect(idx3[:]))
-
-        def make_x(k):
-            make_a(k, 0)
-            make_a(k, 1)
-            pick(k)
+        def pick(k, dst, j0, width):
+            nc.vector.tensor_copy(dst, a_sb[k][:].indirect(idx3[:, j0 // 16 : (j0 + width) // 16]))
 
         def make_b(k):
-            acc = bank(f"b{k}", BANK)
+            acc = banks[(4 + k) % 8]
             for a in range(2):
                 nc.tensor.matmul_mx(
                     out=acc[:],
-                    lhsT=w2p_w[:, a, 2 * k * P : 2 * (k + 1) * P].bitcast(FP4X4),
+                    lhsT=w2p_w[k // PACK][:, a, 2 * (k % PACK) * P : 2 * (k % PACK + 1) * P].bitcast(FP4X4),
                     lhsT_scale=w2p_s[:, a, k * P : (k + 1) * P],
                     rhs=v_c[a][:].bitcast(FP8X4),
                     rhs_scale=v_s[:, a, :],
@@ -217,81 +232,95 @@ def tile_list_free_space_fusion_kernel(
                 )
             return acc
 
-        def take_b(k, acc, cols):
-            b, t = divmod(k, PACK)
-            nc.scalar.activation(b_sb[b][:, t, cols], acc[:, cols], IDENTITY, bias=neg_clear[:, k : k + 1], scale=1.0)
+        def take_b(k, dst, src):
+            nc.scalar.activation(dst, src, IDENTITY, bias=neg_clear[:, k : k + 1], scale=1.0)
 
-        def make_z(b, j0, width):
-            z_g = tile(f"z_g{b}_{j0}", [P, PACK * width], BF16)
+        def make_z(z_g, x, b):
             nc.vector.tensor_tensor(
-                z_g[:].rearrange("p (c i t) -> p c t i", i=2, t=PACK),
-                x_sb[b][:, :, j0 : j0 + width].rearrange("p t (c i) -> p c t i", i=2),
-                b_sb[b][:, :, j0 : j0 + width].rearrange("p t (c i) -> p c t i", i=2),
+                z_g.rearrange("p (c i t) -> p c t i", i=4, t=PACK),
+                x.rearrange("p t (c i) -> p c t i", i=4),
+                b.rearrange("p t (c i) -> p c t i", i=4),
                 MAX,
             )
-            return z_g
 
-        def quantize_z(b, j0, width, z_g, tag=None):
-            z_c = tile(f"z_c{b}_{j0}", [P, width], U32, tag=tag)
-            z_s = tile(f"z_s{b}_{j0}", [P, width], U8)
-            nc.vector.quantize_mx(out=z_c[:].bitcast(FP8X4), scales=z_s[:], in_=z_g[:])
+        def quantize_z(name, width, z_g, tag=None):
+            z_c = tile(f"z_c{name}", [P, width], U32, tag=tag)
+            z_s = tile(f"z_s{name}", [P, width], U8)
+            nc.vector.quantize_mx(out=z_c[:].bitcast(FP8X4), scales=z_s[:], in_=z_g)
             return z_c, z_s
 
-        for k in range(3):
-            make_a(k, 0)
-        for k in range(3):
-            make_a(k, 1)
-            pick(k)
-        for k in range(3, 6):
-            make_x(k)
-        for k in range(4):
-            take_b(k, make_b(k), slice(0, PICKS))
-        z0 = make_z(0, 0, PICKS)
-        make_x(6)
-        make_x(7)
-        z0_c, z0_s = quantize_z(0, 0, PICKS, z0, tag="a_sb7")
-        b_acc = {k: make_b(k) for k in range(4, 8)}
+        make_a(0, 0, 0)
+        make_a(1, 0, 1)
+        for k in range(6):
+            if k > 1:
+                make_a(k, 0, 2 * k % 4)
+            make_a(k, 1, (2 + k if k < 2 else 2 * k + 1) % 4)
+            pick(k, x0[:, k, :] if k < PACK else x1[:, k - PACK, :], 0, PICKS)
+        for k in range(PACK):
+            take_b(k, b0[:, k, :], make_b(k)[:])
+        z0_g = tile("z0_g", [P, PACK * PICKS], BF16)
+        make_z(z0_g[:], x0[:], b0[:])
+        for k in range(6, 8):
+            for h in range(2):
+                make_a(k, h, 4 + 2 * (k - 6) + h)
+            pick(k, x1[:, k - PACK, 0:HALF], 0, HALF)
+            if k == 6:
+                z0_c, z0_s = quantize_z("0", PICKS, z0_g[:], tag=None)
+        b_acc = [make_b(k) for k in range(4, 8)]
+        for t in range(PACK):
+            take_b(4 + t, b1_lo[:, t, :], b_acc[t][:, 0:HALF])
+        for t in range(PACK):
+            take_b(4 + t, b1_hi[:, t, :], b_acc[t][:, HALF:PICKS])
+
         pieces = [(0, 256), (256, 128), (384, 128)]
-        for h in range(2):
-            for k in range(4, 8):
-                take_b(k, b_acc[k], slice(h * HALF, (h + 1) * HALF))
-        z1 = [make_z(1, *pieces[0]), make_z(1, *pieces[1])]
-        z1_q = [quantize_z(1, *pieces[0], z1[0])]
-        z1.append(make_z(1, *pieces[2]))
-        z1_q.extend(quantize_z(1, *pieces[i], z1[i]) for i in (1, 2))
+        z1_g = [tile(f"z1_g{i}", [P, PACK * width], BF16) for i, (j0, width) in enumerate(pieces)]
+        make_z(z1_g[0][:], x1[:, :, 0:HALF], b1_lo)
+        pick(6, x1[:, 2, HALF:PICKS], HALF, HALF)
+        z1_q = [quantize_z("1_0", pieces[0][1], z1_g[0][:])]
+        pick(7, x1[:, 3, HALF:PICKS], HALF, HALF)
+        for i in (1, 2):
+            j0, width = pieces[i]
+            make_z(z1_g[i][:], x1[:, :, j0 : j0 + width], b1_hi[:, :, j0 - HALF : j0 - HALF + width])
+        z1_q.extend(quantize_z(f"1_{i}", pieces[i][1], z1_g[i][:]) for i in (1, 2))
 
         out_rows = out.rearrange("(n p) j -> p n j", p=P)
 
-        def out_pass(acc, n, a, z_c, z_s):
+        def out_pass(acc, n, a, z_c, z_s, start, stop):
             nc.tensor.matmul_mx(
-                out=acc[:],
+                out=acc,
                 lhsT=w3_w[:, a, n * P : (n + 1) * P].bitcast(FP8X4),
                 lhsT_scale=w3_s[4 * a : P, n * P : (n + 1) * P],
                 rhs=z_c.bitcast(FP8X4),
                 rhs_scale=z_s,
-                start=(a == 0),
-                stop=(a == 1),
+                start=start,
+                stop=stop,
             )
+
+        piece_banks = [(4, 5), (6, 7), (0, 1)]
 
         def open_piece(i):
             j0, width = pieces[i]
-            accs = [bank(f"o{i}_{n}", width) for n in range(4)]
+            per = 4 // len(piece_banks[i])
+            accs = [banks[number][:, 0 : per * width].rearrange("p (m j) -> p m j", m=per) for number in piece_banks[i]]
             for n in range(4):
-                out_pass(accs[n], n, 0, z0_c[:, j0 : j0 + width], z0_s[:, j0 : j0 + width])
+                g, m = divmod(n, per)
+                out_pass(accs[g][:, m, :], n, 0, z0_c[:, j0 : j0 + width], z0_s[:, j0 : j0 + width], m == 0, False)
             return accs
 
         def close_piece(i, accs):
             j0, width = pieces[i]
+            per = 4 // len(accs)
             res = tile(f"res{i}", [P, 4, width], F32)
             for n in range(4):
-                out_pass(accs[n], n, 1, z1_q[i][0][:], z1_q[i][1][:])
-                if i == len(pieces) - 1 and n % 2 == 1:
-                    nc.vector.tensor_copy(res[:, n, :], accs[n][:])
+                g, m = divmod(n, per)
+                out_pass(accs[g][:, m, :], n, 1, z1_q[i][0][:], z1_q[i][1][:], False, m == per - 1)
+            for g in range(len(accs)):
+                if i > 0 and g == 1:
+                    nc.vector.tensor_copy(res[:, g * per : (g + 1) * per, :], accs[g])
                 else:
-                    nc.scalar.copy(res[:, n, :], accs[n][:])
+                    nc.scalar.copy(res[:, g * per : (g + 1) * per, :], accs[g])
             nc.sync.dma_start(out_rows[:, :, j0 : j0 + width], res[:])
 
-        accs = [open_piece(0), open_piece(1)]
-        close_piece(0, accs[0])
-        close_piece(1, accs[1])
-        close_piece(2, open_piece(2))
+        accs = [open_piece(i) for i in range(len(pieces))]
+        for i in range(len(pieces)):
+            close_piece(i, accs[i])

@@ -15,6 +15,8 @@ FP8X4 = mybir.dt.float8_e4m3fn_x4
 FP4X4 = mybir.dt.float4_e2m1fn_x4
 IDENTITY = mybir.ActivationFunctionType.Identity
 MAX = mybir.AluOpType.max
+ADD = mybir.AluOpType.add
+MULT = mybir.AluOpType.mult
 
 P = 128
 PACK = 4
@@ -88,6 +90,13 @@ def tile_list_free_space_fusion_kernel(
         nc.sync.dma_start(tab_s[0:32, :].bitcast(I32), tab_scales.rearrange("a q t -> (a q) t").bitcast(I32))
         nc.sync.dma_start(w2_s[0:32, :].bitcast(I32), w2_scales.rearrange("a q c -> (a q) c").bitcast(I32))
         nc.sync.dma_start(idx2[:], offs2)
+
+        def load_w2(b):
+            nc.sync.dma_start(w2_w[b][:].bitcast(I32), w2_rows[:, b].bitcast(I32))
+
+        def load_table(a):
+            nc.sync.dma_start(tab_w[a][:], tab_words[a].rearrange("p t i -> p (t i)").bitcast(I32))
+
         for t in range(PACK - 1):
             load_plane(t)
             load_w1(t)
@@ -95,8 +104,8 @@ def tile_list_free_space_fusion_kernel(
         load_plane(3)
         nc.sync.dma_start(clear_t[:], clear.rearrange("(b p t) -> p b t", p=P, t=PACK))
         for a in range(2):
-            nc.sync.dma_start(w2_w[a][:].bitcast(I32), w2_rows[:, a].bitcast(I32))
-            nc.sync.dma_start(tab_w[a][:], tab_words[a].rearrange("p t i -> p (t i)").bitcast(I32))
+            load_w2(a)
+            load_table(a)
         nc.sync.dma_start(idx3[:], offs3)
 
         v_rows = tile("v_rows", [P, PICKS], U8)
@@ -125,10 +134,9 @@ def tile_list_free_space_fusion_kernel(
 
         def group_w1(q):
             b, half = divmod(q, 2)
-            nc.scalar.copy(
-                w1_g[b][:].rearrange("p (u e m j) -> p u m j e", u=2, e=2, j=PACK)[:, :, half * 64 : (half + 1) * 64],
-                w1_raw[q].rearrange("p j (m u e) -> p u m j e", u=2, e=2),
-            )
+            dst = w1_g[b][:].rearrange("p (u e m j) -> p u m j e", u=2, e=2, j=PACK)[:, :, half * 64 : (half + 1) * 64]
+            src = w1_raw[q].rearrange("p j (m u e) -> p u m j e", u=2, e=2)
+            nc.scalar.copy(dst, src)
 
         group_w1(0)
         page_g = [tile(f"page_g{h}", [P, PACK * BANK], BF16) for h in range(2)]
@@ -167,7 +175,7 @@ def tile_list_free_space_fusion_kernel(
         neg_clear = tile("neg_clear", [P, 2 * PACK], F32)
         nc.scalar.mul(neg_clear[:], clear_t[:].rearrange("p b t -> p (b t)"), -1.0)
 
-        w1_c = tile("w1_c", [P, 2, K_PASS], U32, tag="scan3")
+        w1_c = tile("w1_c", [P, 2, K_PASS], U32, tag="page2")
         w1_s = tile("w1_s", [P, 2, K_PASS], U8)
         for b in range(2):
             nc.vector.quantize_mx(out=w1_c[:, b, :].bitcast(FP8X4), scales=w1_s[:, b, :], in_=w1_g[b][:])
@@ -193,10 +201,9 @@ def tile_list_free_space_fusion_kernel(
 
         a_sb = [tile(f"a_sb{k}", [P, T2], F32) for k in range(8)]
         x0 = tile("x0", [P, PACK, PICKS], F32)
-        b0 = tile("b0", [P, PACK, PICKS], F32)
-        shared = tile("shared", [P, PACK + 2, PICKS], F32)
-        x1 = shared[:, 0:PACK, :]
-        b1_lo = shared[:, 2 : PACK + 2, HALF:PICKS]
+        x1 = tile("x1", [P, PACK, PICKS], F32)
+        x1_lo = [x1[:, 0, 0:HALF], x1[:, 1, 0:HALF], x1[:, 2, HALF:PICKS], x1[:, 3, HALF:PICKS]]
+        x1_hi = x1[:, :, HALF:PICKS]
         b1_hi = tile("b1_hi", [P, PACK, HALF], F32)
 
         def make_a(k, h, number):
@@ -218,8 +225,8 @@ def tile_list_free_space_fusion_kernel(
         def pick(k, dst, j0, width):
             nc.vector.tensor_copy(dst, a_sb[k][:].indirect(idx3[:, j0 // 16 : (j0 + width) // 16]))
 
-        def make_b(k):
-            acc = banks[(4 + k) % 8]
+        def make_b(k, number):
+            acc = banks[number]
             for a in range(2):
                 nc.tensor.matmul_mx(
                     out=acc[:],
@@ -249,38 +256,52 @@ def tile_list_free_space_fusion_kernel(
             nc.vector.quantize_mx(out=z_c[:].bitcast(FP8X4), scales=z_s[:], in_=z_g)
             return z_c, z_s
 
+        def max_out_of_psum(k, dst, acc, x):
+            nc.vector.scalar_tensor_tensor(dst, acc, neg_clear[:, k : k + 1], x, ADD, MAX)
+
         make_a(0, 0, 0)
         make_a(1, 0, 1)
-        for k in range(6):
+        for k in range(PACK):
             if k > 1:
                 make_a(k, 0, 2 * k % 4)
             make_a(k, 1, (2 + k if k < 2 else 2 * k + 1) % 4)
-            pick(k, x0[:, k, :] if k < PACK else x1[:, k - PACK, :], 0, PICKS)
+            pick(k, x0[:, k, :], 0, PICKS)
+        make_a(4, 0, 0)
+        z0_rows = tile("z0_rows", [P, PACK, PICKS], BF16)
         for k in range(PACK):
-            take_b(k, b0[:, k, :], make_b(k)[:])
+            max_out_of_psum(k, z0_rows[:, k, :], make_b(k, 4 + k)[:], x0[:, k, :])
         z0_g = tile("z0_g", [P, PACK * PICKS], BF16)
-        make_z(z0_g[:], x0[:], b0[:])
-        for k in range(6, 8):
-            for h in range(2):
-                make_a(k, h, 4 + 2 * (k - 6) + h)
-            pick(k, x1[:, k - PACK, 0:HALF], 0, HALF)
-            if k == 6:
-                z0_c, z0_s = quantize_z("0", PICKS, z0_g[:], tag=None)
-        b_acc = [make_b(k) for k in range(4, 8)]
-        for t in range(PACK):
-            take_b(4 + t, b1_lo[:, t, :], b_acc[t][:, 0:HALF])
+        nc.gpsimd.tensor_scalar(
+            z0_g[:].rearrange("p (c t) -> p c t", t=PACK), z0_rows[:].rearrange("p t c -> p c t"), 1.0, 0.0, MULT, ADD
+        )
+        later = [(k, h) for k in range(4, 8) for h in range(2)][1:]
+        for i, (k, h) in enumerate(later):
+            make_a(k, h, 4 + i % 4)
+            if h == 1:
+                if k < 6:
+                    pick(k, x1[:, k - PACK, :], 0, PICKS)
+                else:
+                    pick(k, x1_lo[k - PACK], 0, HALF)
+        z0_c, z0_s = quantize_z("0", PICKS, z0_g[:])
+        b_acc = [make_b(k, (k - 3) % 4) for k in range(4, 8)]
+        z1_rows = tile("z1_rows", [P, PACK, HALF], BF16, tag="z0_g")
         for t in range(PACK):
             take_b(4 + t, b1_hi[:, t, :], b_acc[t][:, HALF:PICKS])
+        for t in range(PACK):
+            max_out_of_psum(4 + t, z1_rows[:, t, :], b_acc[t][:, 0:HALF], x1_lo[t])
 
         pieces = [(0, 256), (256, 128), (384, 128)]
-        z1_g = [tile(f"z1_g{i}", [P, PACK * width], BF16) for i, (j0, width) in enumerate(pieces)]
-        make_z(z1_g[0][:], x1[:, :, 0:HALF], b1_lo)
-        pick(6, x1[:, 2, HALF:PICKS], HALF, HALF)
+        z1_g = [tile(f"z1_g{i}", [P, PACK * width], BF16, tag=f"z1_g{i // 2}") for i, (j0, width) in enumerate(pieces)]
+        nc.scalar.copy(
+            z1_g[0][:].rearrange("p (c i t) -> p c t i", i=4, t=PACK),
+            z1_rows[:].rearrange("p t (c i) -> p c t i", i=4),
+        )
+        pick(6, x1_hi[:, 2, :], HALF, HALF)
+        pick(7, x1_hi[:, 3, :], HALF, HALF)
         z1_q = [quantize_z("1_0", pieces[0][1], z1_g[0][:])]
-        pick(7, x1[:, 3, HALF:PICKS], HALF, HALF)
         for i in (1, 2):
             j0, width = pieces[i]
-            make_z(z1_g[i][:], x1[:, :, j0 : j0 + width], b1_hi[:, :, j0 - HALF : j0 - HALF + width])
+            make_z(z1_g[i][:], x1_hi[:, :, j0 - HALF : j0 - HALF + width], b1_hi[:, :, j0 - HALF : j0 - HALF + width])
         z1_q.extend(quantize_z(f"1_{i}", pieces[i][1], z1_g[i][:]) for i in (1, 2))
 
         out_rows = out.rearrange("(n p) j -> p n j", p=P)
@@ -296,7 +317,7 @@ def tile_list_free_space_fusion_kernel(
                 stop=stop,
             )
 
-        piece_banks = [(4, 5), (6, 7), (0, 1)]
+        piece_banks = [(7, 4), (5, 6), (1, 2)]
 
         def open_piece(i):
             j0, width = pieces[i]

@@ -23,6 +23,7 @@ PACK = 4
 K_PASS = P * PACK
 BANK = 512
 HALF = 256
+FIRST_BANKS = [(0, 1), (0, 2), (1, 3), (0, 2), (1, 3)]
 
 
 def tile_list_free_space_fusion_kernel(
@@ -130,11 +131,11 @@ def tile_list_free_space_fusion_kernel(
 
         w2p_w = [deal_w2(0, None)]
 
-        w1_g = [tile(f"w1_g{b}", [P, PACK * K_PASS], BF16) for b in range(2)]
+        w1_g = tile("w1_g", [P, 2, PACK * K_PASS], BF16)
 
         def group_w1(q):
             b, half = divmod(q, 2)
-            dst = w1_g[b][:].rearrange("p (u e m j) -> p u m j e", u=2, e=2, j=PACK)[:, :, half * 64 : (half + 1) * 64]
+            dst = w1_g[:, b, :].rearrange("p (u e m j) -> p u m j e", u=2, e=2, j=PACK)[:, :, half * 64 : (half + 1) * 64]
             src = w1_raw[q].rearrange("p j (m u e) -> p u m j e", u=2, e=2)
             nc.scalar.copy(dst, src)
 
@@ -149,7 +150,8 @@ def tile_list_free_space_fusion_kernel(
             nc.scalar.copy(lane, page[t][:, c0 : c0 + width])
 
         def weave_page(h):
-            nc.scalar.copy(
+            copy = nc.gpsimd.tensor_copy if h == 0 else nc.scalar.copy
+            copy(
                 page_g[h][:].bitcast(F32).rearrange("p (c u) -> p c u", u=2),
                 pairs[:].bitcast(F32)[:, :, h * BANK : (h + 1) * BANK].rearrange("p u c -> p c u"),
             )
@@ -177,8 +179,11 @@ def tile_list_free_space_fusion_kernel(
 
         w1_c = tile("w1_c", [P, 2, K_PASS], U32, tag="page2")
         w1_s = tile("w1_s", [P, 2, K_PASS], U8)
-        for b in range(2):
-            nc.vector.quantize_mx(out=w1_c[:, b, :].bitcast(FP8X4), scales=w1_s[:, b, :], in_=w1_g[b][:])
+        nc.vector.quantize_mx(
+            out=w1_c[:].rearrange("p b c -> p (b c)").bitcast(FP8X4),
+            scales=w1_s[:].rearrange("p b c -> p (b c)"),
+            in_=w1_g[:].rearrange("p b c -> p (b c)"),
+        )
 
         def quantize_page(h, codes_tag, scales_tag):
             codes = tile(f"page_c{h}", [P, BANK], U32, tag=codes_tag)
@@ -200,10 +205,9 @@ def tile_list_free_space_fusion_kernel(
         v_c = [v_c0, v_c1]
 
         a_sb = [tile(f"a_sb{k}", [P, T2], F32) for k in range(8)]
-        x0 = tile("x0", [P, PACK, PICKS], F32)
-        x1 = tile("x1", [P, PACK, PICKS], F32)
-        x1_lo = [x1[:, 0, 0:HALF], x1[:, 1, 0:HALF], x1[:, 2, HALF:PICKS], x1[:, 3, HALF:PICKS]]
-        x1_hi = x1[:, :, HALF:PICKS]
+        shared = tile("shared", [P, PACK + 2, PICKS], F32)
+        x = shared[:, 0:PACK, :]
+        b1_lo = shared[:, 2 : PACK + 2, HALF:PICKS]
         b1_hi = tile("b1_hi", [P, PACK, HALF], F32)
 
         def make_a(k, h, number):
@@ -259,49 +263,43 @@ def tile_list_free_space_fusion_kernel(
         def max_out_of_psum(k, dst, acc, x):
             nc.vector.scalar_tensor_tensor(dst, acc, neg_clear[:, k : k + 1], x, ADD, MAX)
 
-        make_a(0, 0, 0)
-        make_a(1, 0, 1)
         for k in range(PACK):
-            if k > 1:
-                make_a(k, 0, 2 * k % 4)
-            make_a(k, 1, (2 + k if k < 2 else 2 * k + 1) % 4)
-            pick(k, x0[:, k, :], 0, PICKS)
-        make_a(4, 0, 0)
+            for h in range(2):
+                make_a(k, h, FIRST_BANKS[k][h])
+            pick(k, x[:, k, :], 0, PICKS)
+        make_a(4, 0, FIRST_BANKS[4][0])
         z0_rows = tile("z0_rows", [P, PACK, PICKS], BF16)
         for k in range(PACK):
-            max_out_of_psum(k, z0_rows[:, k, :], make_b(k, 4 + k)[:], x0[:, k, :])
+            max_out_of_psum(k, z0_rows[:, k, :], make_b(k, 4 + k)[:], x[:, k, :])
         z0_g = tile("z0_g", [P, PACK * PICKS], BF16)
         nc.gpsimd.tensor_scalar(
             z0_g[:].rearrange("p (c t) -> p c t", t=PACK), z0_rows[:].rearrange("p t c -> p c t"), 1.0, 0.0, MULT, ADD
         )
         later = [(k, h) for k in range(4, 8) for h in range(2)][1:]
         for i, (k, h) in enumerate(later):
-            make_a(k, h, 4 + i % 4)
+            make_a(k, h, FIRST_BANKS[4][1] if i == 0 else 4 + (i - 1) % 4)
             if h == 1:
-                if k < 6:
-                    pick(k, x1[:, k - PACK, :], 0, PICKS)
-                else:
-                    pick(k, x1_lo[k - PACK], 0, HALF)
+                width = PICKS if k < 6 else HALF
+                pick(k, x[:, k - PACK, 0:width], 0, width)
         z0_c, z0_s = quantize_z("0", PICKS, z0_g[:])
-        b_acc = [make_b(k, (k - 3) % 4) for k in range(4, 8)]
-        z1_rows = tile("z1_rows", [P, PACK, HALF], BF16, tag="z0_g")
+        b_acc = [make_b(k, k - 4) for k in range(4, 8)]
+        for t in range(PACK):
+            take_b(4 + t, b1_lo[:, t, :], b_acc[t][:, 0:HALF])
         for t in range(PACK):
             take_b(4 + t, b1_hi[:, t, :], b_acc[t][:, HALF:PICKS])
-        for t in range(PACK):
-            max_out_of_psum(4 + t, z1_rows[:, t, :], b_acc[t][:, 0:HALF], x1_lo[t])
 
         pieces = [(0, 256), (256, 128), (384, 128)]
-        z1_g = [tile(f"z1_g{i}", [P, PACK * width], BF16, tag=f"z1_g{i // 2}") for i, (j0, width) in enumerate(pieces)]
-        nc.scalar.copy(
-            z1_g[0][:].rearrange("p (c i t) -> p c t i", i=4, t=PACK),
-            z1_rows[:].rearrange("p t (c i) -> p c t i", i=4),
-        )
-        pick(6, x1_hi[:, 2, :], HALF, HALF)
-        pick(7, x1_hi[:, 3, :], HALF, HALF)
+        z1_g = [
+            tile(f"z1_g{i}", [P, PACK * width], BF16, tag="z0_g" if i == 0 else None)
+            for i, (j0, width) in enumerate(pieces)
+        ]
+        make_z(z1_g[0][:], x[:, :, 0:HALF], b1_lo)
+        pick(6, x[:, 2, HALF:PICKS], HALF, HALF)
         z1_q = [quantize_z("1_0", pieces[0][1], z1_g[0][:])]
+        pick(7, x[:, 3, HALF:PICKS], HALF, HALF)
         for i in (1, 2):
             j0, width = pieces[i]
-            make_z(z1_g[i][:], x1_hi[:, :, j0 - HALF : j0 - HALF + width], b1_hi[:, :, j0 - HALF : j0 - HALF + width])
+            make_z(z1_g[i][:], x[:, :, j0 : j0 + width], b1_hi[:, :, j0 - HALF : j0 - HALF + width])
         z1_q.extend(quantize_z(f"1_{i}", pieces[i][1], z1_g[i][:]) for i in (1, 2))
 
         out_rows = out.rearrange("(n p) j -> p n j", p=P)
@@ -317,7 +315,7 @@ def tile_list_free_space_fusion_kernel(
                 stop=stop,
             )
 
-        piece_banks = [(7, 4), (5, 6), (1, 2)]
+        piece_banks = [(6, 7), (4, 5), (0, 1)]
 
         def open_piece(i):
             j0, width = pieces[i]

@@ -60,20 +60,16 @@ def tile_list_free_space_fusion_kernel(
         page = [tile(f"page{t}", [P, T2], F32) for t in range(PACK)]
         scan = [tile(f"scan{t}", [P, S], F32) for t in range(PACK)]
         pairs = tile("pairs", [P, 2, 2 * T2], BF16)
-        w1_raw = [
-            pairs[:, q // 2, :].bitcast(F32).rearrange("p (j c) -> p j c", j=PACK)
-            if q % 2 == 0
-            else tile(f"w1_raw{q}", [P, PACK, HALF], F32)[:]
-            for q in range(4)
-        ]
+        w1_lo = pairs[:].rearrange("p u c -> p (u c)").bitcast(F32).rearrange("p (j c) -> p j c", j=PACK)
+        w1_hi = [tile(f"w1_hi{q}", [P, PACK, HALF], F32) for q in range(2)]
         clear_t = tile("clear_t", [P, 2, PACK], F32)
 
         def load_plane(t):
             nc.sync.dma_start(scan[t][:], xs_rows[:, t, :])
             nc.sync.dma_start(page[t][:], base_rows[:, t, :])
 
-        def load_w1(q):
-            nc.sync.dma_start(w1_raw[q], w1_rows[:, :, q * HALF : (q + 1) * HALF])
+        def load_w1_hi(q):
+            nc.sync.dma_start(w1_hi[q][:], w1_rows[:, :, K_PASS + q * HALF : K_PASS + (q + 1) * HALF])
 
         def spread_scales(queue, planes, rows):
             for a in range(2):
@@ -84,29 +80,26 @@ def tile_list_free_space_fusion_kernel(
                     )
 
         tab_w = [tile(f"tab_w{a}", [P, T], I32) for a in range(2)]
-        w2_w = [tile(f"w2_w{b}", [P, 2, H], U8) for b in range(2)]
-        w2_rows = w2_words.rearrange("a p (b c) -> p b a c", b=2)
+        w2_w = tile("w2_w", [P, 2, 2 * H], U8)
         w3_w = tile("w3_w", [P, 2, N], I32)
         nc.sync.dma_start(idx[:], offs)
         nc.sync.dma_start(tab_s[0:32, :].bitcast(I32), tab_scales.rearrange("a q t -> (a q) t").bitcast(I32))
-        nc.sync.dma_start(w2_s[0:32, :].bitcast(I32), w2_scales.rearrange("a q c -> (a q) c").bitcast(I32))
         nc.sync.dma_start(idx2[:], offs2)
-
-        def load_w2(b):
-            nc.sync.dma_start(w2_w[b][:].bitcast(I32), w2_rows[:, b].bitcast(I32))
 
         def load_table(a):
             nc.sync.dma_start(tab_w[a][:], tab_words[a].rearrange("p t i -> p (t i)").bitcast(I32))
 
-        for t in range(PACK - 1):
-            load_plane(t)
-            load_w1(t)
-        load_w1(3)
-        load_plane(3)
+        load_plane(0)
+        nc.sync.dma_start(w2_s[0:32, :].bitcast(I32), w2_scales.rearrange("a q c -> (a q) c").bitcast(I32))
+        load_plane(1)
+        nc.sync.dma_start(w1_lo, w1_rows[:, :, 0:K_PASS])
+        for q in range(2):
+            load_plane(2 + q)
+            load_w1_hi(q)
         nc.sync.dma_start(clear_t[:], clear.rearrange("(b p t) -> p b t", p=P, t=PACK))
         for a in range(2):
-            load_w2(a)
             load_table(a)
+        nc.sync.dma_start(w2_w[:].bitcast(I32), w2_words.rearrange("a p c -> p a c").bitcast(I32))
         nc.sync.dma_start(idx3[:], offs3)
 
         v_rows = tile("v_rows", [P, PICKS], U8)
@@ -119,27 +112,20 @@ def tile_list_free_space_fusion_kernel(
         spread_scales(nc.gpsimd, v_s, v_rows)
         spread_scales(nc.sync, w2p_s, w2p_rows)
 
-        def deal_w2(b, tag):
-            dealt = tile(f"w2p_w{b}", [P, 2, H], U8, tag=tag)
-            for a in range(2):
-                for u in range(2):
-                    nc.gpsimd.tensor_copy(
-                        dealt[:, a, :].rearrange("p (t m e) -> p t m e", t=PACK, e=2)[:, 2 * u : 2 * u + 2],
-                        w2_w[b][:, a, :].rearrange("p (m t e) -> p t m e", t=PACK, e=2)[:, 2 * u : 2 * u + 2],
-                    )
-            return dealt
-
-        w2p_w = [deal_w2(0, None)]
-
         w1_g = tile("w1_g", [P, 2, PACK * K_PASS], BF16)
 
-        def group_w1(q):
-            b, half = divmod(q, 2)
-            dst = w1_g[:, b, :].rearrange("p (u e m j) -> p u m j e", u=2, e=2, j=PACK)[:, :, half * 64 : (half + 1) * 64]
-            src = w1_raw[q].rearrange("p j (m u e) -> p u m j e", u=2, e=2)
-            nc.scalar.copy(dst, src)
-
-        group_w1(0)
+        nc.scalar.copy(
+            w1_g[:, 0, :].rearrange("p (u e m j) -> p u m j e", u=2, e=2, j=PACK),
+            w1_lo.rearrange("p j (m u e) -> p u m j e", u=2, e=2),
+        )
+        nc.gpsimd.tensor_scalar(
+            w1_g[:, 1, :].rearrange("p (t m j) -> p t m j", t=PACK, j=PACK)[:, :, 64:128],
+            w1_hi[1][:].rearrange("p j (m t) -> p t m j", t=PACK),
+            1.0,
+            0.0,
+            MULT,
+            ADD,
+        )
         page_g = [tile(f"page_g{h}", [P, PACK * BANK], BF16) for h in range(2)]
 
         def scatter(t):
@@ -159,10 +145,11 @@ def tile_list_free_space_fusion_kernel(
         for t in range(PACK):
             scatter(t)
         round_plane(0, 0, T2)
-        group_w1(1)
         round_plane(1, 0, T2)
-        group_w1(2)
-        group_w1(3)
+        nc.scalar.copy(
+            w1_g[:, 1, :].rearrange("p (u e m j) -> p u m j e", u=2, e=2, j=PACK)[:, :, 0:64],
+            w1_hi[0][:].rearrange("p j (m u e) -> p u m j e", u=2, e=2),
+        )
         round_plane(2, 0, T2)
         for h in range(2):
             round_plane(3, h * BANK, BANK)
@@ -196,11 +183,22 @@ def tile_list_free_space_fusion_kernel(
             nc.vector.tensor_copy(words[:], tab_w[a][:].bitcast(U32).indirect(idx[:]))
             return words
 
-        v_c0 = gather_words(0, None)
+        v_c0 = gather_words(0, "w1_g")
         page_q0 = quantize_page(0, "tab_w0", None)
         page_q1 = quantize_page(1, "page_g0", None)
         v_c1 = gather_words(1, "pairs")
-        w2p_w.append(deal_w2(1, "tab_w1"))
+
+        def deal_w2(b, tag):
+            dealt = tile(f"w2p_w{b}", [P, 2, H], U8, tag=tag)
+            for a in range(2):
+                for u in range(2):
+                    nc.gpsimd.tensor_copy(
+                        dealt[:, a, :].rearrange("p (t m e) -> p t m e", t=PACK, e=2)[:, 2 * u : 2 * u + 2],
+                        w2_w[:, a, b * H : (b + 1) * H].rearrange("p (m t e) -> p t m e", t=PACK, e=2)[:, 2 * u : 2 * u + 2],
+                    )
+            return dealt
+
+        w2p_w = [deal_w2(0, "page_g1"), deal_w2(1, "tab_w1")]
         page_c, page_s = zip(page_q0, page_q1)
         v_c = [v_c0, v_c1]
 
@@ -271,17 +269,23 @@ def tile_list_free_space_fusion_kernel(
         z0_rows = tile("z0_rows", [P, PACK, PICKS], BF16)
         for k in range(PACK):
             max_out_of_psum(k, z0_rows[:, k, :], make_b(k, 4 + k)[:], x[:, k, :])
-        z0_g = tile("z0_g", [P, PACK * PICKS], BF16)
-        nc.gpsimd.tensor_scalar(
-            z0_g[:].rearrange("p (c t) -> p c t", t=PACK), z0_rows[:].rearrange("p t c -> p c t"), 1.0, 0.0, MULT, ADD
-        )
+        z0_g = [tile(f"z0_g{h}", [P, PACK * HALF], BF16) for h in range(2)]
+        for h in range(2):
+            nc.gpsimd.tensor_scalar(
+                z0_g[h][:].rearrange("p (c t) -> p c t", t=PACK),
+                z0_rows[:, :, h * HALF : (h + 1) * HALF].rearrange("p t c -> p c t"),
+                1.0,
+                0.0,
+                MULT,
+                ADD,
+            )
         later = [(k, h) for k in range(4, 8) for h in range(2)][1:]
         for i, (k, h) in enumerate(later):
             make_a(k, h, FIRST_BANKS[4][1] if i == 0 else 4 + (i - 1) % 4)
             if h == 1:
                 width = PICKS if k < 6 else HALF
                 pick(k, x[:, k - PACK, 0:width], 0, width)
-        z0_c, z0_s = quantize_z("0", PICKS, z0_g[:])
+        z0_q = [quantize_z("0_0", HALF, z0_g[0][:])]
         b_acc = [make_b(k, k - 4) for k in range(4, 8)]
         for t in range(PACK):
             take_b(4 + t, b1_lo[:, t, :], b_acc[t][:, 0:HALF])
@@ -290,13 +294,14 @@ def tile_list_free_space_fusion_kernel(
 
         pieces = [(0, 256), (256, 128), (384, 128)]
         z1_g = [
-            tile(f"z1_g{i}", [P, PACK * width], BF16, tag="z0_g" if i == 0 else None)
+            tile(f"z1_g{i}", [P, PACK * width], BF16, tag="z0_g0" if i == 0 else None)
             for i, (j0, width) in enumerate(pieces)
         ]
         make_z(z1_g[0][:], x[:, :, 0:HALF], b1_lo)
         pick(6, x[:, 2, HALF:PICKS], HALF, HALF)
         z1_q = [quantize_z("1_0", pieces[0][1], z1_g[0][:])]
         pick(7, x[:, 3, HALF:PICKS], HALF, HALF)
+        z0_q.append(quantize_z("0_1", HALF, z0_g[1][:], tag="z0_g0"))
         for i in (1, 2):
             j0, width = pieces[i]
             make_z(z1_g[i][:], x[:, :, j0 : j0 + width], b1_hi[:, :, j0 - HALF : j0 - HALF + width])
@@ -323,7 +328,9 @@ def tile_list_free_space_fusion_kernel(
             accs = [banks[number][:, 0 : per * width].rearrange("p (m j) -> p m j", m=per) for number in piece_banks[i]]
             for n in range(4):
                 g, m = divmod(n, per)
-                out_pass(accs[g][:, m, :], n, 0, z0_c[:, j0 : j0 + width], z0_s[:, j0 : j0 + width], m == 0, False)
+                z_c, z_s = z0_q[j0 // HALF]
+                cols = slice(j0 % HALF, j0 % HALF + width)
+                out_pass(accs[g][:, m, :], n, 0, z_c[:, cols], z_s[:, cols], m == 0, False)
             return accs
 
         def close_piece(i, accs):
@@ -340,6 +347,7 @@ def tile_list_free_space_fusion_kernel(
                     nc.scalar.copy(res[:, g * per : (g + 1) * per, :], accs[g])
             nc.sync.dma_start(out_rows[:, :, j0 : j0 + width], res[:])
 
-        accs = [open_piece(i) for i in range(len(pieces))]
-        for i in range(len(pieces)):
-            close_piece(i, accs[i])
+        close_piece(0, open_piece(0))
+        accs = [open_piece(i) for i in (1, 2)]
+        for i in (1, 2):
+            close_piece(i, accs[i - 1])

@@ -21,9 +21,15 @@ MULT = mybir.AluOpType.mult
 P = 128
 PACK = 4
 K_PASS = P * PACK
+PASSES = 2
+QUADRANTS = 4
 BANK = 512
-HALF = 256
-FIRST_BANKS = [(0, 1), (0, 2), (1, 3), (0, 2), (1, 3)]
+BANKS = 8
+LIST_ROWS = 16
+HALF = PICKS // 2
+W1_QUARTER = H // 4
+OUT_TILES = N // P
+PIECES = [(0, HALF), (HALF, HALF // 2), (HALF + HALF // 2, HALF // 2)]
 
 
 def tile_list_free_space_fusion_kernel(
@@ -37,22 +43,22 @@ def tile_list_free_space_fusion_kernel(
         def tile(name, shape, dtype, tag=None):
             return sb.tile(shape, dtype, name=name, tag=tag or name, align_bytes=64)
 
-        banks = [psum.tile([P, BANK], F32, name=f"bank{number}") for number in range(8)]
+        banks = [psum.tile([P, BANK], F32, name=f"bank{number}") for number in range(BANKS)]
 
-        idx = tile("idx", [P, PICKS // 16], U16)
-        idx2 = tile("idx2", [P, S // 16], U16)
-        idx3 = tile("idx3", [P, PICKS // 16], U16)
+        idx = tile("idx", [P, PICKS // LIST_ROWS], U16)
+        idx2 = tile("idx2", [P, S // LIST_ROWS], U16)
+        idx3 = tile("idx3", [P, PICKS // LIST_ROWS], U16)
 
         tab_s = tile("tab_s", [P, T], U8)
         w2_s = tile("w2_s", [P, H], U8)
         for rows in (tab_s, w2_s):
             nc.vector.memset(rows[32:64, :].bitcast(I32), 0)
             nc.vector.memset(rows[64:P, :].bitcast(I32), 0)
-        v_s = tile("v_s", [P, 2, PICKS], U8)
-        w2p_s = tile("w2p_s", [P, 2, H], U8)
+        v_s = tile("v_s", [P, PASSES, PICKS], U8)
+        w2_dealt_s = tile("w2_dealt_s", [P, PASSES, H], U8)
         w3_s = tile("w3_s", [P, N], U8)
-        for plane in (v_s, w2p_s, w3_s):
-            nc.gpsimd.memset(plane[:].bitcast(I32), 0)
+        for scales in (v_s, w2_dealt_s, w3_s):
+            nc.gpsimd.memset(scales[:].bitcast(I32), 0)
 
         base_rows = base.rearrange("(p t) c -> p t c", t=PACK)
         xs_rows = xs.rearrange("(p t) c -> p t c", t=PACK)
@@ -61,293 +67,273 @@ def tile_list_free_space_fusion_kernel(
         scan = [tile(f"scan{t}", [P, S], F32) for t in range(PACK)]
         pairs = tile("pairs", [P, 2, 2 * T2], BF16)
         w1_lo = pairs[:].rearrange("p u c -> p (u c)").bitcast(F32).rearrange("p (j c) -> p j c", j=PACK)
-        w1_hi = [tile(f"w1_hi{q}", [P, PACK, HALF], F32) for q in range(2)]
-        clear_t = tile("clear_t", [P, 2, PACK], F32)
+        w1_hi = [tile(f"w1_hi{q}", [P, PACK, W1_QUARTER], F32) for q in range(2)]
+        clear_rows = tile("clear_rows", [P, PASSES, PACK], F32)
+        tab_w = [tile(f"tab_w{a}", [P, T], I32) for a in range(PASSES)]
+        w2_w = tile("w2_w", [P, PASSES, 2 * H], U8)
+        w3_w = tile("w3_w", [P, PASSES, N], I32)
 
-        def load_plane(t):
+        def load_row_set(t):
             nc.sync.dma_start(scan[t][:], xs_rows[:, t, :])
             nc.sync.dma_start(page[t][:], base_rows[:, t, :])
 
-        def load_w1_hi(q):
-            nc.sync.dma_start(w1_hi[q][:], w1_rows[:, :, K_PASS + q * HALF : K_PASS + (q + 1) * HALF])
-
-        def spread_scales(queue, planes, rows):
-            for a in range(2):
-                for q in range(4):
-                    first = 16 * a + 4 * q
-                    queue.dma_start(
-                        planes[32 * q : 32 * q + 4, a, :].bitcast(I32), rows[first : first + 4, :].bitcast(I32)
-                    )
-
-        tab_w = [tile(f"tab_w{a}", [P, T], I32) for a in range(2)]
-        w2_w = tile("w2_w", [P, 2, 2 * H], U8)
-        w3_w = tile("w3_w", [P, 2, N], I32)
         nc.sync.dma_start(idx[:], offs)
         nc.sync.dma_start(tab_s[0:32, :].bitcast(I32), tab_scales.rearrange("a q t -> (a q) t").bitcast(I32))
         nc.sync.dma_start(idx2[:], offs2)
-
-        def load_table(a):
-            nc.sync.dma_start(tab_w[a][:], tab_words[a].rearrange("p t i -> p (t i)").bitcast(I32))
-
-        load_plane(0)
+        load_row_set(0)
         nc.sync.dma_start(w2_s[0:32, :].bitcast(I32), w2_scales.rearrange("a q c -> (a q) c").bitcast(I32))
-        load_plane(1)
+        load_row_set(1)
         nc.sync.dma_start(w1_lo, w1_rows[:, :, 0:K_PASS])
         for q in range(2):
-            load_plane(2 + q)
-            load_w1_hi(q)
-        nc.sync.dma_start(clear_t[:], clear.rearrange("(b p t) -> p b t", p=P, t=PACK))
-        for a in range(2):
-            load_table(a)
+            load_row_set(2 + q)
+            first = K_PASS + q * W1_QUARTER
+            nc.sync.dma_start(w1_hi[q][:], w1_rows[:, :, first : first + W1_QUARTER])
+        nc.sync.dma_start(clear_rows[:], clear.rearrange("(g p t) -> p g t", p=P, t=PACK))
+        for a in range(PASSES):
+            nc.sync.dma_start(tab_w[a][:], tab_words[a].rearrange("p c i -> p (c i)").bitcast(I32))
         nc.sync.dma_start(w2_w[:].bitcast(I32), w2_words.rearrange("a p c -> p a c").bitcast(I32))
         nc.sync.dma_start(idx3[:], offs3)
 
+        def spread_scales(queue, scales, rows):
+            for a in range(PASSES):
+                for quadrant in range(QUADRANTS):
+                    first = 16 * a + PACK * quadrant
+                    queue.dma_start(
+                        scales[32 * quadrant : 32 * quadrant + PACK, a, :].bitcast(I32),
+                        rows[first : first + PACK, :].bitcast(I32),
+                    )
+
         v_rows = tile("v_rows", [P, PICKS], U8)
         nc.vector.tensor_copy(v_rows[:], tab_s[:].indirect(idx[:]))
-        w2p_rows = tile("w2p_rows", [P, H], U8)
+        w2_dealt_rows = tile("w2_dealt_rows", [P, H], U8)
         nc.gpsimd.tensor_copy(
-            w2p_rows[:].rearrange("p (b t m) -> p b t m", b=2, t=PACK),
-            w2_s[:].rearrange("p (b m t) -> p b t m", b=2, t=PACK),
+            w2_dealt_rows[:].rearrange("p (g t m) -> p g t m", g=PASSES, t=PACK),
+            w2_s[:].rearrange("p (g m t) -> p g t m", g=PASSES, t=PACK),
         )
         spread_scales(nc.gpsimd, v_s, v_rows)
-        spread_scales(nc.sync, w2p_s, w2p_rows)
+        spread_scales(nc.sync, w2_dealt_s, w2_dealt_rows)
 
-        w1_g = tile("w1_g", [P, 2, PACK * K_PASS], BF16)
-
+        w1_woven = tile("w1_woven", [P, PASSES, PACK * K_PASS], BF16)
+        quarter_m = W1_QUARTER // PACK
         nc.scalar.copy(
-            w1_g[:, 0, :].rearrange("p (u e m j) -> p u m j e", u=2, e=2, j=PACK),
+            w1_woven[:, 0, :].rearrange("p (u e m j) -> p u m j e", u=2, e=2, j=PACK),
             w1_lo.rearrange("p j (m u e) -> p u m j e", u=2, e=2),
         )
         nc.gpsimd.tensor_scalar(
-            w1_g[:, 1, :].rearrange("p (t m j) -> p t m j", t=PACK, j=PACK)[:, :, 64:128],
+            w1_woven[:, 1, :].rearrange("p (t m j) -> p t m j", t=PACK, j=PACK)[:, :, quarter_m:P],
             w1_hi[1][:].rearrange("p j (m t) -> p t m j", t=PACK),
             1.0,
             0.0,
             MULT,
             ADD,
         )
-        page_g = [tile(f"page_g{h}", [P, PACK * BANK], BF16) for h in range(2)]
 
-        def scatter(t):
-            nc.vector.tensor_copy(page[t][:].indirect(idx2[:]), scan[t][:])
+        page_woven = [tile(f"page_woven{h}", [P, PACK * BANK], BF16) for h in range(2)]
 
-        def round_plane(t, c0, width):
-            lane = pairs[:, t // 2, :].rearrange("p (c e) -> p c e", e=2)[:, c0 : c0 + width, t % 2]
-            nc.scalar.copy(lane, page[t][:, c0 : c0 + width])
+        def round_row_set(t, first, width):
+            lane = pairs[:, t // 2, :].rearrange("p (c e) -> p c e", e=2)[:, first : first + width, t % 2]
+            nc.scalar.copy(lane, page[t][:, first : first + width])
 
-        def weave_page(h):
-            copy = nc.gpsimd.tensor_copy if h == 0 else nc.scalar.copy
+        def weave_page(copy, h):
             copy(
-                page_g[h][:].bitcast(F32).rearrange("p (c u) -> p c u", u=2),
+                page_woven[h][:].bitcast(F32).rearrange("p (c u) -> p c u", u=2),
                 pairs[:].bitcast(F32)[:, :, h * BANK : (h + 1) * BANK].rearrange("p u c -> p c u"),
             )
 
         for t in range(PACK):
-            scatter(t)
-        round_plane(0, 0, T2)
-        round_plane(1, 0, T2)
+            nc.vector.tensor_copy(page[t][:].indirect(idx2[:]), scan[t][:])
+        round_row_set(0, 0, T2)
+        round_row_set(1, 0, T2)
         nc.scalar.copy(
-            w1_g[:, 1, :].rearrange("p (u e m j) -> p u m j e", u=2, e=2, j=PACK)[:, :, 0:64],
+            w1_woven[:, 1, :].rearrange("p (u e m j) -> p u m j e", u=2, e=2, j=PACK)[:, :, 0:quarter_m],
             w1_hi[0][:].rearrange("p j (m u e) -> p u m j e", u=2, e=2),
         )
-        round_plane(2, 0, T2)
-        for h in range(2):
-            round_plane(3, h * BANK, BANK)
-            weave_page(h)
+        round_row_set(2, 0, T2)
+        for h, copy in enumerate((nc.gpsimd.tensor_copy, nc.scalar.copy)):
+            round_row_set(PACK - 1, h * BANK, BANK)
+            weave_page(copy, h)
 
         nc.sync.dma_start(w3_w[:], w3_words.rearrange("a p c i -> p a (c i)").bitcast(I32))
-        for q in range(4):
+        for quadrant in range(QUADRANTS):
             nc.sync.dma_start(
-                w3_s[32 * q : 32 * q + 8, :].bitcast(I32), w3_scales[:, 4 * q : 4 * q + 4, :].bitcast(I32)
+                w3_s[32 * quadrant : 32 * quadrant + PASSES * PACK, :].bitcast(I32),
+                w3_scales[:, PACK * quadrant : PACK * (quadrant + 1), :].bitcast(I32),
             )
 
-        neg_clear = tile("neg_clear", [P, 2 * PACK], F32)
-        nc.scalar.mul(neg_clear[:], clear_t[:].rearrange("p b t -> p (b t)"), -1.0)
+        neg_clear = tile("neg_clear", [P, PASSES * PACK], F32)
+        nc.scalar.mul(neg_clear[:], clear_rows[:].rearrange("p g t -> p (g t)"), -1.0)
 
-        w1_c = tile("w1_c", [P, 2, K_PASS], U32, tag="page2")
-        w1_s = tile("w1_s", [P, 2, K_PASS], U8)
-        nc.vector.quantize_mx(
-            out=w1_c[:].rearrange("p b c -> p (b c)").bitcast(FP8X4),
-            scales=w1_s[:].rearrange("p b c -> p (b c)"),
-            in_=w1_g[:].rearrange("p b c -> p (b c)"),
-        )
-
-        def quantize_page(h, codes_tag, scales_tag):
-            codes = tile(f"page_c{h}", [P, BANK], U32, tag=codes_tag)
-            scales = tile(f"page_s{h}", [P, BANK], U8, tag=scales_tag)
-            nc.vector.quantize_mx(out=codes[:].bitcast(FP8X4), scales=scales[:], in_=page_g[h][:])
+        def quantize(name, woven, tag=None):
+            width = woven.shape[1] // PACK
+            codes = tile(f"{name}_codes", [P, width], U32, tag=tag)
+            scales = tile(f"{name}_scales", [P, width], U8)
+            nc.vector.quantize_mx(out=codes[:].bitcast(FP8X4), scales=scales[:], in_=woven)
             return codes, scales
 
         def gather_words(a, tag):
-            words = tile(f"v_c{a}", [P, PICKS], U32, tag=tag)
+            words = tile(f"v_w{a}", [P, PICKS], U32, tag=tag)
             nc.vector.tensor_copy(words[:], tab_w[a][:].bitcast(U32).indirect(idx[:]))
             return words
 
-        v_c0 = gather_words(0, "w1_g")
-        page_q0 = quantize_page(0, "tab_w0", None)
-        page_q1 = quantize_page(1, "page_g0", None)
-        v_c1 = gather_words(1, "pairs")
+        w1_codes, w1_scales = quantize("w1", w1_woven[:].rearrange("p g c -> p (g c)"), tag="page2")
+        v_w = [gather_words(0, "w1_hi1")]
+        page_q = [quantize("page_half0", page_woven[0][:])]
+        page_q.append(quantize("page_half1", page_woven[1][:], tag="pairs"))
+        v_w.append(gather_words(1, "page_woven0"))
 
-        def deal_w2(b, tag):
-            dealt = tile(f"w2p_w{b}", [P, 2, H], U8, tag=tag)
-            for a in range(2):
+        def deal_w2(g, tag):
+            dealt = tile(f"w2_dealt{g}", [P, PASSES, 2 * K_PASS], U8, tag=tag)
+            for a in range(PASSES):
+                group = w2_w[:, a, 2 * g * K_PASS : 2 * (g + 1) * K_PASS]
                 for u in range(2):
                     nc.gpsimd.tensor_copy(
                         dealt[:, a, :].rearrange("p (t m e) -> p t m e", t=PACK, e=2)[:, 2 * u : 2 * u + 2],
-                        w2_w[:, a, b * H : (b + 1) * H].rearrange("p (m t e) -> p t m e", t=PACK, e=2)[:, 2 * u : 2 * u + 2],
+                        group.rearrange("p (m t e) -> p t m e", t=PACK, e=2)[:, 2 * u : 2 * u + 2],
                     )
             return dealt
 
-        w2p_w = [deal_w2(0, "page_g1"), deal_w2(1, "tab_w1")]
-        page_c, page_s = zip(page_q0, page_q1)
-        v_c = [v_c0, v_c1]
+        w2_dealt = [deal_w2(0, "page_woven1"), deal_w2(1, "tab_w1")]
 
-        a_sb = [tile(f"a_sb{k}", [P, T2], F32) for k in range(8)]
+        a_rows = [tile(f"a_rows{k}", [P, T2], F32) for k in range(PASSES * PACK)]
         shared = tile("shared", [P, PACK + 2, PICKS], F32)
-        x = shared[:, 0:PACK, :]
+        picked = shared[:, 0:PACK, :]
         b1_lo = shared[:, 2 : PACK + 2, HALF:PICKS]
         b1_hi = tile("b1_hi", [P, PACK, HALF], F32)
 
-        def make_a(k, h, number):
-            b, t = divmod(k, PACK)
-            acc = banks[number]
+        def less_clear(k, dst, src):
+            nc.scalar.activation(dst, src, IDENTITY, bias=neg_clear[:, k : k + 1], scale=1.0)
+
+        def make_a(k, h, bank):
+            codes, scales = page_q[h]
             nc.tensor.matmul_mx(
-                out=acc[:],
-                lhsT=w1_c[:, b, t * P : (t + 1) * P].bitcast(FP8X4),
-                lhsT_scale=w1_s[:, b, t * P : (t + 1) * P],
-                rhs=page_c[h][:].bitcast(FP8X4),
-                rhs_scale=page_s[h][:],
+                out=bank[:],
+                lhsT=w1_codes[:, k * P : (k + 1) * P].bitcast(FP8X4),
+                lhsT_scale=w1_scales[:, k * P : (k + 1) * P],
+                rhs=codes[:].bitcast(FP8X4),
+                rhs_scale=scales[:],
                 start=True,
                 stop=True,
             )
-            nc.scalar.activation(
-                a_sb[k][:, h * BANK : (h + 1) * BANK], acc[:], IDENTITY, bias=neg_clear[:, k : k + 1], scale=1.0
-            )
+            less_clear(k, a_rows[k][:, h * BANK : (h + 1) * BANK], bank[:])
 
-        def pick(k, dst, j0, width):
-            nc.vector.tensor_copy(dst, a_sb[k][:].indirect(idx3[:, j0 // 16 : (j0 + width) // 16]))
+        def early_bank(k, h):
+            return banks[h if k == 0 else 2 * h + (k + 1) % 2]
 
-        def make_b(k, number):
-            acc = banks[number]
-            for a in range(2):
+        def pick(k, first, width):
+            offsets = idx3[:, first // LIST_ROWS : (first + width) // LIST_ROWS]
+            nc.vector.tensor_copy(picked[:, k % PACK, first : first + width], a_rows[k][:].indirect(offsets))
+
+        def make_b(k, bank):
+            g, t = divmod(k, PACK)
+            for a in range(PASSES):
                 nc.tensor.matmul_mx(
-                    out=acc[:],
-                    lhsT=w2p_w[k // PACK][:, a, 2 * (k % PACK) * P : 2 * (k % PACK + 1) * P].bitcast(FP4X4),
-                    lhsT_scale=w2p_s[:, a, k * P : (k + 1) * P],
-                    rhs=v_c[a][:].bitcast(FP8X4),
+                    out=bank[:],
+                    lhsT=w2_dealt[g][:, a, 2 * t * P : 2 * (t + 1) * P].bitcast(FP4X4),
+                    lhsT_scale=w2_dealt_s[:, a, k * P : (k + 1) * P],
+                    rhs=v_w[a][:].bitcast(FP8X4),
                     rhs_scale=v_s[:, a, :],
                     start=(a == 0),
-                    stop=(a == 1),
+                    stop=(a == PASSES - 1),
                 )
-            return acc
-
-        def take_b(k, dst, src):
-            nc.scalar.activation(dst, src, IDENTITY, bias=neg_clear[:, k : k + 1], scale=1.0)
-
-        def make_z(z_g, x, b):
-            nc.vector.tensor_tensor(
-                z_g.rearrange("p (c i t) -> p c t i", i=4, t=PACK),
-                x.rearrange("p t (c i) -> p c t i", i=4),
-                b.rearrange("p t (c i) -> p c t i", i=4),
-                MAX,
-            )
-
-        def quantize_z(name, width, z_g, tag=None):
-            z_c = tile(f"z_c{name}", [P, width], U32, tag=tag)
-            z_s = tile(f"z_s{name}", [P, width], U8)
-            nc.vector.quantize_mx(out=z_c[:].bitcast(FP8X4), scales=z_s[:], in_=z_g)
-            return z_c, z_s
-
-        def max_out_of_psum(k, dst, acc, x):
-            nc.vector.scalar_tensor_tensor(dst, acc, neg_clear[:, k : k + 1], x, ADD, MAX)
 
         for k in range(PACK):
             for h in range(2):
-                make_a(k, h, FIRST_BANKS[k][h])
-            pick(k, x[:, k, :], 0, PICKS)
-        make_a(4, 0, FIRST_BANKS[4][0])
+                make_a(k, h, early_bank(k, h))
+            pick(k, 0, PICKS)
+        make_a(PACK, 0, early_bank(PACK, 0))
         z0_rows = tile("z0_rows", [P, PACK, PICKS], BF16)
         for k in range(PACK):
-            max_out_of_psum(k, z0_rows[:, k, :], make_b(k, 4 + k)[:], x[:, k, :])
-        z0_g = [tile(f"z0_g{h}", [P, PACK * HALF], BF16) for h in range(2)]
+            make_b(k, banks[PACK + k])
+            nc.vector.scalar_tensor_tensor(
+                z0_rows[:, k, :], banks[PACK + k][:], neg_clear[:, k : k + 1], picked[:, k, :], ADD, MAX
+            )
+        z0_woven = [tile(f"z0_woven{h}", [P, PACK * HALF], BF16) for h in range(2)]
         for h in range(2):
             nc.gpsimd.tensor_scalar(
-                z0_g[h][:].rearrange("p (c t) -> p c t", t=PACK),
+                z0_woven[h][:].rearrange("p (c t) -> p c t", t=PACK),
                 z0_rows[:, :, h * HALF : (h + 1) * HALF].rearrange("p t c -> p c t"),
                 1.0,
                 0.0,
                 MULT,
                 ADD,
             )
-        later = [(k, h) for k in range(4, 8) for h in range(2)][1:]
-        for i, (k, h) in enumerate(later):
-            make_a(k, h, FIRST_BANKS[4][1] if i == 0 else 4 + (i - 1) % 4)
-            if h == 1:
-                width = PICKS if k < 6 else HALF
-                pick(k, x[:, k - PACK, 0:width], 0, width)
-        z0_q = [quantize_z("0_0", HALF, z0_g[0][:])]
-        b_acc = [make_b(k, k - 4) for k in range(4, 8)]
+
+        split_from = PASSES * PACK - 2
+        make_a(PACK, 1, early_bank(PACK, 1))
+        pick(PACK, 0, PICKS)
+        for k in range(PACK + 1, PASSES * PACK):
+            for h in range(2):
+                make_a(k, h, banks[PACK + (2 * (k - PACK - 1) + h) % PACK])
+            pick(k, 0, PICKS if k < split_from else HALF)
+        z0_q = [quantize("z0_half0", z0_woven[0][:], tag="z0_rows")]
         for t in range(PACK):
-            take_b(4 + t, b1_lo[:, t, :], b_acc[t][:, 0:HALF])
+            make_b(PACK + t, banks[t])
         for t in range(PACK):
-            take_b(4 + t, b1_hi[:, t, :], b_acc[t][:, HALF:PICKS])
+            less_clear(PACK + t, b1_lo[:, t, :], banks[t][:, 0:HALF])
+        for t in range(PACK):
+            less_clear(PACK + t, b1_hi[:, t, :], banks[t][:, HALF:PICKS])
 
-        pieces = [(0, 256), (256, 128), (384, 128)]
-        z1_g = [
-            tile(f"z1_g{i}", [P, PACK * width], BF16, tag="z0_g0" if i == 0 else None)
-            for i, (j0, width) in enumerate(pieces)
-        ]
-        make_z(z1_g[0][:], x[:, :, 0:HALF], b1_lo)
-        pick(6, x[:, 2, HALF:PICKS], HALF, HALF)
-        z1_q = [quantize_z("1_0", pieces[0][1], z1_g[0][:])]
-        pick(7, x[:, 3, HALF:PICKS], HALF, HALF)
-        z0_q.append(quantize_z("0_1", HALF, z0_g[1][:], tag="z0_g0"))
-        for i in (1, 2):
-            j0, width = pieces[i]
-            make_z(z1_g[i][:], x[:, :, j0 : j0 + width], b1_hi[:, :, j0 - HALF : j0 - HALF + width])
-        z1_q.extend(quantize_z(f"1_{i}", pieces[i][1], z1_g[i][:]) for i in (1, 2))
+        z1_woven = [tile(f"z1_woven{i}", [P, PACK * width], BF16) for i, (first, width) in enumerate(PIECES)]
 
-        out_rows = out.rearrange("(n p) j -> p n j", p=P)
-
-        def out_pass(acc, n, a, z_c, z_s, start, stop):
-            nc.tensor.matmul_mx(
-                out=acc,
-                lhsT=w3_w[:, a, n * P : (n + 1) * P].bitcast(FP8X4),
-                lhsT_scale=w3_s[4 * a : P, n * P : (n + 1) * P],
-                rhs=z_c.bitcast(FP8X4),
-                rhs_scale=z_s,
-                start=start,
-                stop=stop,
+        def make_z1(i, b_piece):
+            first, width = PIECES[i]
+            nc.vector.tensor_tensor(
+                z1_woven[i][:].rearrange("p (c n t) -> p c t n", n=4, t=PACK),
+                picked[:, :, first : first + width].rearrange("p t (c n) -> p c t n", n=4),
+                b_piece.rearrange("p t (c n) -> p c t n", n=4),
+                MAX,
             )
 
-        piece_banks = [(6, 7), (4, 5), (0, 1)]
+        make_z1(0, b1_lo)
+        pick(split_from, HALF, HALF)
+        z1_q = [quantize("z1_piece0", z1_woven[0][:])]
+        pick(split_from + 1, HALF, HALF)
+        z0_q.append(quantize("z0_half1", z0_woven[1][:], tag="z1_woven0"))
+        for i in (1, 2):
+            first, width = PIECES[i]
+            make_z1(i, b1_hi[:, :, first - HALF : first - HALF + width])
+        z1_q.extend(quantize(f"z1_piece{i}", z1_woven[i][:]) for i in (1, 2))
+
+        out_rows = out.rearrange("(n p) j -> p n j", p=P)
+        piece_banks = [banks[6:8], banks[4:6], banks[0:2]]
+        per_bank = OUT_TILES // 2
+
+        def piece_sums(i):
+            width = PIECES[i][1]
+            return [bank[:, 0 : per_bank * width].rearrange("p (n j) -> p n j", n=per_bank) for bank in piece_banks[i]]
+
+        def out_passes(i, g, codes, scales):
+            for n in range(OUT_TILES):
+                side, place = divmod(n, per_bank)
+                nc.tensor.matmul_mx(
+                    out=piece_sums(i)[side][:, place, :],
+                    lhsT=w3_w[:, g, n * P : (n + 1) * P].bitcast(FP8X4),
+                    lhsT_scale=w3_s[PACK * g : P, n * P : (n + 1) * P],
+                    rhs=codes.bitcast(FP8X4),
+                    rhs_scale=scales,
+                    start=(g == 0 and place == 0),
+                    stop=(g == PASSES - 1 and place == per_bank - 1),
+                )
 
         def open_piece(i):
-            j0, width = pieces[i]
-            per = 4 // len(piece_banks[i])
-            accs = [banks[number][:, 0 : per * width].rearrange("p (m j) -> p m j", m=per) for number in piece_banks[i]]
-            for n in range(4):
-                g, m = divmod(n, per)
-                z_c, z_s = z0_q[j0 // HALF]
-                cols = slice(j0 % HALF, j0 % HALF + width)
-                out_pass(accs[g][:, m, :], n, 0, z_c[:, cols], z_s[:, cols], m == 0, False)
-            return accs
+            first, width = PIECES[i]
+            codes, scales = z0_q[first // HALF]
+            cols = slice(first % HALF, first % HALF + width)
+            out_passes(i, 0, codes[:, cols], scales[:, cols])
 
-        def close_piece(i, accs):
-            j0, width = pieces[i]
-            per = 4 // len(accs)
-            res = tile(f"res{i}", [P, 4, width], F32)
-            for n in range(4):
-                g, m = divmod(n, per)
-                out_pass(accs[g][:, m, :], n, 1, z1_q[i][0][:], z1_q[i][1][:], False, m == per - 1)
-            for g in range(len(accs)):
-                if i > 0 and g == 1:
-                    nc.vector.tensor_copy(res[:, g * per : (g + 1) * per, :], accs[g])
-                else:
-                    nc.scalar.copy(res[:, g * per : (g + 1) * per, :], accs[g])
-            nc.sync.dma_start(out_rows[:, :, j0 : j0 + width], res[:])
+        def close_piece(i, second_copy):
+            first, width = PIECES[i]
+            res = tile(f"res{i}", [P, OUT_TILES, width], F32)
+            codes, scales = z1_q[i]
+            out_passes(i, 1, codes[:], scales[:])
+            sums = piece_sums(i)
+            nc.scalar.copy(res[:, 0:per_bank, :], sums[0])
+            second_copy(res[:, per_bank:OUT_TILES, :], sums[1])
+            nc.sync.dma_start(out_rows[:, :, first : first + width], res[:])
 
-        close_piece(0, open_piece(0))
-        accs = [open_piece(i) for i in (1, 2)]
+        open_piece(0)
+        close_piece(0, nc.scalar.copy)
         for i in (1, 2):
-            close_piece(i, accs[i - 1])
+            open_piece(i)
+        for i in (1, 2):
+            close_piece(i, nc.vector.tensor_copy)

@@ -28,6 +28,7 @@ BANKS = 8
 LIST_ROWS = 16
 HALF = PICKS // 2
 W1_QUARTER = H // 4
+SCATTER_ORDER = (0, 2, 1, 3)
 OUT_TILES = N // P
 PIECES = [(0, HALF), (HALF, HALF // 2), (HALF + HALF // 2, HALF // 2)]
 
@@ -65,8 +66,9 @@ def tile_list_free_space_fusion_kernel(
         w1_rows = w1.rearrange("(p j) r -> p j r", j=PACK)
         page = [tile(f"page{t}", [P, T2], F32) for t in range(PACK)]
         scan = [tile(f"scan{t}", [P, S], F32) for t in range(PACK)]
-        pairs = tile("pairs", [P, 2, 2 * T2], BF16)
-        w1_lo = pairs[:].rearrange("p u c -> p (u c)").bitcast(F32).rearrange("p (j c) -> p j c", j=PACK)
+        staging = tile("staging", [P, 3, 2 * T2], BF16)
+        pairs = staging[:, 0:2, :]
+        w1_lo = staging[:, 1:3, :].rearrange("p u c -> p (u c)").bitcast(F32).rearrange("p (j c) -> p j c", j=PACK)
         w1_hi = [tile(f"w1_hi{q}", [P, PACK, W1_QUARTER], F32) for q in range(2)]
         clear_rows = tile("clear_rows", [P, PASSES, PACK], F32)
         tab_w = [tile(f"tab_w{a}", [P, T], I32) for a in range(PASSES)]
@@ -80,12 +82,12 @@ def tile_list_free_space_fusion_kernel(
         nc.sync.dma_start(idx[:], offs)
         nc.sync.dma_start(tab_s[0:32, :].bitcast(I32), tab_scales.rearrange("a q t -> (a q) t").bitcast(I32))
         nc.sync.dma_start(idx2[:], offs2)
-        load_row_set(0)
+        load_row_set(SCATTER_ORDER[0])
         nc.sync.dma_start(w2_s[0:32, :].bitcast(I32), w2_scales.rearrange("a q c -> (a q) c").bitcast(I32))
-        load_row_set(1)
+        load_row_set(SCATTER_ORDER[1])
         nc.sync.dma_start(w1_lo, w1_rows[:, :, 0:K_PASS])
         for q in range(2):
-            load_row_set(2 + q)
+            load_row_set(SCATTER_ORDER[2 + q])
             first = K_PASS + q * W1_QUARTER
             nc.sync.dma_start(w1_hi[q][:], w1_rows[:, :, first : first + W1_QUARTER])
         nc.sync.dma_start(clear_rows[:], clear.rearrange("(g p t) -> p g t", p=P, t=PACK))
@@ -110,7 +112,7 @@ def tile_list_free_space_fusion_kernel(
             w2_dealt_rows[:].rearrange("p (g t m) -> p g t m", g=PASSES, t=PACK),
             w2_s[:].rearrange("p (g m t) -> p g t m", g=PASSES, t=PACK),
         )
-        spread_scales(nc.gpsimd, v_s, v_rows)
+        spread_scales(nc.sync, v_s, v_rows)
         spread_scales(nc.sync, w2_dealt_s, w2_dealt_rows)
 
         w1_woven = tile("w1_woven", [P, PASSES, PACK * K_PASS], BF16)
@@ -137,18 +139,18 @@ def tile_list_free_space_fusion_kernel(
         def weave_page(copy, h):
             copy(
                 page_woven[h][:].bitcast(F32).rearrange("p (c u) -> p c u", u=2),
-                pairs[:].bitcast(F32)[:, :, h * BANK : (h + 1) * BANK].rearrange("p u c -> p c u"),
+                pairs.bitcast(F32)[:, :, h * BANK : (h + 1) * BANK].rearrange("p u c -> p c u"),
             )
 
-        for t in range(PACK):
+        for t in SCATTER_ORDER:
             nc.vector.tensor_copy(page[t][:].indirect(idx2[:]), scan[t][:])
-        round_row_set(0, 0, T2)
-        round_row_set(1, 0, T2)
+        round_row_set(SCATTER_ORDER[0], 0, T2)
+        round_row_set(SCATTER_ORDER[1], 0, T2)
         nc.scalar.copy(
             w1_woven[:, 1, :].rearrange("p (u e m j) -> p u m j e", u=2, e=2, j=PACK)[:, :, 0:quarter_m],
             w1_hi[0][:].rearrange("p j (m u e) -> p u m j e", u=2, e=2),
         )
-        round_row_set(2, 0, T2)
+        round_row_set(SCATTER_ORDER[2], 0, T2)
         for h, copy in enumerate((nc.gpsimd.tensor_copy, nc.scalar.copy)):
             round_row_set(PACK - 1, h * BANK, BANK)
             weave_page(copy, h)
@@ -163,11 +165,19 @@ def tile_list_free_space_fusion_kernel(
         neg_clear = tile("neg_clear", [P, PASSES * PACK], F32)
         nc.scalar.mul(neg_clear[:], clear_rows[:].rearrange("p g t -> p (g t)"), -1.0)
 
-        def quantize(name, woven, tag=None):
+        def quantize(name, woven, tag=None, parts=1, codes=None):
             width = woven.shape[1] // PACK
-            codes = tile(f"{name}_codes", [P, width], U32, tag=tag)
-            scales = tile(f"{name}_scales", [P, width], U8)
-            nc.vector.quantize_mx(out=codes[:].bitcast(FP8X4), scales=scales[:], in_=woven)
+            if codes is None:
+                codes = tile(f"{name}_codes", [P, width], U32, tag=tag)[:]
+                tag = None
+            scales = tile(f"{name}_scales", [P, width], U8, tag=tag)
+            step = width // parts
+            for first in range(0, width, step):
+                nc.vector.quantize_mx(
+                    out=codes[:, first : first + step].bitcast(FP8X4),
+                    scales=scales[:, first : first + step],
+                    in_=woven[:, PACK * first : PACK * (first + step)],
+                )
             return codes, scales
 
         def gather_words(a, tag):
@@ -175,10 +185,11 @@ def tile_list_free_space_fusion_kernel(
             nc.vector.tensor_copy(words[:], tab_w[a][:].bitcast(U32).indirect(idx[:]))
             return words
 
-        w1_codes, w1_scales = quantize("w1", w1_woven[:].rearrange("p g c -> p (g c)"), tag="page2")
+        w1_codes, w1_scales = quantize("w1", w1_woven[:].rearrange("p g c -> p (g c)"), tag=f"page{SCATTER_ORDER[2]}")
         v_w = [gather_words(0, "w1_hi1")]
-        page_q = [quantize("page_half0", page_woven[0][:])]
-        page_q.append(quantize("page_half1", page_woven[1][:], tag="pairs"))
+        page_codes = tile("page_codes", [P, T2], U32, tag="tab_w0")
+        page_q = [quantize("page_half0", page_woven[0][:], parts=2, codes=page_codes[:, 0:BANK])]
+        page_q.append(quantize("page_half1", page_woven[1][:], tag="staging", parts=2, codes=page_codes[:, BANK:T2]))
         v_w.append(gather_words(1, "page_woven0"))
 
         def deal_w2(g, tag):
@@ -203,18 +214,18 @@ def tile_list_free_space_fusion_kernel(
         def less_clear(k, dst, src):
             nc.scalar.activation(dst, src, IDENTITY, bias=neg_clear[:, k : k + 1], scale=1.0)
 
-        def make_a(k, h, bank):
+        def make_a(k, h, bank, first=0, width=BANK):
             codes, scales = page_q[h]
             nc.tensor.matmul_mx(
-                out=bank[:],
+                out=bank[:, 0:width],
                 lhsT=w1_codes[:, k * P : (k + 1) * P].bitcast(FP8X4),
                 lhsT_scale=w1_scales[:, k * P : (k + 1) * P],
-                rhs=codes[:].bitcast(FP8X4),
-                rhs_scale=scales[:],
+                rhs=codes[:, first : first + width].bitcast(FP8X4),
+                rhs_scale=scales[:, first : first + width],
                 start=True,
                 stop=True,
             )
-            less_clear(k, a_rows[k][:, h * BANK : (h + 1) * BANK], bank[:])
+            less_clear(k, a_rows[k][:, h * BANK + first : h * BANK + first + width], bank[:, 0:width])
 
         def early_bank(k, h):
             return banks[h if k == 0 else 2 * h + (k + 1) % 2]
@@ -236,7 +247,11 @@ def tile_list_free_space_fusion_kernel(
                     stop=(a == PASSES - 1),
                 )
 
-        for k in range(PACK):
+        for h in range(2):
+            make_a(0, h, banks[h], 0, BANK // 2)
+            make_a(0, h, banks[PACK + h], BANK // 2, BANK // 2)
+        pick(0, 0, PICKS)
+        for k in range(1, PACK):
             for h in range(2):
                 make_a(k, h, early_bank(k, h))
             pick(k, 0, PICKS)

@@ -86,6 +86,7 @@ def tile_list_free_space_fusion_kernel(
         nc.sync.dma_start(w2_s[0:32, :].bitcast(I32), w2_scales.rearrange("a q c -> (a q) c").bitcast(I32))
         load_row_set(SCATTER_ORDER[1])
         nc.sync.dma_start(w1_lo, w1_rows[:, :, 0:K_PASS])
+        nc.sync.dma_start(idx3[:], offs3)
         for q in range(2):
             load_row_set(SCATTER_ORDER[2 + q])
             first = K_PASS + q * W1_QUARTER
@@ -94,7 +95,6 @@ def tile_list_free_space_fusion_kernel(
         for a in range(PASSES):
             nc.sync.dma_start(tab_w[a][:], tab_words[a].rearrange("p c i -> p (c i)").bitcast(I32))
         nc.sync.dma_start(w2_w[:].bitcast(I32), w2_words.rearrange("a p c -> p a c").bitcast(I32))
-        nc.sync.dma_start(idx3[:], offs3)
 
         def spread_scales(queue, scales, rows):
             for a in range(PASSES):
@@ -206,9 +206,9 @@ def tile_list_free_space_fusion_kernel(
         w2_dealt = [deal_w2(0, "page_woven1"), deal_w2(1, "tab_w1")]
 
         a_rows = [tile(f"a_rows{k}", [P, T2], F32) for k in range(PASSES * PACK)]
-        shared = tile("shared", [P, PACK + 2, PICKS], F32)
+        shared = tile("shared", [P, 2 * PACK - 1, PICKS], F32)
         picked = shared[:, 0:PACK, :]
-        b1_lo = shared[:, 2 : PACK + 2, HALF:PICKS]
+        b1_lo = shared[:, PACK - 1 : 2 * PACK - 1, HALF:PICKS]
         b1_hi = tile("b1_hi", [P, PACK, HALF], F32)
 
         def less_clear(k, dst, src):
@@ -248,8 +248,8 @@ def tile_list_free_space_fusion_kernel(
                 )
 
         for h in range(2):
-            make_a(0, h, banks[h], 0, BANK // 2)
-            make_a(0, h, banks[PACK + h], BANK // 2, BANK // 2)
+            make_a(0, h, banks[(4, 1)[h]], 0, BANK // 2)
+            make_a(0, h, banks[(0, 5)[h]], BANK // 2, BANK // 2)
         pick(0, 0, PICKS)
         for k in range(1, PACK):
             for h in range(2):
@@ -273,14 +273,14 @@ def tile_list_free_space_fusion_kernel(
                 ADD,
             )
 
-        split_from = PASSES * PACK - 2
+        split_from = PASSES * PACK - 1
         make_a(PACK, 1, early_bank(PACK, 1))
         pick(PACK, 0, PICKS)
         for k in range(PACK + 1, PASSES * PACK):
             for h in range(2):
                 make_a(k, h, banks[PACK + (2 * (k - PACK - 1) + h) % PACK])
             pick(k, 0, PICKS if k < split_from else HALF)
-        z0_q = [quantize("z0_half0", z0_woven[0][:], tag="z0_rows")]
+        z0_q = [quantize("z0_half0", z0_woven[0][:])]
         for t in range(PACK):
             make_b(PACK + t, banks[t])
         for t in range(PACK):
@@ -300,10 +300,10 @@ def tile_list_free_space_fusion_kernel(
             )
 
         make_z1(0, b1_lo)
-        pick(split_from, HALF, HALF)
+        z0_q.append(quantize("z0_half1", z0_woven[1][:]))
+        pick(split_from, *PIECES[1])
         z1_q = [quantize("z1_piece0", z1_woven[0][:])]
-        pick(split_from + 1, HALF, HALF)
-        z0_q.append(quantize("z0_half1", z0_woven[1][:], tag="z1_woven0"))
+        pick(split_from, *PIECES[2])
         for i in (1, 2):
             first, width = PIECES[i]
             make_z1(i, b1_hi[:, :, first - HALF : first - HALF + width])
@@ -343,8 +343,11 @@ def tile_list_free_space_fusion_kernel(
             out_passes(i, 1, codes[:], scales[:])
             sums = piece_sums(i)
             nc.scalar.copy(res[:, 0:per_bank, :], sums[0])
+            if i == 0:
+                nc.sync.dma_start(out_rows[:, 0:per_bank, first : first + width], res[:, 0:per_bank, :])
             second_copy(res[:, per_bank:OUT_TILES, :], sums[1])
-            nc.sync.dma_start(out_rows[:, :, first : first + width], res[:])
+            rest = slice(per_bank if i == 0 else 0, OUT_TILES)
+            nc.sync.dma_start(out_rows[:, rest, first : first + width], res[:, rest, :])
 
         open_piece(0)
         close_piece(0, nc.scalar.copy)

@@ -27,7 +27,7 @@ BANK = 512
 BANKS = 8
 LIST_ROWS = 16
 HALF = PICKS // 2
-W1_QUARTER = H // 4
+W1_PARTS = (320, 192)
 SCATTER_ORDER = (0, 2, 1, 3)
 OUT_TILES = N // P
 PIECES = [(0, HALF), (HALF, HALF // 2), (HALF + HALF // 2, HALF // 2)]
@@ -69,15 +69,23 @@ def tile_list_free_space_fusion_kernel(
         staging = tile("staging", [P, 3, 2 * T2], BF16)
         pairs = staging[:, 0:2, :]
         w1_lo = staging[:, 1:3, :].rearrange("p u c -> p (u c)").bitcast(F32).rearrange("p (j c) -> p j c", j=PACK)
-        w1_hi = [tile(f"w1_hi{q}", [P, PACK, W1_QUARTER], F32) for q in range(2)]
+        w1_hi = [tile(f"w1_hi{q}", [P, PACK, W1_PARTS[q]], F32) for q in range(2)]
         clear_rows = tile("clear_rows", [P, PASSES, PACK], F32)
         tab_w = [tile(f"tab_w{a}", [P, T], I32) for a in range(PASSES)]
-        w2_w = tile("w2_w", [P, PASSES, 2 * H], U8)
+        w2_w = [tile(f"w2_w{g}", [P, PASSES, 2 * K_PASS], U8) for g in range(PASSES)]
         w3_w = tile("w3_w", [P, PASSES, N], I32)
 
         def load_row_set(t):
             nc.sync.dma_start(scan[t][:], xs_rows[:, t, :])
             nc.sync.dma_start(page[t][:], base_rows[:, t, :])
+
+        def load_w1_hi(q):
+            first = K_PASS + q * W1_PARTS[0]
+            nc.sync.dma_start(w1_hi[q][:], w1_rows[:, :, first : first + W1_PARTS[q]])
+
+        def load_w2(g):
+            words = w2_words.rearrange("a p c -> p a c")[:, :, 2 * g * K_PASS : 2 * (g + 1) * K_PASS]
+            nc.sync.dma_start(w2_w[g][:].bitcast(I32), words.bitcast(I32))
 
         nc.sync.dma_start(idx[:], offs)
         nc.sync.dma_start(tab_s[0:32, :].bitcast(I32), tab_scales.rearrange("a q t -> (a q) t").bitcast(I32))
@@ -87,20 +95,21 @@ def tile_list_free_space_fusion_kernel(
         load_row_set(SCATTER_ORDER[1])
         nc.sync.dma_start(w1_lo, w1_rows[:, :, 0:K_PASS])
         nc.sync.dma_start(idx3[:], offs3)
-        for q in range(2):
-            load_row_set(SCATTER_ORDER[2 + q])
-            first = K_PASS + q * W1_QUARTER
-            nc.sync.dma_start(w1_hi[q][:], w1_rows[:, :, first : first + W1_QUARTER])
+        load_row_set(SCATTER_ORDER[2])
+        load_w1_hi(0)
+        load_w2(0)
+        load_row_set(SCATTER_ORDER[3])
+        load_w1_hi(1)
         nc.sync.dma_start(clear_rows[:], clear.rearrange("(g p t) -> p g t", p=P, t=PACK))
         for a in range(PASSES):
             nc.sync.dma_start(tab_w[a][:], tab_words[a].rearrange("p c i -> p (c i)").bitcast(I32))
-        nc.sync.dma_start(w2_w[:].bitcast(I32), w2_words.rearrange("a p c -> p a c").bitcast(I32))
+        load_w2(1)
 
-        def spread_scales(queue, scales, rows):
+        def spread_scales(scales, rows):
             for a in range(PASSES):
                 for quadrant in range(QUADRANTS):
                     first = 16 * a + PACK * quadrant
-                    queue.dma_start(
+                    nc.sync.dma_start(
                         scales[32 * quadrant : 32 * quadrant + PACK, a, :].bitcast(I32),
                         rows[first : first + PACK, :].bitcast(I32),
                     )
@@ -112,17 +121,30 @@ def tile_list_free_space_fusion_kernel(
             w2_dealt_rows[:].rearrange("p (g t m) -> p g t m", g=PASSES, t=PACK),
             w2_s[:].rearrange("p (g m t) -> p g t m", g=PASSES, t=PACK),
         )
-        spread_scales(nc.sync, v_s, v_rows)
-        spread_scales(nc.sync, w2_dealt_s, w2_dealt_rows)
+        spread_scales(v_s, v_rows)
+        spread_scales(w2_dealt_s, w2_dealt_rows)
+
+        def deal_w2(g, tag=None):
+            dealt = tile(f"w2_dealt{g}", [P, PASSES, 2 * K_PASS], U8, tag=tag)
+            for a in range(PASSES):
+                group = w2_w[g][:, a, :]
+                for u in range(2):
+                    nc.gpsimd.tensor_copy(
+                        dealt[:, a, :].rearrange("p (t m e) -> p t m e", t=PACK, e=2)[:, 2 * u : 2 * u + 2],
+                        group.rearrange("p (m t e) -> p t m e", t=PACK, e=2)[:, 2 * u : 2 * u + 2],
+                    )
+            return dealt
+
+        w2_dealt = [deal_w2(0)]
 
         w1_woven = tile("w1_woven", [P, PASSES, PACK * K_PASS], BF16)
-        quarter_m = W1_QUARTER // PACK
+        scalar_m = W1_PARTS[0] // PACK
         nc.scalar.copy(
             w1_woven[:, 0, :].rearrange("p (u e m j) -> p u m j e", u=2, e=2, j=PACK),
             w1_lo.rearrange("p j (m u e) -> p u m j e", u=2, e=2),
         )
         nc.gpsimd.tensor_scalar(
-            w1_woven[:, 1, :].rearrange("p (t m j) -> p t m j", t=PACK, j=PACK)[:, :, quarter_m:P],
+            w1_woven[:, 1, :].rearrange("p (t m j) -> p t m j", t=PACK, j=PACK)[:, :, scalar_m:P],
             w1_hi[1][:].rearrange("p j (m t) -> p t m j", t=PACK),
             1.0,
             0.0,
@@ -147,7 +169,7 @@ def tile_list_free_space_fusion_kernel(
         round_row_set(SCATTER_ORDER[0], 0, T2)
         round_row_set(SCATTER_ORDER[1], 0, T2)
         nc.scalar.copy(
-            w1_woven[:, 1, :].rearrange("p (u e m j) -> p u m j e", u=2, e=2, j=PACK)[:, :, 0:quarter_m],
+            w1_woven[:, 1, :].rearrange("p (u e m j) -> p u m j e", u=2, e=2, j=PACK)[:, :, 0:scalar_m],
             w1_hi[0][:].rearrange("p j (m u e) -> p u m j e", u=2, e=2),
         )
         round_row_set(SCATTER_ORDER[2], 0, T2)
@@ -165,18 +187,21 @@ def tile_list_free_space_fusion_kernel(
         neg_clear = tile("neg_clear", [P, PASSES * PACK], F32)
         nc.scalar.mul(neg_clear[:], clear_rows[:].rearrange("p g t -> p (g t)"), -1.0)
 
-        def quantize(name, woven, tag=None, parts=1, codes=None):
+        def quantize(name, woven, tag=None):
             width = woven.shape[1] // PACK
-            if codes is None:
-                codes = tile(f"{name}_codes", [P, width], U32, tag=tag)[:]
-                tag = None
-            scales = tile(f"{name}_scales", [P, width], U8, tag=tag)
-            step = width // parts
-            for first in range(0, width, step):
+            codes = tile(f"{name}_codes", [P, width], U32, tag=tag)
+            scales = tile(f"{name}_scales", [P, width], U8)
+            nc.vector.quantize_mx(out=codes[:].bitcast(FP8X4), scales=scales[:], in_=woven)
+            return codes, scales
+
+        def quantize_page(h, codes, tag=None):
+            scales = tile(f"page_scales{h}", [P, BANK], U8, tag=tag)
+            for first in (0, BANK // 2):
+                cols = slice(first, first + BANK // 2)
                 nc.vector.quantize_mx(
-                    out=codes[:, first : first + step].bitcast(FP8X4),
-                    scales=scales[:, first : first + step],
-                    in_=woven[:, PACK * first : PACK * (first + step)],
+                    out=codes[:, cols].bitcast(FP8X4),
+                    scales=scales[:, cols],
+                    in_=page_woven[h][:, PACK * first : PACK * (first + BANK // 2)],
                 )
             return codes, scales
 
@@ -188,22 +213,10 @@ def tile_list_free_space_fusion_kernel(
         w1_codes, w1_scales = quantize("w1", w1_woven[:].rearrange("p g c -> p (g c)"), tag=f"page{SCATTER_ORDER[2]}")
         v_w = [gather_words(0, "w1_hi1")]
         page_codes = tile("page_codes", [P, T2], U32, tag="tab_w0")
-        page_q = [quantize("page_half0", page_woven[0][:], parts=2, codes=page_codes[:, 0:BANK])]
-        page_q.append(quantize("page_half1", page_woven[1][:], tag="staging", parts=2, codes=page_codes[:, BANK:T2]))
+        page_q = [quantize_page(0, page_codes[:, 0:BANK]), quantize_page(1, page_codes[:, BANK:T2], tag="staging")]
         v_w.append(gather_words(1, "page_woven0"))
 
-        def deal_w2(g, tag):
-            dealt = tile(f"w2_dealt{g}", [P, PASSES, 2 * K_PASS], U8, tag=tag)
-            for a in range(PASSES):
-                group = w2_w[:, a, 2 * g * K_PASS : 2 * (g + 1) * K_PASS]
-                for u in range(2):
-                    nc.gpsimd.tensor_copy(
-                        dealt[:, a, :].rearrange("p (t m e) -> p t m e", t=PACK, e=2)[:, 2 * u : 2 * u + 2],
-                        group.rearrange("p (m t e) -> p t m e", t=PACK, e=2)[:, 2 * u : 2 * u + 2],
-                    )
-            return dealt
-
-        w2_dealt = [deal_w2(0, "page_woven1"), deal_w2(1, "tab_w1")]
+        w2_dealt.append(deal_w2(1, "page_woven1"))
 
         a_rows = [tile(f"a_rows{k}", [P, T2], F32) for k in range(PASSES * PACK)]
         shared = tile("shared", [P, 2 * PACK - 1, PICKS], F32)
@@ -227,8 +240,9 @@ def tile_list_free_space_fusion_kernel(
             )
             less_clear(k, a_rows[k][:, h * BANK + first : h * BANK + first + width], bank[:, 0:width])
 
-        def early_bank(k, h):
-            return banks[h if k == 0 else 2 * h + (k + 1) % 2]
+        quarter_banks = [banks[number] for number in (6, 0, 1, 5)]
+        half_banks = {1: (0, 6), 2: (5, 4), 3: (1, 7), 4: (0, 2)}
+        b_banks = [banks[number] for number in (6, 5, 4, 7)]
 
         def pick(k, first, width):
             offsets = idx3[:, first // LIST_ROWS : (first + width) // LIST_ROWS]
@@ -247,20 +261,20 @@ def tile_list_free_space_fusion_kernel(
                     stop=(a == PASSES - 1),
                 )
 
-        for h in range(2):
-            make_a(0, h, banks[(4, 1)[h]], 0, BANK // 2)
-            make_a(0, h, banks[(0, 5)[h]], BANK // 2, BANK // 2)
+        for quarter, bank in enumerate(quarter_banks):
+            h, side = divmod(quarter, 2)
+            make_a(0, h, bank, side * BANK // 2, BANK // 2)
         pick(0, 0, PICKS)
         for k in range(1, PACK):
             for h in range(2):
-                make_a(k, h, early_bank(k, h))
+                make_a(k, h, banks[half_banks[k][h]])
             pick(k, 0, PICKS)
-        make_a(PACK, 0, early_bank(PACK, 0))
+        make_a(PACK, 0, banks[half_banks[PACK][0]])
         z0_rows = tile("z0_rows", [P, PACK, PICKS], BF16)
         for k in range(PACK):
-            make_b(k, banks[PACK + k])
+            make_b(k, b_banks[k])
             nc.vector.scalar_tensor_tensor(
-                z0_rows[:, k, :], banks[PACK + k][:], neg_clear[:, k : k + 1], picked[:, k, :], ADD, MAX
+                z0_rows[:, k, :], b_banks[k][:], neg_clear[:, k : k + 1], picked[:, k, :], ADD, MAX
             )
         z0_woven = [tile(f"z0_woven{h}", [P, PACK * HALF], BF16) for h in range(2)]
         for h in range(2):
@@ -273,14 +287,14 @@ def tile_list_free_space_fusion_kernel(
                 ADD,
             )
 
-        split_from = PASSES * PACK - 1
-        make_a(PACK, 1, early_bank(PACK, 1))
+        last = PASSES * PACK - 1
+        make_a(PACK, 1, banks[half_banks[PACK][1]])
         pick(PACK, 0, PICKS)
         for k in range(PACK + 1, PASSES * PACK):
             for h in range(2):
-                make_a(k, h, banks[PACK + (2 * (k - PACK - 1) + h) % PACK])
-            pick(k, 0, PICKS if k < split_from else HALF)
-        z0_q = [quantize("z0_half0", z0_woven[0][:])]
+                make_a(k, h, b_banks[(2 * (k - PACK - 1) + h) % PACK])
+            pick(k, 0, PICKS if k < last else HALF)
+        z0_q = [quantize("z0_half0", z0_woven[0][:], tag="z0_rows")]
         for t in range(PACK):
             make_b(PACK + t, banks[t])
         for t in range(PACK):
@@ -301,16 +315,16 @@ def tile_list_free_space_fusion_kernel(
 
         make_z1(0, b1_lo)
         z0_q.append(quantize("z0_half1", z0_woven[1][:]))
-        pick(split_from, *PIECES[1])
+        pick(last, *PIECES[1])
         z1_q = [quantize("z1_piece0", z1_woven[0][:])]
-        pick(split_from, *PIECES[2])
-        for i in (1, 2):
-            first, width = PIECES[i]
-            make_z1(i, b1_hi[:, :, first - HALF : first - HALF + width])
-        z1_q.extend(quantize(f"z1_piece{i}", z1_woven[i][:]) for i in (1, 2))
+        make_z1(1, b1_hi[:, :, 0 : HALF // 2])
+        pick(last, *PIECES[2])
+        z1_q.append(quantize("z1_piece1", z1_woven[1][:]))
+        make_z1(2, b1_hi[:, :, HALF // 2 : HALF])
+        z1_q.append(quantize("z1_piece2", z1_woven[2][:]))
 
         out_rows = out.rearrange("(n p) j -> p n j", p=P)
-        piece_banks = [banks[6:8], banks[4:6], banks[0:2]]
+        piece_banks = [b_banks[2:4], b_banks[0:2], banks[0:2]]
         per_bank = OUT_TILES // 2
 
         def piece_sums(i):
@@ -336,22 +350,22 @@ def tile_list_free_space_fusion_kernel(
             cols = slice(first % HALF, first % HALF + width)
             out_passes(i, 0, codes[:, cols], scales[:, cols])
 
-        def close_piece(i, second_copy):
+        def close_piece(i, second_copy, store_by_bank=False):
             first, width = PIECES[i]
             res = tile(f"res{i}", [P, OUT_TILES, width], F32)
             codes, scales = z1_q[i]
             out_passes(i, 1, codes[:], scales[:])
             sums = piece_sums(i)
             nc.scalar.copy(res[:, 0:per_bank, :], sums[0])
-            if i == 0:
+            if store_by_bank:
                 nc.sync.dma_start(out_rows[:, 0:per_bank, first : first + width], res[:, 0:per_bank, :])
             second_copy(res[:, per_bank:OUT_TILES, :], sums[1])
-            rest = slice(per_bank if i == 0 else 0, OUT_TILES)
+            rest = slice(per_bank if store_by_bank else 0, OUT_TILES)
             nc.sync.dma_start(out_rows[:, rest, first : first + width], res[:, rest, :])
 
         open_piece(0)
-        close_piece(0, nc.scalar.copy)
+        close_piece(0, nc.scalar.copy, store_by_bank=True)
         for i in (1, 2):
             open_piece(i)
-        for i in (1, 2):
-            close_piece(i, nc.vector.tensor_copy)
+        close_piece(1, nc.scalar.copy)
+        close_piece(2, nc.vector.tensor_copy)

@@ -324,16 +324,20 @@ def tile_list_free_space_fusion_kernel(
         z1_q.append(quantize("z1_piece2", z1_woven[2][:]))
 
         out_rows = out.rearrange("(n p) j -> p n j", p=P)
-        piece_banks = [b_banks[2:4], b_banks[0:2], banks[0:2]]
-        per_bank = OUT_TILES // 2
+        piece_banks = [b_banks[2:4], b_banks[0:2], banks[0:OUT_TILES]]
+
+        def per_bank(i):
+            return OUT_TILES // len(piece_banks[i])
 
         def piece_sums(i):
             width = PIECES[i][1]
-            return [bank[:, 0 : per_bank * width].rearrange("p (n j) -> p n j", n=per_bank) for bank in piece_banks[i]]
+            return [
+                bank[:, 0 : per_bank(i) * width].rearrange("p (n j) -> p n j", n=per_bank(i)) for bank in piece_banks[i]
+            ]
 
         def out_passes(i, g, codes, scales):
             for n in range(OUT_TILES):
-                side, place = divmod(n, per_bank)
+                side, place = divmod(n, per_bank(i))
                 nc.tensor.matmul_mx(
                     out=piece_sums(i)[side][:, place, :],
                     lhsT=w3_w[:, g, n * P : (n + 1) * P].bitcast(FP8X4),
@@ -341,7 +345,7 @@ def tile_list_free_space_fusion_kernel(
                     rhs=codes.bitcast(FP8X4),
                     rhs_scale=scales,
                     start=(g == 0 and place == 0),
-                    stop=(g == PASSES - 1 and place == per_bank - 1),
+                    stop=(g == PASSES - 1 and place == per_bank(i) - 1),
                 )
 
         def open_piece(i):
@@ -350,22 +354,22 @@ def tile_list_free_space_fusion_kernel(
             cols = slice(first % HALF, first % HALF + width)
             out_passes(i, 0, codes[:, cols], scales[:, cols])
 
-        def close_piece(i, second_copy, store_by_bank=False):
+        def close_piece(i, copies, stores):
             first, width = PIECES[i]
             res = tile(f"res{i}", [P, OUT_TILES, width], F32)
             codes, scales = z1_q[i]
             out_passes(i, 1, codes[:], scales[:])
-            sums = piece_sums(i)
-            nc.scalar.copy(res[:, 0:per_bank, :], sums[0])
-            if store_by_bank:
-                nc.sync.dma_start(out_rows[:, 0:per_bank, first : first + width], res[:, 0:per_bank, :])
-            second_copy(res[:, per_bank:OUT_TILES, :], sums[1])
-            rest = slice(per_bank if store_by_bank else 0, OUT_TILES)
-            nc.sync.dma_start(out_rows[:, rest, first : first + width], res[:, rest, :])
+            per_store = OUT_TILES // stores
+            for side, (copy, sums) in enumerate(zip(copies, piece_sums(i))):
+                done = (side + 1) * per_bank(i)
+                copy(res[:, done - per_bank(i) : done, :], sums)
+                if done % per_store == 0:
+                    rows = slice(done - per_store, done)
+                    nc.sync.dma_start(out_rows[:, rows, first : first + width], res[:, rows, :])
 
         open_piece(0)
-        close_piece(0, nc.scalar.copy, store_by_bank=True)
+        close_piece(0, [nc.scalar.copy] * 2, 2)
         for i in (1, 2):
             open_piece(i)
-        close_piece(1, nc.scalar.copy)
-        close_piece(2, nc.vector.tensor_copy)
+        close_piece(1, [nc.scalar.copy] * 2, 1)
+        close_piece(2, [nc.scalar.copy, nc.vector.tensor_copy] * 2, 2)

@@ -17,6 +17,8 @@ IDENTITY = mybir.ActivationFunctionType.Identity
 MAX = mybir.AluOpType.max
 ADD = mybir.AluOpType.add
 MULT = mybir.AluOpType.mult
+SUBTRACT = mybir.AluOpType.subtract
+RELU = mybir.ActivationFunctionType.Relu
 
 P = 128
 PACK = 4
@@ -29,6 +31,7 @@ LIST_ROWS = 16
 HALF = PICKS // 2
 W1_PARTS = (320, 192)
 SCATTER_ORDER = (0, 2, 1, 3)
+PAGE_PARTS = [(0, 512), (512, 256), (768, 256)]
 OUT_TILES = N // P
 PIECES = [(0, HALF), (HALF, HALF // 2), (HALF + HALF // 2, HALF // 2)]
 
@@ -124,13 +127,13 @@ def tile_list_free_space_fusion_kernel(
         spread_scales(v_s, v_rows)
         spread_scales(w2_dealt_s, w2_dealt_rows)
 
-        def deal_w2(g, tag=None):
-            dealt = tile(f"w2_dealt{g}", [P, PASSES, 2 * K_PASS], U8, tag=tag)
+        def deal_w2(g, tags=(None, None)):
+            dealt = [tile(f"w2_dealt{g}{u}", [P, PASSES, K_PASS], U8, tag=tags[u])[:] for u in range(2)]
             for a in range(PASSES):
                 group = w2_w[g][:, a, :]
                 for u in range(2):
                     nc.gpsimd.tensor_copy(
-                        dealt[:, a, :].rearrange("p (t m e) -> p t m e", t=PACK, e=2)[:, 2 * u : 2 * u + 2],
+                        dealt[u][:, a, :].rearrange("p (t m e) -> p t m e", t=2, e=2),
                         group.rearrange("p (m t e) -> p t m e", t=PACK, e=2)[:, 2 * u : 2 * u + 2],
                     )
             return dealt
@@ -152,16 +155,17 @@ def tile_list_free_space_fusion_kernel(
             ADD,
         )
 
-        page_woven = [tile(f"page_woven{h}", [P, PACK * BANK], BF16) for h in range(2)]
+        page_woven = [tile(f"page_woven{i}", [P, PACK * width], BF16) for i, (first, width) in enumerate(PAGE_PARTS)]
 
         def round_row_set(t, first, width):
             lane = pairs[:, t // 2, :].rearrange("p (c e) -> p c e", e=2)[:, first : first + width, t % 2]
             nc.scalar.copy(lane, page[t][:, first : first + width])
 
-        def weave_page(copy, h):
+        def weave_page(copy, i):
+            first, width = PAGE_PARTS[i]
             copy(
-                page_woven[h][:].bitcast(F32).rearrange("p (c u) -> p c u", u=2),
-                pairs.bitcast(F32)[:, :, h * BANK : (h + 1) * BANK].rearrange("p u c -> p c u"),
+                page_woven[i][:].bitcast(F32).rearrange("p (c u) -> p c u", u=2),
+                pairs.bitcast(F32)[:, :, first : first + width].rearrange("p u c -> p c u"),
             )
 
         for t in SCATTER_ORDER:
@@ -173,9 +177,11 @@ def tile_list_free_space_fusion_kernel(
             w1_hi[0][:].rearrange("p j (m u e) -> p u m j e", u=2, e=2),
         )
         round_row_set(SCATTER_ORDER[2], 0, T2)
-        for h, copy in enumerate((nc.gpsimd.tensor_copy, nc.scalar.copy)):
-            round_row_set(PACK - 1, h * BANK, BANK)
-            weave_page(copy, h)
+        round_row_set(PACK - 1, 0, BANK)
+        weave_page(nc.gpsimd.tensor_copy, 0)
+        round_row_set(PACK - 1, BANK, BANK)
+        for i in (1, 2):
+            weave_page(nc.scalar.copy, i)
 
         nc.sync.dma_start(w3_w[:], w3_words.rearrange("a p c i -> p a (c i)").bitcast(I32))
         for quadrant in range(QUADRANTS):
@@ -201,7 +207,7 @@ def tile_list_free_space_fusion_kernel(
                 nc.vector.quantize_mx(
                     out=codes[:, cols].bitcast(FP8X4),
                     scales=scales[:, cols],
-                    in_=page_woven[h][:, PACK * first : PACK * (first + BANK // 2)],
+                    in_=page_woven[0][:, PACK * first : PACK * (first + BANK // 2)] if h == 0 else page_woven[1 + first // HALF][:],
                 )
             return codes, scales
 
@@ -216,9 +222,10 @@ def tile_list_free_space_fusion_kernel(
         page_q = [quantize_page(0, page_codes[:, 0:BANK]), quantize_page(1, page_codes[:, BANK:T2], tag="staging")]
         v_w.append(gather_words(1, "page_woven0"))
 
-        w2_dealt.append(deal_w2(1, "page_woven1"))
+        w2_dealt.append(deal_w2(1, ("page_woven2", "page_woven1")))
 
-        a_rows = [tile(f"a_rows{k}", [P, T2], F32) for k in range(PASSES * PACK)]
+        gap = tile("gap", [P, PICKS], F32)
+        a_rows = [tile(f"a_rows{k}", [P, T2], F32, tag={3: "w2_dealt00", 4: "w2_dealt01", 5: "gap"}.get(k)) for k in range(PASSES * PACK)]
         shared = tile("shared", [P, 2 * PACK - 1, PICKS], F32)
         picked = shared[:, 0:PACK, :]
         b1_lo = shared[:, PACK - 1 : 2 * PACK - 1, HALF:PICKS]
@@ -241,41 +248,50 @@ def tile_list_free_space_fusion_kernel(
             less_clear(k, a_rows[k][:, h * BANK + first : h * BANK + first + width], bank[:, 0:width])
 
         quarter_banks = [banks[number] for number in (6, 0, 1, 5)]
-        half_banks = {1: (0, 6), 2: (5, 4), 3: (1, 7), 4: (0, 2)}
-        b_banks = [banks[number] for number in (6, 5, 4, 7)]
+        half_banks = {1: (0, 6), 2: (5, 4), 3: (1, 7), 4: (2, 1), 5: (7, 2), 6: (1, 7), 7: (2, 1)}
+        b_banks = [banks[number] for number in (2, 3, 0, 6)]
 
         def pick(k, first, width):
             offsets = idx3[:, first // LIST_ROWS : (first + width) // LIST_ROWS]
             nc.vector.tensor_copy(picked[:, k % PACK, first : first + width], a_rows[k][:].indirect(offsets))
 
-        def make_b(k, bank):
+        def make_b(k, sums, cols=slice(0, PICKS)):
             g, t = divmod(k, PACK)
-            for a in range(PASSES):
+            for a in reversed(range(PASSES)):
                 nc.tensor.matmul_mx(
-                    out=bank[:],
-                    lhsT=w2_dealt[g][:, a, 2 * t * P : 2 * (t + 1) * P].bitcast(FP4X4),
+                    out=sums,
+                    lhsT=w2_dealt[g][t // 2][:, a, 2 * (t % 2) * P : 2 * (t % 2 + 1) * P].bitcast(FP4X4),
                     lhsT_scale=w2_dealt_s[:, a, k * P : (k + 1) * P],
-                    rhs=v_w[a][:].bitcast(FP8X4),
-                    rhs_scale=v_s[:, a, :],
-                    start=(a == 0),
-                    stop=(a == PASSES - 1),
+                    rhs=v_w[a][:, cols].bitcast(FP8X4),
+                    rhs_scale=v_s[:, a, cols],
+                    start=(a == PASSES - 1),
+                    stop=(a == 0),
                 )
 
         for quarter, bank in enumerate(quarter_banks):
             h, side = divmod(quarter, 2)
             make_a(0, h, bank, side * BANK // 2, BANK // 2)
         pick(0, 0, PICKS)
+        z0_rows = tile("z0_rows", [P, PACK, PICKS], BF16)
+        b0 = tile("b0", [P, PICKS], F32)
+        rise = tile("rise", [P, PICKS], F32)
         for k in range(1, PACK):
             for h in range(2):
                 make_a(k, h, banks[half_banks[k][h]])
             pick(k, 0, PICKS)
-        make_a(PACK, 0, banks[half_banks[PACK][0]])
-        z0_rows = tile("z0_rows", [P, PACK, PICKS], BF16)
-        for k in range(PACK):
-            make_b(k, b_banks[k])
+            if k == 2:
+                make_b(0, b_banks[0][:])
+                less_clear(0, b0[:], b_banks[0][:])
+                nc.gpsimd.tensor_tensor(gap[:], picked[:, 0, :], b0[:], SUBTRACT)
+        for k in range(1, PACK):
+            make_b(k, b_banks[k][:])
             nc.vector.scalar_tensor_tensor(
                 z0_rows[:, k, :], b_banks[k][:], neg_clear[:, k : k + 1], picked[:, k, :], ADD, MAX
             )
+        make_a(PACK, 0, banks[half_banks[PACK][0]])
+        nc.scalar.activation(rise[:], gap[:], RELU)
+        make_a(PACK, 1, banks[half_banks[PACK][1]])
+        nc.gpsimd.tensor_tensor(z0_rows[:, 0, :], rise[:], b0[:], ADD)
         z0_woven = [tile(f"z0_woven{h}", [P, PACK * HALF], BF16) for h in range(2)]
         for h in range(2):
             nc.gpsimd.tensor_scalar(
@@ -288,19 +304,18 @@ def tile_list_free_space_fusion_kernel(
             )
 
         last = PASSES * PACK - 1
-        make_a(PACK, 1, banks[half_banks[PACK][1]])
-        pick(PACK, 0, PICKS)
-        for k in range(PACK + 1, PASSES * PACK):
-            for h in range(2):
-                make_a(k, h, b_banks[(2 * (k - PACK - 1) + h) % PACK])
+        for k in range(PACK, PASSES * PACK):
+            for h in range(2 if k > PACK else 0):
+                make_a(k, h, banks[half_banks[k][h]])
             pick(k, 0, PICKS if k < last else HALF)
-        z0_q = [quantize("z0_half0", z0_woven[0][:], tag="z0_rows")]
-        for t in range(PACK):
-            make_b(PACK + t, banks[t])
-        for t in range(PACK):
-            less_clear(PACK + t, b1_lo[:, t, :], banks[t][:, 0:HALF])
-        for t in range(PACK):
-            less_clear(PACK + t, b1_hi[:, t, :], banks[t][:, HALF:PICKS])
+        z0_q = [quantize("z0_half0", z0_woven[0][:], tag="page_woven2")]
+        for h, (rows, numbers) in enumerate(((b1_lo, (7, 2)), (b1_hi, (1, 7)))):
+            for pair, number in enumerate(numbers):
+                tiles = (2 * pair, 2 * pair + 1)
+                for t in tiles:
+                    make_b(PACK + t, banks[number][:, t % 2 * HALF : (t % 2 + 1) * HALF], slice(h * HALF, (h + 1) * HALF))
+                for t in tiles:
+                    less_clear(PACK + t, rows[:, t, :], banks[number][:, t % 2 * HALF : (t % 2 + 1) * HALF])
 
         z1_woven = [tile(f"z1_woven{i}", [P, PACK * width], BF16) for i, (first, width) in enumerate(PIECES)]
 
@@ -314,7 +329,7 @@ def tile_list_free_space_fusion_kernel(
             )
 
         make_z1(0, b1_lo)
-        z0_q.append(quantize("z0_half1", z0_woven[1][:]))
+        z0_q.append(quantize("z0_half1", z0_woven[1][:], tag="page_woven1"))
         pick(last, *PIECES[1])
         z1_q = [quantize("z1_piece0", z1_woven[0][:])]
         make_z1(1, b1_hi[:, :, 0 : HALF // 2])
@@ -324,7 +339,7 @@ def tile_list_free_space_fusion_kernel(
         z1_q.append(quantize("z1_piece2", z1_woven[2][:]))
 
         out_rows = out.rearrange("(n p) j -> p n j", p=P)
-        piece_banks = [b_banks[2:4], b_banks[0:2], banks[0:OUT_TILES]]
+        piece_banks = [[banks[5], banks[4]], [banks[0], banks[6]], [banks[3], banks[2]]]
 
         def per_bank(i):
             return OUT_TILES // len(piece_banks[i])
@@ -372,4 +387,4 @@ def tile_list_free_space_fusion_kernel(
         for i in (1, 2):
             open_piece(i)
         close_piece(1, [nc.scalar.copy] * 2, 1)
-        close_piece(2, [nc.scalar.copy, nc.vector.tensor_copy] * 2, 2)
+        close_piece(2, [nc.scalar.copy, nc.vector.tensor_copy], 1)

@@ -96,11 +96,11 @@ def tile_list_free_space_fusion_kernel(
         load_row_set(SCATTER_ORDER[0])
         nc.sync.dma_start(w2_s[0:32, :].bitcast(I32), w2_scales.rearrange("a q c -> (a q) c").bitcast(I32))
         load_row_set(SCATTER_ORDER[1])
+        load_w2(0)
         nc.sync.dma_start(w1_lo, w1_rows[:, :, 0:K_PASS])
         nc.sync.dma_start(idx3[:], offs3)
         load_row_set(SCATTER_ORDER[2])
         load_w1_hi(0)
-        load_w2(0)
         load_row_set(SCATTER_ORDER[3])
         load_w1_hi(1)
         nc.sync.dma_start(clear_rows[:], clear.rearrange("(g p t) -> p g t", p=P, t=PACK))
@@ -133,8 +133,8 @@ def tile_list_free_space_fusion_kernel(
                 group = w2_w[g][:, a, :]
                 for u in range(2):
                     nc.gpsimd.tensor_copy(
-                        dealt[u][:, a, :].rearrange("p (t m e) -> p t m e", t=2, e=2),
-                        group.rearrange("p (m t e) -> p t m e", t=PACK, e=2)[:, 2 * u : 2 * u + 2],
+                        dealt[u][:, a, :].bitcast(U16).rearrange("p (t m) -> p t m", t=2),
+                        group.bitcast(U16).rearrange("p (m t) -> p t m", t=PACK)[:, 2 * u : 2 * u + 2],
                     )
             return dealt
 

@@ -31,7 +31,8 @@ LIST_ROWS = 16
 HALF = PICKS // 2
 W1_PARTS = (320, 192)
 SCATTER_ORDER = (0, 2, 1, 3)
-PAGE_PARTS = [(0, 512), (512, 256), (768, 256)]
+PAGE_PARTS = [(0, BANK), (BANK, BANK // 2), (BANK + BANK // 2, BANK // 2)]
+LEAD = S // 4
 OUT_TILES = N // P
 PIECES = [(0, HALF), (HALF, HALF // 2), (HALF + HALF // 2, HALF // 2)]
 
@@ -93,7 +94,11 @@ def tile_list_free_space_fusion_kernel(
         nc.sync.dma_start(idx[:], offs)
         nc.sync.dma_start(tab_s[0:32, :].bitcast(I32), tab_scales.rearrange("a q t -> (a q) t").bitcast(I32))
         nc.sync.dma_start(idx2[:], offs2)
-        load_row_set(SCATTER_ORDER[0])
+        first_set = SCATTER_ORDER[0]
+        lead = tile("lead", [P, LEAD], F32)
+        nc.sync.dma_start(page[first_set][:], base_rows[:, first_set, :])
+        nc.sync.dma_start(lead[:], xs_rows[:, first_set, 0:LEAD])
+        nc.sync.dma_start(scan[first_set][:, LEAD:S], xs_rows[:, first_set, LEAD:S])
         nc.sync.dma_start(w2_s[0:32, :].bitcast(I32), w2_scales.rearrange("a q c -> (a q) c").bitcast(I32))
         load_row_set(SCATTER_ORDER[1])
         load_w2(0)
@@ -168,7 +173,9 @@ def tile_list_free_space_fusion_kernel(
                 pairs.bitcast(F32)[:, :, first : first + width].rearrange("p u c -> p c u"),
             )
 
-        for t in SCATTER_ORDER:
+        nc.vector.tensor_copy(page[first_set][:].indirect(idx2[:, 0 : LEAD // LIST_ROWS]), lead[:])
+        nc.vector.tensor_copy(page[first_set][:].indirect(idx2[:, LEAD // LIST_ROWS :]), scan[first_set][:, LEAD:S])
+        for t in SCATTER_ORDER[1:]:
             nc.vector.tensor_copy(page[t][:].indirect(idx2[:]), scan[t][:])
         round_row_set(SCATTER_ORDER[0], 0, T2)
         round_row_set(SCATTER_ORDER[1], 0, T2)
@@ -200,14 +207,19 @@ def tile_list_free_space_fusion_kernel(
             nc.vector.quantize_mx(out=codes[:].bitcast(FP8X4), scales=scales[:], in_=woven)
             return codes, scales
 
+        page_quarters = [
+            page_woven[0][:, 0 : PACK * BANK // 2],
+            page_woven[0][:, PACK * BANK // 2 : PACK * BANK],
+            page_woven[1][:],
+            page_woven[2][:],
+        ]
+
         def quantize_page(h, codes, tag=None):
             scales = tile(f"page_scales{h}", [P, BANK], U8, tag=tag)
-            for first in (0, BANK // 2):
-                cols = slice(first, first + BANK // 2)
+            for side in range(2):
+                cols = slice(side * BANK // 2, (side + 1) * BANK // 2)
                 nc.vector.quantize_mx(
-                    out=codes[:, cols].bitcast(FP8X4),
-                    scales=scales[:, cols],
-                    in_=page_woven[0][:, PACK * first : PACK * (first + BANK // 2)] if h == 0 else page_woven[1 + first // HALF][:],
+                    out=codes[:, cols].bitcast(FP8X4), scales=scales[:, cols], in_=page_quarters[2 * h + side]
                 )
             return codes, scales
 
@@ -225,10 +237,12 @@ def tile_list_free_space_fusion_kernel(
         w2_dealt.append(deal_w2(1, ("page_woven2", "page_woven1")))
 
         gap = tile("gap", [P, PICKS], F32)
-        a_rows = [tile(f"a_rows{k}", [P, T2], F32, tag={3: "w2_dealt00", 4: "w2_dealt01", 5: "gap"}.get(k)) for k in range(PASSES * PACK)]
-        shared = tile("shared", [P, 2 * PACK - 1, PICKS], F32)
-        picked = shared[:, 0:PACK, :]
-        b1_lo = shared[:, PACK - 1 : 2 * PACK - 1, HALF:PICKS]
+        held_by = {3: "w2_dealt00", 4: "w2_dealt01", 5: "gap"}
+        a_rows = [tile(f"a_rows{k}", [P, T2], F32, tag=held_by.get(k)) for k in range(PASSES * PACK)]
+        lo_first = (PACK - 1) * PICKS + PIECES[2][0]
+        shared = tile("shared", [P, lo_first + PACK * HALF], F32)
+        picked = shared[:, 0 : PACK * PICKS].rearrange("p (t c) -> p t c", t=PACK)
+        b1_lo = shared[:, lo_first:].rearrange("p (t c) -> p t c", t=PACK)
         b1_hi = tile("b1_hi", [P, PACK, HALF], F32)
 
         def less_clear(k, dst, src):
@@ -250,6 +264,11 @@ def tile_list_free_space_fusion_kernel(
         quarter_banks = [banks[number] for number in (6, 0, 1, 5)]
         half_banks = {1: (0, 6), 2: (5, 4), 3: (1, 7), 4: (2, 1), 5: (7, 2), 6: (1, 7), 7: (2, 1)}
         b_banks = [banks[number] for number in (2, 3, 0, 6)]
+        b1_banks = [[banks[number] for number in pair] for pair in ((7, 2), (1, 7))]
+
+        def make_tile(k):
+            for h in range(2):
+                make_a(k, h, banks[half_banks[k][h]])
 
         def pick(k, first, width):
             offsets = idx3[:, first // LIST_ROWS : (first + width) // LIST_ROWS]
@@ -275,14 +294,14 @@ def tile_list_free_space_fusion_kernel(
         z0_rows = tile("z0_rows", [P, PACK, PICKS], BF16)
         b0 = tile("b0", [P, PICKS], F32)
         rise = tile("rise", [P, PICKS], F32)
-        for k in range(1, PACK):
-            for h in range(2):
-                make_a(k, h, banks[half_banks[k][h]])
+        for k in (1, 2):
+            make_tile(k)
             pick(k, 0, PICKS)
-            if k == 2:
-                make_b(0, b_banks[0][:])
-                less_clear(0, b0[:], b_banks[0][:])
-                nc.gpsimd.tensor_tensor(gap[:], picked[:, 0, :], b0[:], SUBTRACT)
+        make_b(0, b_banks[0][:])
+        less_clear(0, b0[:], b_banks[0][:])
+        nc.gpsimd.tensor_tensor(gap[:], picked[:, 0, :], b0[:], SUBTRACT)
+        make_tile(3)
+        pick(3, 0, PICKS)
         for k in range(1, PACK):
             make_b(k, b_banks[k][:])
             nc.vector.scalar_tensor_tensor(
@@ -292,30 +311,28 @@ def tile_list_free_space_fusion_kernel(
         nc.scalar.activation(rise[:], gap[:], RELU)
         make_a(PACK, 1, banks[half_banks[PACK][1]])
         nc.gpsimd.tensor_tensor(z0_rows[:, 0, :], rise[:], b0[:], ADD)
-        z0_woven = [tile(f"z0_woven{h}", [P, PACK * HALF], BF16) for h in range(2)]
-        for h in range(2):
-            nc.gpsimd.tensor_scalar(
-                z0_woven[h][:].rearrange("p (c t) -> p c t", t=PACK),
-                z0_rows[:, :, h * HALF : (h + 1) * HALF].rearrange("p t c -> p c t"),
-                1.0,
-                0.0,
-                MULT,
-                ADD,
-            )
+        z0_woven = tile("z0_woven", [P, PACK * PICKS], BF16)
+        nc.gpsimd.tensor_scalar(
+            z0_woven[:].rearrange("p (c t) -> p c t", t=PACK),
+            z0_rows[:].rearrange("p t c -> p c t"),
+            1.0,
+            0.0,
+            MULT,
+            ADD,
+        )
 
         last = PASSES * PACK - 1
-        for k in range(PACK, PASSES * PACK):
-            for h in range(2 if k > PACK else 0):
-                make_a(k, h, banks[half_banks[k][h]])
-            pick(k, 0, PICKS if k < last else HALF)
-        z0_q = [quantize("z0_half0", z0_woven[0][:], tag="page_woven2")]
-        for h, (rows, numbers) in enumerate(((b1_lo, (7, 2)), (b1_hi, (1, 7)))):
-            for pair, number in enumerate(numbers):
-                tiles = (2 * pair, 2 * pair + 1)
-                for t in tiles:
-                    make_b(PACK + t, banks[number][:, t % 2 * HALF : (t % 2 + 1) * HALF], slice(h * HALF, (h + 1) * HALF))
-                for t in tiles:
-                    less_clear(PACK + t, rows[:, t, :], banks[number][:, t % 2 * HALF : (t % 2 + 1) * HALF])
+        pick(PACK, 0, PICKS)
+        for k in range(PACK + 1, PASSES * PACK):
+            make_tile(k)
+            pick(k, 0, PICKS if k < last else PIECES[2][0])
+        z0_q = [quantize("z0_half0", z0_woven[:, 0 : PACK * HALF], tag="page_woven2")]
+        for h, rows in enumerate((b1_lo, b1_hi)):
+            for u, bank in enumerate(b1_banks[h]):
+                for e in range(2):
+                    make_b(PACK + 2 * u + e, bank[:, e * HALF : (e + 1) * HALF], slice(h * HALF, (h + 1) * HALF))
+                for e in range(2):
+                    less_clear(PACK + 2 * u + e, rows[:, 2 * u + e, :], bank[:, e * HALF : (e + 1) * HALF])
 
         z1_woven = [tile(f"z1_woven{i}", [P, PACK * width], BF16) for i, (first, width) in enumerate(PIECES)]
 
@@ -329,8 +346,7 @@ def tile_list_free_space_fusion_kernel(
             )
 
         make_z1(0, b1_lo)
-        z0_q.append(quantize("z0_half1", z0_woven[1][:], tag="page_woven1"))
-        pick(last, *PIECES[1])
+        z0_q.append(quantize("z0_half1", z0_woven[:, PACK * HALF : PACK * PICKS], tag="page_woven1"))
         z1_q = [quantize("z1_piece0", z1_woven[0][:])]
         make_z1(1, b1_hi[:, :, 0 : HALF // 2])
         pick(last, *PIECES[2])
@@ -339,20 +355,16 @@ def tile_list_free_space_fusion_kernel(
         z1_q.append(quantize("z1_piece2", z1_woven[2][:]))
 
         out_rows = out.rearrange("(n p) j -> p n j", p=P)
-        piece_banks = [[banks[5], banks[4]], [banks[0], banks[6]], [banks[3], banks[2]]]
-
-        def per_bank(i):
-            return OUT_TILES // len(piece_banks[i])
+        piece_banks = [[banks[number] for number in pair] for pair in ((5, 4), (0, 6), (3, 2))]
+        per_bank = OUT_TILES // 2
 
         def piece_sums(i):
             width = PIECES[i][1]
-            return [
-                bank[:, 0 : per_bank(i) * width].rearrange("p (n j) -> p n j", n=per_bank(i)) for bank in piece_banks[i]
-            ]
+            return [bank[:, 0 : per_bank * width].rearrange("p (n j) -> p n j", n=per_bank) for bank in piece_banks[i]]
 
         def out_passes(i, g, codes, scales):
             for n in range(OUT_TILES):
-                side, place = divmod(n, per_bank(i))
+                side, place = divmod(n, per_bank)
                 nc.tensor.matmul_mx(
                     out=piece_sums(i)[side][:, place, :],
                     lhsT=w3_w[:, g, n * P : (n + 1) * P].bitcast(FP8X4),
@@ -360,7 +372,7 @@ def tile_list_free_space_fusion_kernel(
                     rhs=codes.bitcast(FP8X4),
                     rhs_scale=scales,
                     start=(g == 0 and place == 0),
-                    stop=(g == PASSES - 1 and place == per_bank(i) - 1),
+                    stop=(g == PASSES - 1 and place == per_bank - 1),
                 )
 
         def open_piece(i):
@@ -369,22 +381,22 @@ def tile_list_free_space_fusion_kernel(
             cols = slice(first % HALF, first % HALF + width)
             out_passes(i, 0, codes[:, cols], scales[:, cols])
 
-        def close_piece(i, copies, stores):
+        def close_piece(i, second_copy, store_by_bank=False):
             first, width = PIECES[i]
             res = tile(f"res{i}", [P, OUT_TILES, width], F32)
             codes, scales = z1_q[i]
             out_passes(i, 1, codes[:], scales[:])
-            per_store = OUT_TILES // stores
-            for side, (copy, sums) in enumerate(zip(copies, piece_sums(i))):
-                done = (side + 1) * per_bank(i)
-                copy(res[:, done - per_bank(i) : done, :], sums)
-                if done % per_store == 0:
-                    rows = slice(done - per_store, done)
-                    nc.sync.dma_start(out_rows[:, rows, first : first + width], res[:, rows, :])
+            sums = piece_sums(i)
+            nc.scalar.copy(res[:, 0:per_bank, :], sums[0])
+            if store_by_bank:
+                nc.sync.dma_start(out_rows[:, 0:per_bank, first : first + width], res[:, 0:per_bank, :])
+            second_copy(res[:, per_bank:OUT_TILES, :], sums[1])
+            rest = slice(per_bank if store_by_bank else 0, OUT_TILES)
+            nc.sync.dma_start(out_rows[:, rest, first : first + width], res[:, rest, :])
 
         open_piece(0)
-        close_piece(0, [nc.scalar.copy] * 2, 2)
+        close_piece(0, nc.scalar.copy, store_by_bank=True)
         for i in (1, 2):
             open_piece(i)
-        close_piece(1, [nc.scalar.copy] * 2, 1)
-        close_piece(2, [nc.scalar.copy, nc.vector.tensor_copy], 1)
+        close_piece(1, nc.scalar.copy)
+        close_piece(2, nc.vector.tensor_copy)

@@ -76,7 +76,7 @@ def tile_list_free_space_fusion_kernel(
         w1_hi = [tile(f"w1_hi{q}", [P, PACK, W1_PARTS[q]], F32) for q in range(2)]
         clear_rows = tile("clear_rows", [P, PASSES, PACK], F32)
         tab_w = [tile(f"tab_w{a}", [P, T], I32) for a in range(PASSES)]
-        w2_w = [tile(f"w2_w{g}", [P, PASSES, 2 * K_PASS], U8) for g in range(PASSES)]
+        w2_w = tile("w2_w", [P, PASSES, 2 * H], U8)
         w3_w = tile("w3_w", [P, PASSES, N], I32)
 
         def load_row_set(t):
@@ -86,10 +86,6 @@ def tile_list_free_space_fusion_kernel(
         def load_w1_hi(q):
             first = K_PASS + q * W1_PARTS[0]
             nc.sync.dma_start(w1_hi[q][:], w1_rows[:, :, first : first + W1_PARTS[q]])
-
-        def load_w2(g):
-            words = w2_words.rearrange("a p c -> p a c")[:, :, 2 * g * K_PASS : 2 * (g + 1) * K_PASS]
-            nc.sync.dma_start(w2_w[g][:].bitcast(I32), words.bitcast(I32))
 
         nc.sync.dma_start(idx[:], offs)
         nc.sync.dma_start(tab_s[0:32, :].bitcast(I32), tab_scales.rearrange("a q t -> (a q) t").bitcast(I32))
@@ -101,7 +97,6 @@ def tile_list_free_space_fusion_kernel(
         nc.sync.dma_start(scan[first_set][:, LEAD:S], xs_rows[:, first_set, LEAD:S])
         nc.sync.dma_start(w2_s[0:32, :].bitcast(I32), w2_scales.rearrange("a q c -> (a q) c").bitcast(I32))
         load_row_set(SCATTER_ORDER[1])
-        load_w2(0)
         nc.sync.dma_start(w1_lo, w1_rows[:, :, 0:K_PASS])
         nc.sync.dma_start(idx3[:], offs3)
         load_row_set(SCATTER_ORDER[2])
@@ -111,7 +106,7 @@ def tile_list_free_space_fusion_kernel(
         nc.sync.dma_start(clear_rows[:], clear.rearrange("(g p t) -> p g t", p=P, t=PACK))
         for a in range(PASSES):
             nc.sync.dma_start(tab_w[a][:], tab_words[a].rearrange("p c i -> p (c i)").bitcast(I32))
-        load_w2(1)
+        nc.sync.dma_start(w2_w[:].bitcast(I32), w2_words.rearrange("a p c -> p a c").bitcast(I32))
 
         def spread_scales(scales, rows):
             for a in range(PASSES):
@@ -132,18 +127,14 @@ def tile_list_free_space_fusion_kernel(
         spread_scales(v_s, v_rows)
         spread_scales(w2_dealt_s, w2_dealt_rows)
 
-        def deal_w2(g, tags=(None, None)):
+        def deal_w2(g, tags):
             dealt = [tile(f"w2_dealt{g}{u}", [P, PASSES, K_PASS], U8, tag=tags[u])[:] for u in range(2)]
-            for a in range(PASSES):
-                group = w2_w[g][:, a, :]
-                for u in range(2):
-                    nc.gpsimd.tensor_copy(
-                        dealt[u][:, a, :].bitcast(U16).rearrange("p (t m) -> p t m", t=2),
-                        group.bitcast(U16).rearrange("p (m t) -> p t m", t=PACK)[:, 2 * u : 2 * u + 2],
-                    )
+            group = w2_w[:].bitcast(U16)[:, :, g * K_PASS : (g + 1) * K_PASS].rearrange("p a (m t) -> p a t m", t=PACK)
+            for u in range(2):
+                nc.gpsimd.tensor_copy(
+                    dealt[u].bitcast(U16).rearrange("p a (t m) -> p a t m", t=2), group[:, :, 2 * u : 2 * u + 2]
+                )
             return dealt
-
-        w2_dealt = [deal_w2(0)]
 
         w1_woven = tile("w1_woven", [P, PASSES, PACK * K_PASS], BF16)
         scalar_m = W1_PARTS[0] // PACK
@@ -234,10 +225,10 @@ def tile_list_free_space_fusion_kernel(
         page_q = [quantize_page(0, page_codes[:, 0:BANK]), quantize_page(1, page_codes[:, BANK:T2], tag="staging")]
         v_w.append(gather_words(1, "page_woven0"))
 
-        w2_dealt.append(deal_w2(1, ("page_woven2", "page_woven1")))
+        w2_dealt = [deal_w2(0, ("page_woven2", "page_woven1"))]
 
         gap = tile("gap", [P, PICKS], F32)
-        held_by = {3: "w2_dealt00", 4: "w2_dealt01", 5: "gap"}
+        held_by = {3: "page_woven2", 4: "page_woven1", 5: "gap"}
         a_rows = [tile(f"a_rows{k}", [P, T2], F32, tag=held_by.get(k)) for k in range(PASSES * PACK)]
         lo_first = (PACK - 1) * PICKS + PIECES[2][0]
         shared = tile("shared", [P, lo_first + PACK * HALF], F32)
@@ -291,6 +282,7 @@ def tile_list_free_space_fusion_kernel(
             h, side = divmod(quarter, 2)
             make_a(0, h, bank, side * BANK // 2, BANK // 2)
         pick(0, 0, PICKS)
+        w2_dealt.append(deal_w2(1, ("tab_w1", "a_rows0")))
         z0_rows = tile("z0_rows", [P, PACK, PICKS], BF16)
         b0 = tile("b0", [P, PICKS], F32)
         rise = tile("rise", [P, PICKS], F32)
@@ -326,7 +318,7 @@ def tile_list_free_space_fusion_kernel(
         for k in range(PACK + 1, PASSES * PACK):
             make_tile(k)
             pick(k, 0, PICKS if k < last else PIECES[2][0])
-        z0_q = [quantize("z0_half0", z0_woven[:, 0 : PACK * HALF], tag="page_woven2")]
+        z0_q = [quantize("z0_half0", z0_woven[:, 0 : PACK * HALF], tag="tab_w1")]
         for h, rows in enumerate((b1_lo, b1_hi)):
             for u, bank in enumerate(b1_banks[h]):
                 for e in range(2):
@@ -346,7 +338,7 @@ def tile_list_free_space_fusion_kernel(
             )
 
         make_z1(0, b1_lo)
-        z0_q.append(quantize("z0_half1", z0_woven[:, PACK * HALF : PACK * PICKS], tag="page_woven1"))
+        z0_q.append(quantize("z0_half1", z0_woven[:, PACK * HALF : PACK * PICKS], tag="a_rows0"))
         z1_q = [quantize("z1_piece0", z1_woven[0][:])]
         make_z1(1, b1_hi[:, :, 0 : HALF // 2])
         pick(last, *PIECES[2])

@@ -29,7 +29,7 @@ BANK = 512
 BANKS = 8
 LIST_ROWS = 16
 HALF = PICKS // 2
-W1_PARTS = (320, 192)
+W1_PARTS = (256, 256)
 SCATTER_ORDER = (0, 2, 1, 3)
 PAGE_PARTS = [(0, BANK), (BANK, BANK // 2), (BANK + BANK // 2, BANK // 2)]
 LEAD = S // 4
@@ -98,7 +98,6 @@ def tile_list_free_space_fusion_kernel(
         nc.sync.dma_start(w2_s[0:32, :].bitcast(I32), w2_scales.rearrange("a q c -> (a q) c").bitcast(I32))
         load_row_set(SCATTER_ORDER[1])
         nc.sync.dma_start(w1_lo, w1_rows[:, :, 0:K_PASS])
-        nc.sync.dma_start(idx3[:], offs3)
         load_row_set(SCATTER_ORDER[2])
         load_w1_hi(0)
         load_row_set(SCATTER_ORDER[3])
@@ -106,6 +105,7 @@ def tile_list_free_space_fusion_kernel(
         nc.sync.dma_start(clear_rows[:], clear.rearrange("(g p t) -> p g t", p=P, t=PACK))
         for a in range(PASSES):
             nc.sync.dma_start(tab_w[a][:], tab_words[a].rearrange("p c i -> p (c i)").bitcast(I32))
+        nc.sync.dma_start(idx3[:], offs3)
         nc.sync.dma_start(w2_w[:].bitcast(I32), w2_words.rearrange("a p c -> p a c").bitcast(I32))
 
         def spread_scales(scales, rows):

@@ -59,11 +59,6 @@ def tile_list_free_space_fusion_kernel(
         for rows in (tab_s, w2_s):
             nc.vector.memset(rows[32:64, :].bitcast(I32), 0)
             nc.vector.memset(rows[64:P, :].bitcast(I32), 0)
-        v_s = tile("v_s", [P, PASSES, PICKS], U8)
-        w2_dealt_s = tile("w2_dealt_s", [P, PASSES, H], U8)
-        w3_s = tile("w3_s", [P, N], U8)
-        for scales in (v_s, w2_dealt_s, w3_s):
-            nc.gpsimd.memset(scales[:].bitcast(I32), 0)
 
         base_rows = base.rearrange("(p t) c -> p t c", t=PACK)
         xs_rows = xs.rearrange("(p t) c -> p t c", t=PACK)
@@ -119,6 +114,11 @@ def tile_list_free_space_fusion_kernel(
 
         v_rows = tile("v_rows", [P, PICKS], U8)
         nc.vector.tensor_copy(v_rows[:], tab_s[:].indirect(idx[:]))
+        planes = tile("planes", [P, PASSES * PICKS + PASSES * H + N], U8, tag="tab_s")
+        nc.gpsimd.memset(planes[:].bitcast(I32), 0)
+        v_s = planes[:, 0 : PASSES * PICKS].rearrange("p (a c) -> p a c", a=PASSES)
+        w2_dealt_s = planes[:, PASSES * PICKS : PASSES * (PICKS + H)].rearrange("p (a c) -> p a c", a=PASSES)
+        w3_s = planes[:, PASSES * (PICKS + H) :]
         w2_dealt_rows = tile("w2_dealt_rows", [P, H], U8)
         nc.gpsimd.tensor_copy(
             w2_dealt_rows[:].rearrange("p (g t m) -> p g t m", g=PASSES, t=PACK),
@@ -373,22 +373,22 @@ def tile_list_free_space_fusion_kernel(
             cols = slice(first % HALF, first % HALF + width)
             out_passes(i, 0, codes[:, cols], scales[:, cols])
 
-        def close_piece(i, second_copy, store_by_bank=False):
+        def close_piece(i, second_copy, first_store=None):
             first, width = PIECES[i]
             res = tile(f"res{i}", [P, OUT_TILES, width], F32)
             codes, scales = z1_q[i]
             out_passes(i, 1, codes[:], scales[:])
             sums = piece_sums(i)
             nc.scalar.copy(res[:, 0:per_bank, :], sums[0])
-            if store_by_bank:
-                nc.sync.dma_start(out_rows[:, 0:per_bank, first : first + width], res[:, 0:per_bank, :])
+            if first_store:
+                first_store(out_rows[:, 0:per_bank, first : first + width], res[:, 0:per_bank, :])
             second_copy(res[:, per_bank:OUT_TILES, :], sums[1])
-            rest = slice(per_bank if store_by_bank else 0, OUT_TILES)
+            rest = slice(per_bank if first_store else 0, OUT_TILES)
             nc.sync.dma_start(out_rows[:, rest, first : first + width], res[:, rest, :])
 
         open_piece(0)
-        close_piece(0, nc.scalar.copy, store_by_bank=True)
+        close_piece(0, nc.scalar.copy, nc.sync.dma_start)
         for i in (1, 2):
             open_piece(i)
         close_piece(1, nc.scalar.copy)
-        close_piece(2, nc.vector.tensor_copy)
+        close_piece(2, nc.vector.tensor_copy, nc.scalar.dma_start)

@@ -83,12 +83,12 @@ def tile_list_free_space_fusion_kernel(
             nc.sync.dma_start(w1_hi[q][:], w1_rows[:, :, first : first + W1_PARTS[q]])
 
         nc.sync.dma_start(idx[:], offs)
-        nc.sync.dma_start(tab_s[0:32, :].bitcast(I32), tab_scales.rearrange("a q t -> (a q) t").bitcast(I32))
+        nc.scalar.dma_start(tab_s[0:32, :].bitcast(I32), tab_scales.rearrange("a q t -> (a q) t").bitcast(I32))
         nc.sync.dma_start(idx2[:], offs2)
         first_set = SCATTER_ORDER[0]
         lead = tile("lead", [P, LEAD], F32)
         nc.sync.dma_start(page[first_set][:], base_rows[:, first_set, :])
-        nc.sync.dma_start(lead[:], xs_rows[:, first_set, 0:LEAD])
+        nc.scalar.dma_start(lead[:], xs_rows[:, first_set, 0:LEAD])
         nc.sync.dma_start(scan[first_set][:, LEAD:S], xs_rows[:, first_set, LEAD:S])
         nc.sync.dma_start(w2_s[0:32, :].bitcast(I32), w2_scales.rearrange("a q c -> (a q) c").bitcast(I32))
         load_row_set(SCATTER_ORDER[1])

@@ -84,10 +84,10 @@ def tile_list_free_space_fusion_kernel(
 
         nc.sync.dma_start(idx[:], offs)
         nc.scalar.dma_start(tab_s[0:32, :].bitcast(I32), tab_scales.rearrange("a q t -> (a q) t").bitcast(I32))
-        nc.sync.dma_start(idx2[:], offs2)
         first_set = SCATTER_ORDER[0]
         lead = tile("lead", [P, LEAD], F32)
         nc.sync.dma_start(page[first_set][:], base_rows[:, first_set, :])
+        nc.sync.dma_start(idx2[:], offs2)
         nc.scalar.dma_start(lead[:], xs_rows[:, first_set, 0:LEAD])
         nc.sync.dma_start(scan[first_set][:, LEAD:S], xs_rows[:, first_set, LEAD:S])
         nc.sync.dma_start(w2_s[0:32, :].bitcast(I32), w2_scales.rearrange("a q c -> (a q) c").bitcast(I32))
@@ -222,7 +222,7 @@ def tile_list_free_space_fusion_kernel(
         w1_codes, w1_scales = quantize("w1", w1_woven[:].rearrange("p g c -> p (g c)"), tag=f"page{SCATTER_ORDER[2]}")
         v_w = [gather_words(0, "w1_hi1")]
         page_codes = tile("page_codes", [P, T2], U32, tag="tab_w0")
-        page_q = [quantize_page(0, page_codes[:, 0:BANK]), quantize_page(1, page_codes[:, BANK:T2], tag="staging")]
+        page_q = [quantize_page(0, page_codes[:, 0:BANK]), quantize_page(1, page_codes[:, BANK:T2])]
         v_w.append(gather_words(1, "page_woven0"))
 
         w2_dealt = [deal_w2(0, ("page_woven2", "page_woven1"))]
@@ -373,22 +373,20 @@ def tile_list_free_space_fusion_kernel(
             cols = slice(first % HALF, first % HALF + width)
             out_passes(i, 0, codes[:, cols], scales[:, cols])
 
-        def close_piece(i, second_copy, first_store=None):
+        def close_piece(i, copies, stores):
             first, width = PIECES[i]
             res = tile(f"res{i}", [P, OUT_TILES, width], F32)
             codes, scales = z1_q[i]
             out_passes(i, 1, codes[:], scales[:])
             sums = piece_sums(i)
-            nc.scalar.copy(res[:, 0:per_bank, :], sums[0])
-            if first_store:
-                first_store(out_rows[:, 0:per_bank, first : first + width], res[:, 0:per_bank, :])
-            second_copy(res[:, per_bank:OUT_TILES, :], sums[1])
-            rest = slice(per_bank if first_store else 0, OUT_TILES)
-            nc.sync.dma_start(out_rows[:, rest, first : first + width], res[:, rest, :])
+            for side, copy in enumerate(copies):
+                rows = slice(side * per_bank, (side + 1) * per_bank)
+                copy(res[:, rows, :], sums[side])
+                stores[side](out_rows[:, rows, first : first + width], res[:, rows, :])
 
         open_piece(0)
-        close_piece(0, nc.scalar.copy, nc.sync.dma_start)
+        close_piece(0, [nc.scalar.copy] * 2, [nc.sync.dma_start] * 2)
         for i in (1, 2):
             open_piece(i)
-        close_piece(1, nc.scalar.copy)
-        close_piece(2, nc.vector.tensor_copy, nc.scalar.dma_start)
+        close_piece(1, [nc.scalar.copy] * 2, [nc.sync.dma_start] * 2)
+        close_piece(2, [nc.vector.tensor_copy, nc.scalar.copy], [nc.sync.dma_start, nc.scalar.dma_start])

@@ -25,6 +25,7 @@ PACK = 4
 K_PASS = P * PACK
 PASSES = 2
 QUADRANTS = 4
+COMPACT = P - 32
 BANK = 512
 BANKS = 8
 LIST_ROWS = 16
@@ -57,8 +58,7 @@ def tile_list_free_space_fusion_kernel(
         tab_s = tile("tab_s", [P, T], U8)
         w2_s = tile("w2_s", [P, H], U8)
         for rows in (tab_s, w2_s):
-            nc.vector.memset(rows[32:64, :].bitcast(I32), 0)
-            nc.vector.memset(rows[64:P, :].bitcast(I32), 0)
+            nc.vector.memset(rows[0:COMPACT, :].bitcast(I32), 0)
 
         base_rows = base.rearrange("(p t) c -> p t c", t=PACK)
         xs_rows = xs.rearrange("(p t) c -> p t c", t=PACK)
@@ -83,14 +83,14 @@ def tile_list_free_space_fusion_kernel(
             nc.sync.dma_start(w1_hi[q][:], w1_rows[:, :, first : first + W1_PARTS[q]])
 
         nc.sync.dma_start(idx[:], offs)
-        nc.scalar.dma_start(tab_s[0:32, :].bitcast(I32), tab_scales.rearrange("a q t -> (a q) t").bitcast(I32))
+        nc.scalar.dma_start(tab_s[COMPACT:P, :].bitcast(I32), tab_scales.rearrange("a q t -> (a q) t").bitcast(I32))
         first_set = SCATTER_ORDER[0]
         lead = tile("lead", [P, LEAD], F32)
         nc.sync.dma_start(page[first_set][:], base_rows[:, first_set, :])
         nc.sync.dma_start(idx2[:], offs2)
         nc.scalar.dma_start(lead[:], xs_rows[:, first_set, 0:LEAD])
         nc.sync.dma_start(scan[first_set][:, LEAD:S], xs_rows[:, first_set, LEAD:S])
-        nc.sync.dma_start(w2_s[0:32, :].bitcast(I32), w2_scales.rearrange("a q c -> (a q) c").bitcast(I32))
+        nc.sync.dma_start(w2_s[COMPACT:P, :].bitcast(I32), w2_scales.rearrange("a q c -> (a q) c").bitcast(I32))
         load_row_set(SCATTER_ORDER[1])
         nc.sync.dma_start(w1_lo, w1_rows[:, :, 0:K_PASS])
         load_row_set(SCATTER_ORDER[2])
@@ -106,7 +106,7 @@ def tile_list_free_space_fusion_kernel(
         def spread_scales(scales, rows):
             for a in range(PASSES):
                 for quadrant in range(QUADRANTS):
-                    first = 16 * a + PACK * quadrant
+                    first = COMPACT + 16 * a + PACK * quadrant
                     nc.sync.dma_start(
                         scales[32 * quadrant : 32 * quadrant + PACK, a, :].bitcast(I32),
                         rows[first : first + PACK, :].bitcast(I32),
@@ -380,9 +380,10 @@ def tile_list_free_space_fusion_kernel(
             out_passes(i, 1, codes[:], scales[:])
             sums = piece_sums(i)
             for side, copy in enumerate(copies):
-                rows = slice(side * per_bank, (side + 1) * per_bank)
-                copy(res[:, rows, :], sums[side])
-                stores[side](out_rows[:, rows, first : first + width], res[:, rows, :])
+                for places in ([slice(0, 1), slice(1, 2)] if i == 0 and side == 0 else [slice(0, per_bank)]):
+                    rows = slice(side * per_bank + places.start, side * per_bank + places.stop)
+                    copy(res[:, rows, :], sums[side][:, places, :])
+                    stores[side](out_rows[:, rows, first : first + width], res[:, rows, :])
 
         open_piece(0)
         close_piece(0, [nc.scalar.copy] * 2, [nc.sync.dma_start] * 2)

@@ -220,6 +220,16 @@ def tile_list_free_space_fusion_kernel(
             return words
 
         w1_codes, w1_scales = quantize("w1", w1_woven[:].rearrange("p g c -> p (g c)"), tag=f"page{SCATTER_ORDER[2]}")
+        for turn in range(3):
+            nc.tensor.matmul_mx(
+                out=banks[7][:],
+                lhsT=w1_codes[:, 0:P].bitcast(FP8X4),
+                lhsT_scale=w1_scales[:, 0:P],
+                rhs=w1_codes[:, 0:BANK].bitcast(FP8X4),
+                rhs_scale=w1_scales[:, 0:BANK],
+                start=True,
+                stop=True,
+            )
         v_w = [gather_words(0, "w1_hi1")]
         page_codes = tile("page_codes", [P, T2], U32, tag="tab_w0")
         page_q = [quantize_page(0, page_codes[:, 0:BANK]), quantize_page(1, page_codes[:, BANK:T2])]

@@ -219,8 +219,14 @@ def tile_list_free_space_fusion_kernel(
             nc.vector.tensor_copy(words[:], tab_w[a][:].bitcast(U32).indirect(idx[:]))
             return words
 
-        w1_codes, w1_scales = quantize("w1", w1_woven[:].rearrange("p g c -> p (g c)"), tag=f"page{SCATTER_ORDER[2]}")
-        for turn in range(3):
+        w1_codes = tile("w1_codes", [P, H], U32, tag=f"page{SCATTER_ORDER[2]}")
+        w1_scales = tile("w1_scales", [P, H], U8)
+        for g in range(PASSES):
+            cols = slice(g * K_PASS, (g + 1) * K_PASS)
+            nc.vector.quantize_mx(
+                out=w1_codes[:, cols].bitcast(FP8X4), scales=w1_scales[:, cols], in_=w1_woven[:, g, :]
+            )
+        for turn in range(4):
             nc.tensor.matmul_mx(
                 out=banks[7][:],
                 lhsT=w1_codes[:, 0:P].bitcast(FP8X4),

@@ -71,7 +71,7 @@ def tile_list_free_space_fusion_kernel(
         w1_hi = [tile(f"w1_hi{q}", [P, PACK, W1_PARTS[q]], F32) for q in range(2)]
         clear_rows = tile("clear_rows", [P, PASSES, PACK], F32)
         tab_w = [tile(f"tab_w{a}", [P, T], I32) for a in range(PASSES)]
-        w2_w = tile("w2_w", [P, PASSES, 2 * H], U8)
+        w2_w = [tile(f"w2_w{g}", [P, PASSES, 2 * K_PASS], U8) for g in range(PASSES)]
         w3_w = tile("w3_w", [P, PASSES, N], I32)
 
         def load_row_set(t):
@@ -81,6 +81,10 @@ def tile_list_free_space_fusion_kernel(
         def load_w1_hi(q):
             first = K_PASS + q * W1_PARTS[0]
             nc.sync.dma_start(w1_hi[q][:], w1_rows[:, :, first : first + W1_PARTS[q]])
+
+        def load_w2(g):
+            words = w2_words.rearrange("a p c -> p a c")[:, :, 2 * g * K_PASS : 2 * (g + 1) * K_PASS]
+            nc.sync.dma_start(w2_w[g][:].bitcast(I32), words.bitcast(I32))
 
         nc.sync.dma_start(idx[:], offs)
         nc.scalar.dma_start(tab_s[COMPACT:P, :].bitcast(I32), tab_scales.rearrange("a q t -> (a q) t").bitcast(I32))
@@ -101,7 +105,7 @@ def tile_list_free_space_fusion_kernel(
         for a in range(PASSES):
             nc.sync.dma_start(tab_w[a][:], tab_words[a].rearrange("p c i -> p (c i)").bitcast(I32))
         nc.sync.dma_start(idx3[:], offs3)
-        nc.sync.dma_start(w2_w[:].bitcast(I32), w2_words.rearrange("a p c -> p a c").bitcast(I32))
+        load_w2(0)
 
         def spread_scales(scales, rows):
             for a in range(PASSES):
@@ -126,10 +130,11 @@ def tile_list_free_space_fusion_kernel(
         )
         spread_scales(v_s, v_rows)
         spread_scales(w2_dealt_s, w2_dealt_rows)
+        load_w2(1)
 
         def deal_w2(g, tags):
             dealt = [tile(f"w2_dealt{g}{u}", [P, PASSES, K_PASS], U8, tag=tags[u])[:] for u in range(2)]
-            group = w2_w[:].bitcast(U16)[:, :, g * K_PASS : (g + 1) * K_PASS].rearrange("p a (m t) -> p a t m", t=PACK)
+            group = w2_w[g][:].bitcast(U16).rearrange("p a (m t) -> p a t m", t=PACK)
             for u in range(2):
                 nc.gpsimd.tensor_copy(
                     dealt[u].bitcast(U16).rearrange("p a (t m) -> p a t m", t=2), group[:, :, 2 * u : 2 * u + 2]

@@ -26,6 +26,7 @@ K_PASS = P * PACK
 PASSES = 2
 QUADRANTS = 4
 COMPACT = P - 32
+IN_FLIGHT = 8
 BANK = 512
 BANKS = 8
 LIST_ROWS = 16
@@ -56,9 +57,10 @@ def tile_list_free_space_fusion_kernel(
         idx3 = tile("idx3", [P, PICKS // LIST_ROWS], U16)
 
         tab_s = tile("tab_s", [P, T], U8)
-        w2_s = tile("w2_s", [P, H], U8)
-        for rows in (tab_s, w2_s):
-            nc.vector.memset(rows[0:COMPACT, :].bitcast(I32), 0)
+        w2_s = tile("w2_s", [P, PASSES * H], U8)
+        nc.vector.memset(tab_s[0:COMPACT, :].bitcast(I32), 0)
+        nc.gpsimd.memset(w2_s[0:COMPACT, :].bitcast(I32), 0)
+        nc.gpsimd.memset(w2_s[COMPACT : COMPACT + 16, :].bitcast(I32), 0)
 
         base_rows = base.rearrange("(p t) c -> p t c", t=PACK)
         xs_rows = xs.rearrange("(p t) c -> p t c", t=PACK)
@@ -71,7 +73,7 @@ def tile_list_free_space_fusion_kernel(
         w1_hi = [tile(f"w1_hi{q}", [P, PACK, W1_PARTS[q]], F32) for q in range(2)]
         clear_rows = tile("clear_rows", [P, PASSES, PACK], F32)
         tab_w = [tile(f"tab_w{a}", [P, T], I32) for a in range(PASSES)]
-        w2_w = [tile(f"w2_w{g}", [P, PASSES, 2 * K_PASS], U8) for g in range(PASSES)]
+        w2_w = tile("w2_w", [P, PASSES, 2 * H], U8)
         w3_w = tile("w3_w", [P, PASSES, N], I32)
 
         def load_row_set(t):
@@ -82,10 +84,6 @@ def tile_list_free_space_fusion_kernel(
             first = K_PASS + q * W1_PARTS[0]
             nc.sync.dma_start(w1_hi[q][:], w1_rows[:, :, first : first + W1_PARTS[q]])
 
-        def load_w2(g):
-            words = w2_words.rearrange("a p c -> p a c")[:, :, 2 * g * K_PASS : 2 * (g + 1) * K_PASS]
-            nc.sync.dma_start(w2_w[g][:].bitcast(I32), words.bitcast(I32))
-
         nc.sync.dma_start(idx[:], offs)
         nc.scalar.dma_start(tab_s[COMPACT:P, :].bitcast(I32), tab_scales.rearrange("a q t -> (a q) t").bitcast(I32))
         first_set = SCATTER_ORDER[0]
@@ -94,7 +92,10 @@ def tile_list_free_space_fusion_kernel(
         nc.sync.dma_start(idx2[:], offs2)
         nc.scalar.dma_start(lead[:], xs_rows[:, first_set, 0:LEAD])
         nc.sync.dma_start(scan[first_set][:, LEAD:S], xs_rows[:, first_set, LEAD:S])
-        nc.sync.dma_start(w2_s[COMPACT:P, :].bitcast(I32), w2_scales.rearrange("a q c -> (a q) c").bitcast(I32))
+        nc.sync.dma_start(
+            w2_s[COMPACT + 16 : P, :].rearrange("q (a c) -> q a c", a=PASSES).bitcast(I32),
+            w2_scales.rearrange("a q c -> q a c").bitcast(I32),
+        )
         load_row_set(SCATTER_ORDER[1])
         nc.sync.dma_start(w1_lo, w1_rows[:, :, 0:K_PASS])
         load_row_set(SCATTER_ORDER[2])
@@ -105,16 +106,6 @@ def tile_list_free_space_fusion_kernel(
         for a in range(PASSES):
             nc.sync.dma_start(tab_w[a][:], tab_words[a].rearrange("p c i -> p (c i)").bitcast(I32))
         nc.sync.dma_start(idx3[:], offs3)
-        load_w2(0)
-
-        def spread_scales(scales, rows):
-            for a in range(PASSES):
-                for quadrant in range(QUADRANTS):
-                    first = COMPACT + 16 * a + PACK * quadrant
-                    nc.sync.dma_start(
-                        scales[32 * quadrant : 32 * quadrant + PACK, a, :].bitcast(I32),
-                        rows[first : first + PACK, :].bitcast(I32),
-                    )
 
         v_rows = tile("v_rows", [P, PICKS], U8)
         nc.vector.tensor_copy(v_rows[:], tab_s[:].indirect(idx[:]))
@@ -123,18 +114,28 @@ def tile_list_free_space_fusion_kernel(
         v_s = planes[:, 0 : PASSES * PICKS].rearrange("p (a c) -> p a c", a=PASSES)
         w2_dealt_s = planes[:, PASSES * PICKS : PASSES * (PICKS + H)].rearrange("p (a c) -> p a c", a=PASSES)
         w3_s = planes[:, PASSES * (PICKS + H) :]
-        w2_dealt_rows = tile("w2_dealt_rows", [P, H], U8)
+        w2_dealt_rows = tile("w2_dealt_rows", [P, PASSES * H], U8)
         nc.gpsimd.tensor_copy(
-            w2_dealt_rows[:].rearrange("p (g t m) -> p g t m", g=PASSES, t=PACK),
-            w2_s[:].rearrange("p (g m t) -> p g t m", g=PASSES, t=PACK),
+            w2_dealt_rows[:].rearrange("p (g t m) -> p g t m", t=PACK, m=P),
+            w2_s[:].rearrange("p (g m t) -> p g t m", t=PACK, m=P),
         )
-        spread_scales(v_s, v_rows)
-        spread_scales(w2_dealt_s, w2_dealt_rows)
-        load_w2(1)
+        spreads = []
+        for a in range(PASSES):
+            for quadrant in range(QUADRANTS):
+                first = COMPACT + 16 * a + PACK * quadrant
+                spreads.append((v_s[32 * quadrant : 32 * quadrant + PACK, a, :], v_rows[first : first + PACK, :]))
+        for quadrant in range(QUADRANTS):
+            first = COMPACT + 16 + PACK * quadrant
+            both = w2_dealt_s[32 * quadrant : 32 * quadrant + PACK].rearrange("p a c -> p (a c)")
+            spreads.append((both, w2_dealt_rows[first : first + PACK, :]))
+        for place, (rows, compact) in enumerate(spreads):
+            if place == len(spreads) - (IN_FLIGHT - 1):
+                nc.sync.dma_start(w2_w[:].bitcast(I32), w2_words.rearrange("a p c -> p a c").bitcast(I32))
+            nc.sync.dma_start(rows.bitcast(I32), compact.bitcast(I32))
 
         def deal_w2(g, tags):
             dealt = [tile(f"w2_dealt{g}{u}", [P, PASSES, K_PASS], U8, tag=tags[u])[:] for u in range(2)]
-            group = w2_w[g][:].bitcast(U16).rearrange("p a (m t) -> p a t m", t=PACK)
+            group = w2_w[:].bitcast(U16)[:, :, g * K_PASS : (g + 1) * K_PASS].rearrange("p a (m t) -> p a t m", t=PACK)
             for u in range(2):
                 nc.gpsimd.tensor_copy(
                     dealt[u].bitcast(U16).rearrange("p a (t m) -> p a t m", t=2), group[:, :, 2 * u : 2 * u + 2]

@@ -14,11 +14,11 @@ U8 = mybir.dt.uint8
 FP8X4 = mybir.dt.float8_e4m3fn_x4
 FP4X4 = mybir.dt.float4_e2m1fn_x4
 IDENTITY = mybir.ActivationFunctionType.Identity
+RELU = mybir.ActivationFunctionType.Relu
 MAX = mybir.AluOpType.max
 ADD = mybir.AluOpType.add
 MULT = mybir.AluOpType.mult
 SUBTRACT = mybir.AluOpType.subtract
-RELU = mybir.ActivationFunctionType.Relu
 
 P = 128
 PACK = 4
@@ -31,11 +31,11 @@ BANK = 512
 BANKS = 8
 LIST_ROWS = 16
 HALF = PICKS // 2
-W1_PARTS = (256, 256)
-SCATTER_ORDER = (0, 2, 1, 3)
-PAGE_PARTS = [(0, BANK), (BANK, BANK // 2), (BANK + BANK // 2, BANK // 2)]
+QUARTER = T2 // 4
+W1_PART = 256
 LEAD = S // 4
 OUT_TILES = N // P
+ASIDE = 0
 PIECES = [(0, HALF), (HALF, HALF // 2), (HALF + HALF // 2, HALF // 2)]
 
 
@@ -67,10 +67,9 @@ def tile_list_free_space_fusion_kernel(
         w1_rows = w1.rearrange("(p j) r -> p j r", j=PACK)
         page = [tile(f"page{t}", [P, T2], F32) for t in range(PACK)]
         scan = [tile(f"scan{t}", [P, S], F32) for t in range(PACK)]
-        staging = tile("staging", [P, 3, 2 * T2], BF16)
-        pairs = staging[:, 0:2, :]
-        w1_lo = staging[:, 1:3, :].rearrange("p u c -> p (u c)").bitcast(F32).rearrange("p (j c) -> p j c", j=PACK)
-        w1_hi = [tile(f"w1_hi{q}", [P, PACK, W1_PARTS[q]], F32) for q in range(2)]
+        lead = tile("lead", [P, LEAD], F32)
+        w1_lo = tile("w1_lo", [P, PACK, K_PASS], F32)
+        w1_hi = [tile(f"w1_hi{q}", [P, PACK, W1_PART], F32) for q in range(2)]
         clear_rows = tile("clear_rows", [P, PASSES, PACK], F32)
         tab_w = [tile(f"tab_w{a}", [P, T], I32) for a in range(PASSES)]
         w2_w = tile("w2_w", [P, PASSES, 2 * H], U8)
@@ -81,39 +80,47 @@ def tile_list_free_space_fusion_kernel(
             nc.sync.dma_start(page[t][:], base_rows[:, t, :])
 
         def load_w1_hi(q):
-            first = K_PASS + q * W1_PARTS[0]
-            nc.sync.dma_start(w1_hi[q][:], w1_rows[:, :, first : first + W1_PARTS[q]])
+            first = K_PASS + q * W1_PART
+            nc.sync.dma_start(w1_hi[q][:], w1_rows[:, :, first : first + W1_PART])
+
+        def load_table(a):
+            nc.sync.dma_start(tab_w[a][:], tab_words[a].rearrange("p c i -> p (c i)").bitcast(I32))
 
         nc.sync.dma_start(idx[:], offs)
         nc.scalar.dma_start(tab_s[COMPACT:P, :].bitcast(I32), tab_scales.rearrange("a q t -> (a q) t").bitcast(I32))
-        first_set = SCATTER_ORDER[0]
-        lead = tile("lead", [P, LEAD], F32)
-        nc.sync.dma_start(page[first_set][:], base_rows[:, first_set, :])
+        nc.sync.dma_start(page[0][:], base_rows[:, 0, :])
         nc.sync.dma_start(idx2[:], offs2)
-        nc.scalar.dma_start(lead[:], xs_rows[:, first_set, 0:LEAD])
-        nc.sync.dma_start(scan[first_set][:, LEAD:S], xs_rows[:, first_set, LEAD:S])
+        nc.scalar.dma_start(lead[:], xs_rows[:, 0, 0:LEAD])
+        nc.sync.dma_start(scan[0][:, LEAD:S], xs_rows[:, 0, LEAD:S])
         nc.sync.dma_start(
             w2_s[COMPACT + 16 : P, :].rearrange("q (a c) -> q a c", a=PASSES).bitcast(I32),
             w2_scales.rearrange("a q c -> q a c").bitcast(I32),
         )
-        load_row_set(SCATTER_ORDER[1])
-        nc.sync.dma_start(w1_lo, w1_rows[:, :, 0:K_PASS])
-        load_row_set(SCATTER_ORDER[2])
+        load_row_set(1)
+        nc.sync.dma_start(w1_lo[:], w1_rows[:, :, 0:K_PASS])
+        load_row_set(2)
         load_w1_hi(0)
-        load_row_set(SCATTER_ORDER[3])
+        load_row_set(3)
         load_w1_hi(1)
         nc.sync.dma_start(clear_rows[:], clear.rearrange("(g p t) -> p g t", p=P, t=PACK))
-        for a in range(PASSES):
-            nc.sync.dma_start(tab_w[a][:], tab_words[a].rearrange("p c i -> p (c i)").bitcast(I32))
-        nc.sync.dma_start(idx3[:], offs3)
+        load_table(0)
 
         v_rows = tile("v_rows", [P, PICKS], U8)
         nc.vector.tensor_copy(v_rows[:], tab_s[:].indirect(idx[:]))
-        planes = tile("planes", [P, PASSES * PICKS + PASSES * H + N], U8, tag="tab_s")
+        planes = tile("planes", [P, PASSES * PICKS + PASSES * H + T2], U8, tag="tab_s")
         nc.gpsimd.memset(planes[:].bitcast(I32), 0)
         v_s = planes[:, 0 : PASSES * PICKS].rearrange("p (a c) -> p a c", a=PASSES)
         w2_dealt_s = planes[:, PASSES * PICKS : PASSES * (PICKS + H)].rearrange("p (a c) -> p a c", a=PASSES)
-        w3_s = planes[:, PASSES * (PICKS + H) :]
+        page_scales = planes[:, PASSES * (PICKS + H) :]
+        w3_s = page_scales.rearrange("p (a c) -> p a c", a=PASSES)
+        for quadrant in range(QUADRANTS):
+            nc.sync.dma_start(
+                w3_s[32 * quadrant + PACK : 32 * quadrant + 2 * PACK].bitcast(I32),
+                w3_scales[:, PACK * quadrant : PACK * (quadrant + 1), :].rearrange("a q c -> q a c").bitcast(I32),
+            )
+        load_table(1)
+        nc.sync.dma_start(idx3[:], offs3)
+
         w2_dealt_rows = tile("w2_dealt_rows", [P, PASSES * H], U8)
         nc.gpsimd.tensor_copy(
             w2_dealt_rows[:].rearrange("p (g t m) -> p g t m", t=PACK, m=P),
@@ -132,92 +139,67 @@ def tile_list_free_space_fusion_kernel(
             if place == len(spreads) - (IN_FLIGHT - 1):
                 nc.sync.dma_start(w2_w[:].bitcast(I32), w2_words.rearrange("a p c -> p a c").bitcast(I32))
             nc.sync.dma_start(rows.bitcast(I32), compact.bitcast(I32))
+        nc.sync.dma_start(w3_w[:], w3_words.rearrange("a p c i -> p a (c i)").bitcast(I32))
 
-        def deal_w2(g, tags):
-            dealt = [tile(f"w2_dealt{g}{u}", [P, PASSES, K_PASS], U8, tag=tags[u])[:] for u in range(2)]
-            group = w2_w[:].bitcast(U16)[:, :, g * K_PASS : (g + 1) * K_PASS].rearrange("p a (m t) -> p a t m", t=PACK)
-            for u in range(2):
-                nc.gpsimd.tensor_copy(
-                    dealt[u].bitcast(U16).rearrange("p a (t m) -> p a t m", t=2), group[:, :, 2 * u : 2 * u + 2]
-                )
-            return dealt
+        woven_lo = tile("woven_lo", [P, PACK * 3 * QUARTER], BF16, tag="w2_s")
+        woven_hi = tile("woven_hi", [P, PACK * QUARTER], BF16, tag="w1_lo")
+
+        def woven(first, width):
+            if first < 3 * QUARTER:
+                return woven_lo[:, PACK * first : PACK * (first + width)]
+            return woven_hi[:, PACK * (first - 3 * QUARTER) : PACK * (first - 3 * QUARTER + width)]
+
+        def lane(t, first, width):
+            return woven(first, width).rearrange("p (c t) -> p c t", t=PACK)[:, :, t]
+
+        def scalar_lane(t, first, width):
+            nc.scalar.copy(lane(t, first, width), page[t][:, first : first + width])
+
+        def gpsimd_lane(t, first, width):
+            nc.gpsimd.tensor_scalar(lane(t, first, width), page[t][:, first : first + width], 1.0, 0.0, MULT, ADD)
 
         w1_woven = tile("w1_woven", [P, PASSES, PACK * K_PASS], BF16)
-        scalar_m = W1_PARTS[0] // PACK
+        part_m = W1_PART // PACK
+
+        nc.vector.tensor_copy(page[0][:].indirect(idx2[:, 0 : LEAD // LIST_ROWS]), lead[:])
+        nc.vector.tensor_copy(page[0][:].indirect(idx2[:, LEAD // LIST_ROWS :]), scan[0][:, LEAD:S])
+        for t in range(1, PACK):
+            nc.vector.tensor_copy(page[t][:].indirect(idx2[:]), scan[t][:])
+
         nc.scalar.copy(
             w1_woven[:, 0, :].rearrange("p (u e m j) -> p u m j e", u=2, e=2, j=PACK),
-            w1_lo.rearrange("p j (m u e) -> p u m j e", u=2, e=2),
+            w1_lo[:].rearrange("p j (m u e) -> p u m j e", u=2, e=2),
         )
+        for t in (0, 1):
+            scalar_lane(t, 3 * QUARTER, QUARTER)
+            gpsimd_lane(t, 0, 3 * QUARTER)
+        nc.scalar.copy(
+            w1_woven[:, 1, :].rearrange("p (u e m j) -> p u m j e", u=2, e=2, j=PACK)[:, :, 0:part_m],
+            w1_hi[0][:].rearrange("p j (m u e) -> p u m j e", u=2, e=2),
+        )
+        gpsimd_lane(2, 0, QUARTER)
+        scalar_lane(2, QUARTER, 2 * QUARTER)
+        scalar_lane(2, 3 * QUARTER, QUARTER)
         nc.gpsimd.tensor_scalar(
-            w1_woven[:, 1, :].rearrange("p (t m j) -> p t m j", t=PACK, j=PACK)[:, :, scalar_m:P],
+            w1_woven[:, 1, :].rearrange("p (t m j) -> p t m j", t=PACK, j=PACK)[:, :, part_m:P],
             w1_hi[1][:].rearrange("p j (m t) -> p t m j", t=PACK),
             1.0,
             0.0,
             MULT,
             ADD,
         )
-
-        page_woven = [tile(f"page_woven{i}", [P, PACK * width], BF16) for i, (first, width) in enumerate(PAGE_PARTS)]
-
-        def round_row_set(t, first, width):
-            lane = pairs[:, t // 2, :].rearrange("p (c e) -> p c e", e=2)[:, first : first + width, t % 2]
-            nc.scalar.copy(lane, page[t][:, first : first + width])
-
-        def weave_page(copy, i):
-            first, width = PAGE_PARTS[i]
-            copy(
-                page_woven[i][:].bitcast(F32).rearrange("p (c u) -> p c u", u=2),
-                pairs.bitcast(F32)[:, :, first : first + width].rearrange("p u c -> p c u"),
-            )
-
-        nc.vector.tensor_copy(page[first_set][:].indirect(idx2[:, 0 : LEAD // LIST_ROWS]), lead[:])
-        nc.vector.tensor_copy(page[first_set][:].indirect(idx2[:, LEAD // LIST_ROWS :]), scan[first_set][:, LEAD:S])
-        for t in SCATTER_ORDER[1:]:
-            nc.vector.tensor_copy(page[t][:].indirect(idx2[:]), scan[t][:])
-        round_row_set(SCATTER_ORDER[0], 0, T2)
-        round_row_set(SCATTER_ORDER[1], 0, T2)
-        nc.scalar.copy(
-            w1_woven[:, 1, :].rearrange("p (u e m j) -> p u m j e", u=2, e=2, j=PACK)[:, :, 0:scalar_m],
-            w1_hi[0][:].rearrange("p j (m u e) -> p u m j e", u=2, e=2),
-        )
-        round_row_set(SCATTER_ORDER[2], 0, T2)
-        round_row_set(PACK - 1, 0, BANK)
-        weave_page(nc.gpsimd.tensor_copy, 0)
-        round_row_set(PACK - 1, BANK, BANK)
-        for i in (1, 2):
-            weave_page(nc.scalar.copy, i)
-
-        nc.sync.dma_start(w3_w[:], w3_words.rearrange("a p c i -> p a (c i)").bitcast(I32))
-        for quadrant in range(QUADRANTS):
-            nc.sync.dma_start(
-                w3_s[32 * quadrant : 32 * quadrant + PASSES * PACK, :].bitcast(I32),
-                w3_scales[:, PACK * quadrant : PACK * (quadrant + 1), :].bitcast(I32),
-            )
+        gpsimd_lane(3, 0, QUARTER)
+        for quarter in range(1, 4):
+            scalar_lane(3, quarter * QUARTER, QUARTER)
 
         neg_clear = tile("neg_clear", [P, PASSES * PACK], F32)
         nc.scalar.mul(neg_clear[:], clear_rows[:].rearrange("p g t -> p (g t)"), -1.0)
 
-        def quantize(name, woven, tag=None):
-            width = woven.shape[1] // PACK
+        def quantize(name, src, tag=None):
+            width = src.shape[1] // PACK
             codes = tile(f"{name}_codes", [P, width], U32, tag=tag)
             scales = tile(f"{name}_scales", [P, width], U8)
-            nc.vector.quantize_mx(out=codes[:].bitcast(FP8X4), scales=scales[:], in_=woven)
-            return codes, scales
-
-        page_quarters = [
-            page_woven[0][:, 0 : PACK * BANK // 2],
-            page_woven[0][:, PACK * BANK // 2 : PACK * BANK],
-            page_woven[1][:],
-            page_woven[2][:],
-        ]
-
-        def quantize_page(h, codes, tag=None):
-            scales = tile(f"page_scales{h}", [P, BANK], U8, tag=tag)
-            for side in range(2):
-                cols = slice(side * BANK // 2, (side + 1) * BANK // 2)
-                nc.vector.quantize_mx(
-                    out=codes[:, cols].bitcast(FP8X4), scales=scales[:, cols], in_=page_quarters[2 * h + side]
-                )
+            nc.vector.quantize_mx(out=codes[:].bitcast(FP8X4), scales=scales[:], in_=src)
             return codes, scales
 
         def gather_words(a, tag):
@@ -225,7 +207,7 @@ def tile_list_free_space_fusion_kernel(
             nc.vector.tensor_copy(words[:], tab_w[a][:].bitcast(U32).indirect(idx[:]))
             return words
 
-        w1_codes = tile("w1_codes", [P, H], U32, tag=f"page{SCATTER_ORDER[2]}")
+        w1_codes = tile("w1_codes", [P, H], U32, tag="page2")
         w1_scales = tile("w1_scales", [P, H], U8)
         for g in range(PASSES):
             cols = slice(g * K_PASS, (g + 1) * K_PASS)
@@ -243,14 +225,30 @@ def tile_list_free_space_fusion_kernel(
                 stop=True,
             )
         v_w = [gather_words(0, "w1_hi1")]
-        page_codes = tile("page_codes", [P, T2], U32, tag="tab_w0")
-        page_q = [quantize_page(0, page_codes[:, 0:BANK]), quantize_page(1, page_codes[:, BANK:T2])]
-        v_w.append(gather_words(1, "page_woven0"))
+        page_codes = tile("page_codes", [P, T2], U32)
+        for quarter in range(4):
+            cols = slice(quarter * QUARTER, (quarter + 1) * QUARTER)
+            nc.vector.quantize_mx(
+                out=page_codes[:, cols].bitcast(FP8X4),
+                scales=page_scales[:, cols],
+                in_=woven(quarter * QUARTER, QUARTER),
+            )
+        v_w.append(gather_words(1, "w2_s"))
 
-        w2_dealt = [deal_w2(0, ("page_woven2", "page_woven1"))]
+        def deal_w2(g, tags):
+            dealt = [tile(f"w2_dealt{g}{u}", [P, PASSES, K_PASS], U8, tag=tags[u])[:] for u in range(2)]
+            group = w2_w[:].bitcast(U16)[:, :, g * K_PASS : (g + 1) * K_PASS].rearrange("p a (m t) -> p a t m", t=PACK)
+            for u in range(2):
+                nc.gpsimd.tensor_copy(
+                    dealt[u].bitcast(U16).rearrange("p a (t m) -> p a t m", t=2), group[:, :, 2 * u : 2 * u + 2]
+                )
+            return dealt
 
-        gap = tile("gap", [P, PICKS], F32)
-        held_by = {3: "page_woven2", 4: "page_woven1", 5: "gap"}
+        w2_dealt = [deal_w2(0, ("w1_lo", "second_pair"))]
+
+        past = PICKS + ASIDE
+        gap = tile("gap", [P, past], F32)
+        held_by = {3: "w1_lo", 4: "second_pair", 5: "gap"}
         a_rows = [tile(f"a_rows{k}", [P, T2], F32, tag=held_by.get(k)) for k in range(PASSES * PACK)]
         lo_first = (PACK - 1) * PICKS + PIECES[2][0]
         shared = tile("shared", [P, lo_first + PACK * HALF], F32)
@@ -261,27 +259,30 @@ def tile_list_free_space_fusion_kernel(
         def less_clear(k, dst, src):
             nc.scalar.activation(dst, src, IDENTITY, bias=neg_clear[:, k : k + 1], scale=1.0)
 
-        def make_a(k, h, bank, first=0, width=BANK):
-            codes, scales = page_q[h]
+        def make_a(k, bank, first, width):
+            cols = slice(first, first + width)
             nc.tensor.matmul_mx(
                 out=bank[:, 0:width],
                 lhsT=w1_codes[:, k * P : (k + 1) * P].bitcast(FP8X4),
                 lhsT_scale=w1_scales[:, k * P : (k + 1) * P],
-                rhs=codes[:, first : first + width].bitcast(FP8X4),
-                rhs_scale=scales[:, first : first + width],
+                rhs=page_codes[:, cols].bitcast(FP8X4),
+                rhs_scale=page_scales[:, cols],
                 start=True,
                 stop=True,
             )
-            less_clear(k, a_rows[k][:, h * BANK + first : h * BANK + first + width], bank[:, 0:width])
+            less_clear(k, a_rows[k][:, cols], bank[:, 0:width])
 
         quarter_banks = [banks[number] for number in (6, 0, 1, 5)]
         half_banks = {1: (0, 6), 2: (5, 4), 3: (1, 7), 4: (2, 1), 5: (7, 2), 6: (1, 7), 7: (2, 1)}
         b_banks = [banks[number] for number in (2, 3, 0, 6)]
         b1_banks = [[banks[number] for number in pair] for pair in ((7, 2), (1, 7))]
 
+        def make_half(k, h):
+            make_a(k, banks[half_banks[k][h]], h * BANK, BANK)
+
         def make_tile(k):
             for h in range(2):
-                make_a(k, h, banks[half_banks[k][h]])
+                make_half(k, h)
 
         def pick(k, first, width):
             offsets = idx3[:, first // LIST_ROWS : (first + width) // LIST_ROWS]
@@ -301,34 +302,43 @@ def tile_list_free_space_fusion_kernel(
                 )
 
         for quarter, bank in enumerate(quarter_banks):
-            h, side = divmod(quarter, 2)
-            make_a(0, h, bank, side * BANK // 2, BANK // 2)
+            make_a(0, bank, quarter * QUARTER, QUARTER)
         pick(0, 0, PICKS)
         w2_dealt.append(deal_w2(1, ("tab_w1", "a_rows0")))
-        z0_rows = tile("z0_rows", [P, PACK, PICKS], BF16)
-        b0 = tile("b0", [P, PICKS], F32)
-        rise = tile("rise", [P, PICKS], F32)
+        z0_rows = tile("z0_rows", [P, PACK * PICKS], BF16)
+        floor = tile("floor", [P, past], F32)
+        rise = tile("rise", [P, past], F32)
         for k in (1, 2):
             make_tile(k)
             pick(k, 0, PICKS)
         make_b(0, b_banks[0][:])
-        less_clear(0, b0[:], b_banks[0][:])
-        nc.gpsimd.tensor_tensor(gap[:], picked[:, 0, :], b0[:], SUBTRACT)
+        less_clear(0, floor[:, 0:PICKS], b_banks[0][:])
+        make_b(1, b_banks[1][:])
+        if ASIDE:
+            less_clear(1, floor[:, PICKS:past], b_banks[1][:, 0:ASIDE])
+        nc.gpsimd.tensor_tensor(gap[:], shared[:, 0:past], floor[:], SUBTRACT)
         make_tile(3)
         pick(3, 0, PICKS)
         for k in range(1, PACK):
-            make_b(k, b_banks[k][:])
+            if k > 1:
+                make_b(k, b_banks[k][:])
+            first = ASIDE if k == 1 else 0
             nc.vector.scalar_tensor_tensor(
-                z0_rows[:, k, :], b_banks[k][:], neg_clear[:, k : k + 1], picked[:, k, :], ADD, MAX
+                z0_rows[:, k * PICKS + first : (k + 1) * PICKS],
+                b_banks[k][:, first:PICKS],
+                neg_clear[:, k : k + 1],
+                picked[:, k, first:PICKS],
+                ADD,
+                MAX,
             )
-        make_a(PACK, 0, banks[half_banks[PACK][0]])
+        make_half(PACK, 0)
         nc.scalar.activation(rise[:], gap[:], RELU)
-        make_a(PACK, 1, banks[half_banks[PACK][1]])
-        nc.gpsimd.tensor_tensor(z0_rows[:, 0, :], rise[:], b0[:], ADD)
+        make_half(PACK, 1)
+        nc.gpsimd.tensor_tensor(z0_rows[:, 0:past], rise[:], floor[:], ADD)
         z0_woven = tile("z0_woven", [P, PACK * PICKS], BF16)
         nc.gpsimd.tensor_scalar(
             z0_woven[:].rearrange("p (c t) -> p c t", t=PACK),
-            z0_rows[:].rearrange("p t c -> p c t"),
+            z0_rows[:].rearrange("p (t c) -> p c t", t=PACK),
             1.0,
             0.0,
             MULT,
@@ -382,7 +392,7 @@ def tile_list_free_space_fusion_kernel(
                 nc.tensor.matmul_mx(
                     out=piece_sums(i)[side][:, place, :],
                     lhsT=w3_w[:, g, n * P : (n + 1) * P].bitcast(FP8X4),
-                    lhsT_scale=w3_s[PACK * g : P, n * P : (n + 1) * P],
+                    lhsT_scale=w3_s[PACK:P, g, n * P : (n + 1) * P],
                     rhs=codes.bitcast(FP8X4),
                     rhs_scale=scales,
                     start=(g == 0 and place == 0),

@@ -26,7 +26,6 @@ K_PASS = P * PACK
 PASSES = 2
 QUADRANTS = 4
 COMPACT = P - 32
-IN_FLIGHT = 8
 BANK = 512
 BANKS = 8
 LIST_ROWS = 16
@@ -107,39 +106,44 @@ def tile_list_free_space_fusion_kernel(
 
         v_rows = tile("v_rows", [P, PICKS], U8)
         nc.vector.tensor_copy(v_rows[:], tab_s[:].indirect(idx[:]))
-        planes = tile("planes", [P, PASSES * PICKS + PASSES * H + T2], U8, tag="tab_s")
+        planes = tile("planes", [P, PASSES * PICKS + PASSES * H + N], U8, tag="tab_s")
         nc.gpsimd.memset(planes[:].bitcast(I32), 0)
         v_s = planes[:, 0 : PASSES * PICKS].rearrange("p (a c) -> p a c", a=PASSES)
+        page_scales = planes[PACK:P, 0:T2]
         w2_dealt_s = planes[:, PASSES * PICKS : PASSES * (PICKS + H)].rearrange("p (a c) -> p a c", a=PASSES)
-        page_scales = planes[:, PASSES * (PICKS + H) :]
-        w3_s = page_scales.rearrange("p (a c) -> p a c", a=PASSES)
-        for quadrant in range(QUADRANTS):
-            nc.sync.dma_start(
-                w3_s[32 * quadrant + PACK : 32 * quadrant + 2 * PACK].bitcast(I32),
-                w3_scales[:, PACK * quadrant : PACK * (quadrant + 1), :].rearrange("a q c -> q a c").bitcast(I32),
-            )
-        load_table(1)
-        nc.sync.dma_start(idx3[:], offs3)
-
+        w3_s = planes[:, PASSES * (PICKS + H) :]
         w2_dealt_rows = tile("w2_dealt_rows", [P, PASSES * H], U8)
         nc.gpsimd.tensor_copy(
             w2_dealt_rows[:].rearrange("p (g t m) -> p g t m", t=PACK, m=P),
             w2_s[:].rearrange("p (g m t) -> p g t m", t=PACK, m=P),
         )
-        spreads = []
-        for a in range(PASSES):
-            for quadrant in range(QUADRANTS):
+
+        def spread_table_scales(quadrant):
+            for a in range(PASSES):
                 first = COMPACT + 16 * a + PACK * quadrant
-                spreads.append((v_s[32 * quadrant : 32 * quadrant + PACK, a, :], v_rows[first : first + PACK, :]))
-        for quadrant in range(QUADRANTS):
+                nc.sync.dma_start(
+                    v_s[32 * quadrant : 32 * quadrant + PACK, a, :].bitcast(I32),
+                    v_rows[first : first + PACK, :].bitcast(I32),
+                )
+
+        for quadrant in range(1, QUADRANTS):
+            spread_table_scales(quadrant)
+        load_table(1)
+        nc.sync.dma_start(idx3[:], offs3)
+        spread_table_scales(0)
+        nc.sync.dma_start(w2_w[:].bitcast(I32), w2_words.rearrange("a p c -> p a c").bitcast(I32))
+        for quadrant in (0, 2, 1, 3):
             first = COMPACT + 16 + PACK * quadrant
-            both = w2_dealt_s[32 * quadrant : 32 * quadrant + PACK].rearrange("p a c -> p (a c)")
-            spreads.append((both, w2_dealt_rows[first : first + PACK, :]))
-        for place, (rows, compact) in enumerate(spreads):
-            if place == len(spreads) - (IN_FLIGHT - 1):
-                nc.sync.dma_start(w2_w[:].bitcast(I32), w2_words.rearrange("a p c -> p a c").bitcast(I32))
-            nc.sync.dma_start(rows.bitcast(I32), compact.bitcast(I32))
+            nc.sync.dma_start(
+                w2_dealt_s[32 * quadrant : 32 * quadrant + PACK].rearrange("p a c -> p (a c)").bitcast(I32),
+                w2_dealt_rows[first : first + PACK, :].bitcast(I32),
+            )
         nc.sync.dma_start(w3_w[:], w3_words.rearrange("a p c i -> p a (c i)").bitcast(I32))
+        for quadrant in range(QUADRANTS):
+            nc.sync.dma_start(
+                w3_s[32 * quadrant : 32 * quadrant + PASSES * PACK, :].bitcast(I32),
+                w3_scales[:, PACK * quadrant : PACK * (quadrant + 1), :].bitcast(I32),
+            )
 
         woven_lo = tile("woven_lo", [P, PACK * 3 * QUARTER], BF16, tag="w2_s")
         woven_hi = tile("woven_hi", [P, PACK * QUARTER], BF16, tag="w1_lo")
@@ -392,7 +396,7 @@ def tile_list_free_space_fusion_kernel(
                 nc.tensor.matmul_mx(
                     out=piece_sums(i)[side][:, place, :],
                     lhsT=w3_w[:, g, n * P : (n + 1) * P].bitcast(FP8X4),
-                    lhsT_scale=w3_s[PACK:P, g, n * P : (n + 1) * P],
+                    lhsT_scale=w3_s[PACK * g : P, n * P : (n + 1) * P],
                     rhs=codes.bitcast(FP8X4),
                     rhs_scale=scales,
                     start=(g == 0 and place == 0),

@@ -251,8 +251,9 @@ def tile_list_free_space_fusion_kernel(
         w2_dealt = [deal_w2(0, ("w1_lo", "second_pair"))]
 
         past = PICKS + ASIDE
-        gap = tile("gap", [P, past], F32)
-        held_by = {3: "w1_lo", 4: "second_pair", 5: "gap"}
+        z0_rows = tile("z0_rows", [P, PACK * PICKS], BF16)
+        gap = z0_rows[:, 2 * PICKS : PACK * PICKS].bitcast(F32)
+        held_by = {3: "w1_lo", 4: "second_pair"}
         a_rows = [tile(f"a_rows{k}", [P, T2], F32, tag=held_by.get(k)) for k in range(PASSES * PACK)]
         lo_first = (PACK - 1) * PICKS + PIECES[2][0]
         shared = tile("shared", [P, lo_first + PACK * HALF], F32)
@@ -309,7 +310,6 @@ def tile_list_free_space_fusion_kernel(
             make_a(0, bank, quarter * QUARTER, QUARTER)
         pick(0, 0, PICKS)
         w2_dealt.append(deal_w2(1, ("tab_w1", "a_rows0")))
-        z0_rows = tile("z0_rows", [P, PACK * PICKS], BF16)
         floor = tile("floor", [P, past], F32)
         rise = tile("rise", [P, past], F32)
         for k in (1, 2):
@@ -320,13 +320,9 @@ def tile_list_free_space_fusion_kernel(
         make_b(1, b_banks[1][:])
         if ASIDE:
             less_clear(1, floor[:, PICKS:past], b_banks[1][:, 0:ASIDE])
-        nc.gpsimd.tensor_tensor(gap[:], shared[:, 0:past], floor[:], SUBTRACT)
-        make_tile(3)
-        pick(3, 0, PICKS)
-        for k in range(1, PACK):
-            if k > 1:
-                make_b(k, b_banks[k][:])
-            first = ASIDE if k == 1 else 0
+        nc.gpsimd.tensor_tensor(gap, shared[:, 0:past], floor[:], SUBTRACT)
+
+        def larger(k, first):
             nc.vector.scalar_tensor_tensor(
                 z0_rows[:, k * PICKS + first : (k + 1) * PICKS],
                 b_banks[k][:, first:PICKS],
@@ -335,8 +331,16 @@ def tile_list_free_space_fusion_kernel(
                 ADD,
                 MAX,
             )
+
+        larger(1, ASIDE)
+        make_tile(3)
+        pick(3, 0, PICKS)
+        for k in (2, 3):
+            make_b(k, b_banks[k][:])
         make_half(PACK, 0)
-        nc.scalar.activation(rise[:], gap[:], RELU)
+        nc.scalar.activation(rise[:], gap, RELU)
+        for k in (2, 3):
+            larger(k, 0)
         make_half(PACK, 1)
         nc.gpsimd.tensor_tensor(z0_rows[:, 0:past], rise[:], floor[:], ADD)
         z0_woven = tile("z0_woven", [P, PACK * PICKS], BF16)

@@ -14,12 +14,13 @@ U8 = mybir.dt.uint8
 FP8X4 = mybir.dt.float8_e4m3fn_x4
 FP4X4 = mybir.dt.float4_e2m1fn_x4
 IDENTITY = mybir.ActivationFunctionType.Identity
-RELU = mybir.ActivationFunctionType.Relu
 MAX = mybir.AluOpType.max
+MIN = mybir.AluOpType.min
 ADD = mybir.AluOpType.add
 MULT = mybir.AluOpType.mult
 SUBTRACT = mybir.AluOpType.subtract
 
+LARGEST = (2.0 - 2.0**-23) * 2.0**127
 P = 128
 PACK = 4
 K_PASS = P * PACK
@@ -321,6 +322,7 @@ def tile_list_free_space_fusion_kernel(
         if ASIDE:
             less_clear(1, floor[:, PICKS:past], b_banks[1][:, 0:ASIDE])
         nc.gpsimd.tensor_tensor(gap, shared[:, 0:past], floor[:], SUBTRACT)
+        nc.gpsimd.tensor_scalar(rise[:], gap, LARGEST, 0.0, MIN, MAX)
 
         def larger(k, first):
             nc.vector.scalar_tensor_tensor(
@@ -337,11 +339,9 @@ def tile_list_free_space_fusion_kernel(
         pick(3, 0, PICKS)
         for k in (2, 3):
             make_b(k, b_banks[k][:])
-        make_half(PACK, 0)
-        nc.scalar.activation(rise[:], gap, RELU)
         for k in (2, 3):
             larger(k, 0)
-        make_half(PACK, 1)
+        make_tile(PACK)
         nc.gpsimd.tensor_tensor(z0_rows[:, 0:past], rise[:], floor[:], ADD)
         z0_woven = tile("z0_woven", [P, PACK * PICKS], BF16)
         nc.gpsimd.tensor_scalar(

from contextlib import ExitStack

import concourse.mybir as mybir

K, K2, H, N, T, PICKS, T2, S = 1024, 512, 1024, 512, 2048, 512, 1024, 512
FLOPS = 2 * K2 * H * T2 + 2 * K * H * PICKS + 2 * H * N * PICKS

F32 = mybir.dt.float32
BF16 = mybir.dt.bfloat16
I32 = mybir.dt.int32
U32 = mybir.dt.uint32
U16 = mybir.dt.uint16
U8 = mybir.dt.uint8
FP8X4 = mybir.dt.float8_e4m3fn_x4
FP4X4 = mybir.dt.float4_e2m1fn_x4
IDENTITY = mybir.ActivationFunctionType.Identity
MAX = mybir.AluOpType.max
MIN = mybir.AluOpType.min
ADD = mybir.AluOpType.add
MULT = mybir.AluOpType.mult
SUBTRACT = mybir.AluOpType.subtract

LARGEST = (2.0 - 2.0**-23) * 2.0**127
P = 128
PACK = 4
K_PASS = P * PACK
PASSES = 2
QUADRANTS = 4
COMPACT = P - 32
BANK = 512
BANKS = 8
LIST_ROWS = 16
HALF = PICKS // 2
QUARTER = T2 // 4
W1_PART = 256
LEAD = S // 4
OUT_TILES = N // P
ASIDE = 0
PIECES = [(0, HALF), (HALF, HALF // 2), (HALF + HALF // 2, HALF // 2)]


def tile_list_free_space_fusion_kernel(
    tc, xs, base, w1, clear, tab_words, tab_scales, w2_words, w2_scales, w3_words, w3_scales, offs, offs2, offs3, out
):
    nc = tc.nc
    with ExitStack() as ctx:
        sb = ctx.enter_context(tc.tile_pool(name="sb", bufs=1))
        psum = ctx.enter_context(tc.psum_pool(name="psum", bufs=1))

        def tile(name, shape, dtype, tag=None):
            return sb.tile(shape, dtype, name=name, tag=tag or name, align_bytes=64)

        banks = [psum.tile([P, BANK], F32, name=f"bank{number}") for number in range(BANKS)]

        idx = tile("idx", [P, PICKS // LIST_ROWS], U16)
        idx2 = tile("idx2", [P, S // LIST_ROWS], U16)
        idx3 = tile("idx3", [P, PICKS // LIST_ROWS], U16)

        tab_s = tile("tab_s", [P, T], U8)
        w2_s = tile("w2_s", [P, PASSES * H], U8)
        nc.vector.memset(tab_s[0:COMPACT, :].bitcast(I32), 0)
        nc.gpsimd.memset(w2_s[0:COMPACT, :].bitcast(I32), 0)
        nc.gpsimd.memset(w2_s[COMPACT : COMPACT + 16, :].bitcast(I32), 0)

        base_rows = base.rearrange("(p t) c -> p t c", t=PACK)
        xs_rows = xs.rearrange("(p t) c -> p t c", t=PACK)
        w1_rows = w1.rearrange("(p j) r -> p j r", j=PACK)
        page = [tile(f"page{t}", [P, T2], F32) for t in range(PACK)]
        scan = [tile(f"scan{t}", [P, S], F32) for t in range(PACK)]
        lead = tile("lead", [P, LEAD], F32)
        w1_lo = tile("w1_lo", [P, PACK, K_PASS], F32)
        w1_hi = [tile(f"w1_hi{q}", [P, PACK, W1_PART], F32) for q in range(2)]
        clear_rows = tile("clear_rows", [P, PASSES, PACK], F32)
        tab_w = [tile(f"tab_w{a}", [P, T], I32) for a in range(PASSES)]
        w2_w = tile("w2_w", [P, PASSES, 2 * H], U8)
        w3_w = tile("w3_w", [P, PASSES, N], I32)

        def load_row_set(t):
            nc.sync.dma_start(scan[t][:], xs_rows[:, t, :])
            nc.sync.dma_start(page[t][:], base_rows[:, t, :])

        def load_w1_hi(q):
            first = K_PASS + q * W1_PART
            nc.sync.dma_start(w1_hi[q][:], w1_rows[:, :, first : first + W1_PART])

        def load_table(a):
            nc.sync.dma_start(tab_w[a][:], tab_words[a].rearrange("p c i -> p (c i)").bitcast(I32))

        nc.sync.dma_start(idx[:], offs)
        nc.scalar.dma_start(tab_s[COMPACT:P, :].bitcast(I32), tab_scales.rearrange("a q t -> (a q) t").bitcast(I32))
        nc.sync.dma_start(page[0][:], base_rows[:, 0, :])
        nc.sync.dma_start(idx2[:], offs2)
        nc.scalar.dma_start(lead[:], xs_rows[:, 0, 0:LEAD])
        nc.sync.dma_start(scan[0][:, LEAD:S], xs_rows[:, 0, LEAD:S])
        nc.sync.dma_start(
            w2_s[COMPACT + 16 : P, :].rearrange("q (a c) -> q a c", a=PASSES).bitcast(I32),
            w2_scales.rearrange("a q c -> q a c").bitcast(I32),
        )
        load_row_set(1)
        nc.sync.dma_start(w1_lo[:], w1_rows[:, :, 0:K_PASS])
        load_row_set(2)
        load_w1_hi(0)
        load_row_set(3)
        load_w1_hi(1)
        nc.sync.dma_start(clear_rows[:], clear.rearrange("(g p t) -> p g t", p=P, t=PACK))
        load_table(0)

        v_rows = tile("v_rows", [P, PICKS], U8)
        nc.vector.tensor_copy(v_rows[:], tab_s[:].indirect(idx[:]))
        planes = tile("planes", [P, PASSES * PICKS + PASSES * H + N], U8, tag="tab_s")
        nc.gpsimd.memset(planes[:].bitcast(I32), 0)
        v_s = planes[:, 0 : PASSES * PICKS].rearrange("p (a c) -> p a c", a=PASSES)
        page_scales = planes[PACK:P, 0:T2]
        w2_dealt_s = planes[:, PASSES * PICKS : PASSES * (PICKS + H)].rearrange("p (a c) -> p a c", a=PASSES)
        w3_s = planes[:, PASSES * (PICKS + H) :]
        w2_dealt_rows = tile("w2_dealt_rows", [P, PASSES * H], U8)
        nc.gpsimd.tensor_copy(
            w2_dealt_rows[:].rearrange("p (g t m) -> p g t m", t=PACK, m=P),
            w2_s[:].rearrange("p (g m t) -> p g t m", t=PACK, m=P),
        )

        def spread_table_scales(quadrant):
            for a in range(PASSES):
                first = COMPACT + 16 * a + PACK * quadrant
                nc.sync.dma_start(
                    v_s[32 * quadrant : 32 * quadrant + PACK, a, :].bitcast(I32),
                    v_rows[first : first + PACK, :].bitcast(I32),
                )

        for quadrant in range(1, QUADRANTS):
            spread_table_scales(quadrant)
        load_table(1)
        nc.sync.dma_start(idx3[:], offs3)
        spread_table_scales(0)
        nc.sync.dma_start(w2_w[:].bitcast(I32), w2_words.rearrange("a p c -> p a c").bitcast(I32))
        for quadrant in (0, 2, 1, 3):
            first = COMPACT + 16 + PACK * quadrant
            nc.sync.dma_start(
                w2_dealt_s[32 * quadrant : 32 * quadrant + PACK].rearrange("p a c -> p (a c)").bitcast(I32),
                w2_dealt_rows[first : first + PACK, :].bitcast(I32),
            )
        nc.sync.dma_start(w3_w[:], w3_words.rearrange("a p c i -> p a (c i)").bitcast(I32))
        for quadrant in range(QUADRANTS):
            nc.sync.dma_start(
                w3_s[32 * quadrant : 32 * quadrant + PASSES * PACK, :].bitcast(I32),
                w3_scales[:, PACK * quadrant : PACK * (quadrant + 1), :].bitcast(I32),
            )

        woven_lo = tile("woven_lo", [P, PACK * 3 * QUARTER], BF16, tag="w2_s")
        woven_hi = tile("woven_hi", [P, PACK * QUARTER], BF16, tag="w1_lo")

        def woven(first, width):
            if first < 3 * QUARTER:
                return woven_lo[:, PACK * first : PACK * (first + width)]
            return woven_hi[:, PACK * (first - 3 * QUARTER) : PACK * (first - 3 * QUARTER + width)]

        def lane(t, first, width):
            return woven(first, width).rearrange("p (c t) -> p c t", t=PACK)[:, :, t]

        def scalar_lane(t, first, width):
            nc.scalar.copy(lane(t, first, width), page[t][:, first : first + width])

        def gpsimd_lane(t, first, width):
            nc.gpsimd.tensor_scalar(lane(t, first, width), page[t][:, first : first + width], 1.0, 0.0, MULT, ADD)

        w1_woven = tile("w1_woven", [P, PASSES, PACK * K_PASS], BF16)
        part_m = W1_PART // PACK

        nc.vector.tensor_copy(page[0][:].indirect(idx2[:, 0 : LEAD // LIST_ROWS]), lead[:])
        nc.vector.tensor_copy(page[0][:].indirect(idx2[:, LEAD // LIST_ROWS :]), scan[0][:, LEAD:S])
        for t in range(1, PACK):
            nc.vector.tensor_copy(page[t][:].indirect(idx2[:]), scan[t][:])

        nc.scalar.copy(
            w1_woven[:, 0, :].rearrange("p (u e m j) -> p u m j e", u=2, e=2, j=PACK),
            w1_lo[:].rearrange("p j (m u e) -> p u m j e", u=2, e=2),
        )
        for t in (0, 1):
            scalar_lane(t, 3 * QUARTER, QUARTER)
            gpsimd_lane(t, 0, 3 * QUARTER)
        nc.scalar.copy(
            w1_woven[:, 1, :].rearrange("p (u e m j) -> p u m j e", u=2, e=2, j=PACK)[:, :, 0:part_m],
            w1_hi[0][:].rearrange("p j (m u e) -> p u m j e", u=2, e=2),
        )
        gpsimd_lane(2, 0, QUARTER)
        scalar_lane(2, QUARTER, 2 * QUARTER)
        scalar_lane(2, 3 * QUARTER, QUARTER)
        nc.gpsimd.tensor_scalar(
            w1_woven[:, 1, :].rearrange("p (t m j) -> p t m j", t=PACK, j=PACK)[:, :, part_m:P],
            w1_hi[1][:].rearrange("p j (m t) -> p t m j", t=PACK),
            1.0,
            0.0,
            MULT,
            ADD,
        )
        gpsimd_lane(3, 0, QUARTER)
        for quarter in range(1, 4):
            scalar_lane(3, quarter * QUARTER, QUARTER)

        neg_clear = tile("neg_clear", [P, PASSES * PACK], F32)
        nc.scalar.mul(neg_clear[:], clear_rows[:].rearrange("p g t -> p (g t)"), -1.0)

        def quantize(name, src, tag=None):
            width = src.shape[1] // PACK
            codes = tile(f"{name}_codes", [P, width], U32, tag=tag)
            scales = tile(f"{name}_scales", [P, width], U8)
            nc.vector.quantize_mx(out=codes[:].bitcast(FP8X4), scales=scales[:], in_=src)
            return codes, scales

        def gather_words(a, tag):
            words = tile(f"v_w{a}", [P, PICKS], U32, tag=tag)
            nc.vector.tensor_copy(words[:], tab_w[a][:].bitcast(U32).indirect(idx[:]))
            return words

        w1_codes = tile("w1_codes", [P, H], U32, tag="page2")
        w1_scales = tile("w1_scales", [P, H], U8)
        for g in range(PASSES):
            cols = slice(g * K_PASS, (g + 1) * K_PASS)
            nc.vector.quantize_mx(
                out=w1_codes[:, cols].bitcast(FP8X4), scales=w1_scales[:, cols], in_=w1_woven[:, g, :]
            )
        for turn in range(4):
            nc.tensor.matmul_mx(
                out=banks[7][:],
                lhsT=w1_codes[:, 0:P].bitcast(FP8X4),
                lhsT_scale=w1_scales[:, 0:P],
                rhs=w1_codes[:, 0:BANK].bitcast(FP8X4),
                rhs_scale=w1_scales[:, 0:BANK],
                start=True,
                stop=True,
            )
        v_w = [gather_words(0, "w1_hi1")]
        page_codes = tile("page_codes", [P, T2], U32)
        for quarter in range(4):
            cols = slice(quarter * QUARTER, (quarter + 1) * QUARTER)
            nc.vector.quantize_mx(
                out=page_codes[:, cols].bitcast(FP8X4),
                scales=page_scales[:, cols],
                in_=woven(quarter * QUARTER, QUARTER),
            )
        v_w.append(gather_words(1, "w2_s"))

        def deal_w2(g, tags):
            dealt = [tile(f"w2_dealt{g}{u}", [P, PASSES, K_PASS], U8, tag=tags[u])[:] for u in range(2)]
            group = w2_w[:].bitcast(U16)[:, :, g * K_PASS : (g + 1) * K_PASS].rearrange("p a (m t) -> p a t m", t=PACK)
            for u in range(2):
                nc.gpsimd.tensor_copy(
                    dealt[u].bitcast(U16).rearrange("p a (t m) -> p a t m", t=2), group[:, :, 2 * u : 2 * u + 2]
                )
            return dealt

        w2_dealt = [deal_w2(0, ("w1_lo", "second_pair"))]

        past = PICKS + ASIDE
        z0_rows = tile("z0_rows", [P, PACK * PICKS], BF16)
        gap = z0_rows[:, 2 * PICKS : PACK * PICKS].bitcast(F32)
        held_by = {3: "w1_lo", 4: "second_pair"}
        a_rows = [tile(f"a_rows{k}", [P, T2], F32, tag=held_by.get(k)) for k in range(PASSES * PACK)]
        lo_first = (PACK - 1) * PICKS + PIECES[2][0]
        shared = tile("shared", [P, lo_first + PACK * HALF], F32)
        picked = shared[:, 0 : PACK * PICKS].rearrange("p (t c) -> p t c", t=PACK)
        b1_lo = shared[:, lo_first:].rearrange("p (t c) -> p t c", t=PACK)
        b1_hi = tile("b1_hi", [P, PACK, HALF], F32)

        def less_clear(k, dst, src):
            nc.scalar.activation(dst, src, IDENTITY, bias=neg_clear[:, k : k + 1], scale=1.0)

        def make_a(k, bank, first, width):
            cols = slice(first, first + width)
            nc.tensor.matmul_mx(
                out=bank[:, 0:width],
                lhsT=w1_codes[:, k * P : (k + 1) * P].bitcast(FP8X4),
                lhsT_scale=w1_scales[:, k * P : (k + 1) * P],
                rhs=page_codes[:, cols].bitcast(FP8X4),
                rhs_scale=page_scales[:, cols],
                start=True,
                stop=True,
            )
            less_clear(k, a_rows[k][:, cols], bank[:, 0:width])

        quarter_banks = [banks[number] for number in (6, 0, 1, 5)]
        half_banks = {1: (0, 6), 2: (5, 4), 3: (1, 7), 4: (2, 1), 5: (7, 2), 6: (1, 7), 7: (2, 1)}
        b_banks = [banks[number] for number in (2, 3, 0, 6)]
        b1_banks = [[banks[number] for number in pair] for pair in ((7, 2), (1, 7))]

        def make_half(k, h):
            make_a(k, banks[half_banks[k][h]], h * BANK, BANK)

        def make_tile(k):
            for h in range(2):
                make_half(k, h)

        def pick(k, first, width):
            offsets = idx3[:, first // LIST_ROWS : (first + width) // LIST_ROWS]
            nc.vector.tensor_copy(picked[:, k % PACK, first : first + width], a_rows[k][:].indirect(offsets))

        def make_b(k, sums, cols=slice(0, PICKS)):
            g, t = divmod(k, PACK)
            for a in reversed(range(PASSES)):
                nc.tensor.matmul_mx(
                    out=sums,
                    lhsT=w2_dealt[g][t // 2][:, a, 2 * (t % 2) * P : 2 * (t % 2 + 1) * P].bitcast(FP4X4),
                    lhsT_scale=w2_dealt_s[:, a, k * P : (k + 1) * P],
                    rhs=v_w[a][:, cols].bitcast(FP8X4),
                    rhs_scale=v_s[:, a, cols],
                    start=(a == PASSES - 1),
                    stop=(a == 0),
                )

        for quarter, bank in enumerate(quarter_banks):
            make_a(0, bank, quarter * QUARTER, QUARTER)
        pick(0, 0, PICKS)
        w2_dealt.append(deal_w2(1, ("tab_w1", "a_rows0")))
        floor = tile("floor", [P, past], F32)
        rise = tile("rise", [P, past], F32)
        for k in (1, 2):
            make_tile(k)
            pick(k, 0, PICKS)
        make_b(0, b_banks[0][:])
        less_clear(0, floor[:, 0:PICKS], b_banks[0][:])
        make_b(1, b_banks[1][:])
        if ASIDE:
            less_clear(1, floor[:, PICKS:past], b_banks[1][:, 0:ASIDE])
        nc.gpsimd.tensor_tensor(gap, shared[:, 0:past], floor[:], SUBTRACT)
        nc.gpsimd.tensor_scalar(rise[:], gap, LARGEST, 0.0, MIN, MAX)

        def larger(k, first):
            nc.vector.scalar_tensor_tensor(
                z0_rows[:, k * PICKS + first : (k + 1) * PICKS],
                b_banks[k][:, first:PICKS],
                neg_clear[:, k : k + 1],
                picked[:, k, first:PICKS],
                ADD,
                MAX,
            )

        larger(1, ASIDE)
        make_tile(3)
        pick(3, 0, PICKS)
        for k in (2, 3):
            make_b(k, b_banks[k][:])
        for k in (2, 3):
            larger(k, 0)
        make_tile(PACK)
        nc.gpsimd.tensor_tensor(z0_rows[:, 0:past], rise[:], floor[:], ADD)
        z0_woven = tile("z0_woven", [P, PACK * PICKS], BF16)
        nc.gpsimd.tensor_scalar(
            z0_woven[:].rearrange("p (c t) -> p c t", t=PACK),
            z0_rows[:].rearrange("p (t c) -> p c t", t=PACK),
            1.0,
            0.0,
            MULT,
            ADD,
        )

        last = PASSES * PACK - 1
        pick(PACK, 0, PICKS)
        for k in range(PACK + 1, PASSES * PACK):
            make_tile(k)
            pick(k, 0, PICKS if k < last else PIECES[2][0])
        z0_q = [quantize("z0_half0", z0_woven[:, 0 : PACK * HALF], tag="tab_w1")]
        for h, rows in enumerate((b1_lo, b1_hi)):
            for u, bank in enumerate(b1_banks[h]):
                for e in range(2):
                    make_b(PACK + 2 * u + e, bank[:, e * HALF : (e + 1) * HALF], slice(h * HALF, (h + 1) * HALF))
                for e in range(2):
                    less_clear(PACK + 2 * u + e, rows[:, 2 * u + e, :], bank[:, e * HALF : (e + 1) * HALF])

        z1_woven = [tile(f"z1_woven{i}", [P, PACK * width], BF16) for i, (first, width) in enumerate(PIECES)]

        def make_z1(i, b_piece):
            first, width = PIECES[i]
            nc.vector.tensor_tensor(
                z1_woven[i][:].rearrange("p (c n t) -> p c t n", n=4, t=PACK),
                picked[:, :, first : first + width].rearrange("p t (c n) -> p c t n", n=4),
                b_piece.rearrange("p t (c n) -> p c t n", n=4),
                MAX,
            )

        make_z1(0, b1_lo)
        z0_q.append(quantize("z0_half1", z0_woven[:, PACK * HALF : PACK * PICKS], tag="a_rows0"))
        z1_q = [quantize("z1_piece0", z1_woven[0][:])]
        make_z1(1, b1_hi[:, :, 0 : HALF // 2])
        pick(last, *PIECES[2])
        z1_q.append(quantize("z1_piece1", z1_woven[1][:]))
        make_z1(2, b1_hi[:, :, HALF // 2 : HALF])
        z1_q.append(quantize("z1_piece2", z1_woven[2][:]))

        out_rows = out.rearrange("(n p) j -> p n j", p=P)
        piece_banks = [[banks[number] for number in pair] for pair in ((5, 4), (0, 6), (3, 2))]
        per_bank = OUT_TILES // 2

        def piece_sums(i):
            width = PIECES[i][1]
            return [bank[:, 0 : per_bank * width].rearrange("p (n j) -> p n j", n=per_bank) for bank in piece_banks[i]]

        def out_passes(i, g, codes, scales):
            for n in range(OUT_TILES):
                side, place = divmod(n, per_bank)
                nc.tensor.matmul_mx(
                    out=piece_sums(i)[side][:, place, :],
                    lhsT=w3_w[:, g, n * P : (n + 1) * P].bitcast(FP8X4),
                    lhsT_scale=w3_s[PACK * g : P, n * P : (n + 1) * P],
                    rhs=codes.bitcast(FP8X4),
                    rhs_scale=scales,
                    start=(g == 0 and place == 0),
                    stop=(g == PASSES - 1 and place == per_bank - 1),
                )

        def open_piece(i):
            first, width = PIECES[i]
            codes, scales = z0_q[first // HALF]
            cols = slice(first % HALF, first % HALF + width)
            out_passes(i, 0, codes[:, cols], scales[:, cols])

        def close_piece(i, copies, stores):
            first, width = PIECES[i]
            res = tile(f"res{i}", [P, OUT_TILES, width], F32)
            codes, scales = z1_q[i]
            out_passes(i, 1, codes[:], scales[:])
            sums = piece_sums(i)
            for side, copy in enumerate(copies):
                for places in ([slice(0, 1), slice(1, 2)] if i == 0 and side == 0 else [slice(0, per_bank)]):
                    rows = slice(side * per_bank + places.start, side * per_bank + places.stop)
                    copy(res[:, rows, :], sums[side][:, places, :])
                    stores[side](out_rows[:, rows, first : first + width], res[:, rows, :])

        open_piece(0)
        close_piece(0, [nc.scalar.copy] * 2, [nc.sync.dma_start] * 2)
        for i in (1, 2):
            open_piece(i)
        close_piece(1, [nc.scalar.copy] * 2, [nc.sync.dma_start] * 2)
        close_piece(2, [nc.vector.tensor_copy, nc.scalar.copy], [nc.sync.dma_start, nc.scalar.dma_start])
